import numpy as np, ml_dtypes
CORES = [3,11,19,27,35,43,51,59]
N = 8
BF = ml_dtypes.bfloat16
W, C, CUT, VI, HE, EPS = 2048, 256, 128, 3, 11, 144
def parts(rng, p):
    m = len(p); ty = rng.integers(24, 248, (m, 16)); s = rng.choice(m, (N, 8, W), p=p); u = rng.choice(m, (N, 8, C), p=p)
    x = np.clip(ty[s].transpose(0, 1, 3, 2) + rng.integers(-2, 3, (N, 8, 16, W)), 16, 255)
    x = np.where(rng.random(x.shape) < 0.01, rng.integers(16, 256, x.shape), x)
    ta = rng.integers(0, W, (N, 8, C)); iv = rng.integers(1, W // 8 + 1, (N, 8, 16, C))
    iv = np.where(rng.random((N, 8, 1, C)) < 0.25, rng.integers(1, W, iv.shape), iv)
    e = rng.choice(np.array([EPS // 4, EPS // 2, EPS - EPS // 8, EPS + EPS // 4]), (N, 8, 1, C))
    d = np.clip(32 * ty[u].transpose(0, 1, 3, 2) + rng.integers(-e, e + 1, (N, 8, 16, C)), 512, 8160)
    d = np.where(rng.random(d.shape) < 0.03, rng.integers(512, 8161, d.shape), d)
    return x, ta, iv, d
def gains(rng):
    return 0.5 + rng.random((N, 8, 16, W), dtype=np.float32)
def pack(x, gain, ta, iv, d):
    return {"xs": np.ascontiguousarray(x.reshape(N, 128, W)).astype(np.float32).astype(BF), "gn": np.ascontiguousarray(gain.reshape(N, 128, W)).astype(np.float32).astype(BF),
            "tau": np.ascontiguousarray(ta).astype(np.int32), "iv": np.ascontiguousarray(iv.reshape(N, 128, C)).astype(np.int32), "pf": np.ascontiguousarray(d.reshape(N, 128, C)).astype(np.int32)}
def setup_inputs(rng):
    x, ta, iv, d = parts(rng, [0.4, 0.3, 0.3])
    return pack(x, gains(rng), ta, iv, d)
def setup_inputs_spread(rng):
    x, ta, iv, d = parts(rng, [0.45, 0.3, 0.15, 0.1])
    iv = np.clip(np.exp2((W.bit_length() - 1) * rng.random(iv.shape)).astype(np.int64), 1, W - 1)
    return pack(x, gains(rng) * np.exp2(rng.integers(-1, 2, (N, 8, 1, W))), ta, iv, d)
def setup_inputs_ends(rng):
    i = np.arange(16); v = i[:, None] & i; par = (v ^ (v >> 1) ^ (v >> 2) ^ (v >> 3)) & 1
    ty = par[rng.permutation(16)[:4]][:, rng.permutation(16)] ^ rng.integers(0, 2, 16)
    s = np.repeat(rng.integers(1, 4, (N, 8, W // 8)), 8, axis=2); s[..., 1:17] = 0; s[..., W - 17:W - 1] = 0
    nf = np.where((rng.random((N, 8, W)) < 0.08) & (s > 0), rng.integers(3, 6, (N, 8, W)), 0)[:, :, None, :]
    x = ty[s].transpose(0, 1, 3, 2) ^ (np.argsort(rng.random((N, 8, 16, W), dtype=np.float32), axis=2) < nf)
    u = rng.integers(1, 4, (N, 8, C)); nd = np.where(rng.random((N, 8, C)) < 0.3, rng.integers(1, 5, (N, 8, C)), 0)
    for q in range(N - 1, -1, -2):
        u[q, :, 0] = 0; u[q, :, C - 1] = 0; nd[q, :, 0] = 0; nd[q, :, C - 1] = 16 - HE
    d = ty[u].transpose(0, 1, 3, 2) ^ (np.argsort(rng.random((N, 8, 16, C)), axis=2) < nd[:, :, None, :])
    near = (np.sum(d != ty[0][:, None], axis=2) <= 16 - HE) & (u > 0)
    d = np.where(near[:, :, None, :], ty[u].transpose(0, 1, 3, 2), d)
    mode = rng.integers(0, 3, (N, 8, 1, C)); iv = np.where(mode == 2, rng.integers(0, 2, (N, 8, 16, C)), mode)
    iv = np.where(iv == 1, W - 1, 1); jump = rng.random((N, 8, C)) < 0.8
    iv[:, :, 0] = np.where(jump, rng.integers(1, W, (N, 8, C)), iv[:, :, 0])
    iv[:, :, 8] = np.where(jump & (rng.random((N, 8, C)) < 0.5), rng.integers(1, W, (N, 8, C)), iv[:, :, 8])
    ta = np.where(rng.random((N, 8, C)) < 0.7, (W - 1) * rng.integers(0, 2, (N, 8, C)), rng.integers(0, W, (N, 8, C)))
    iv[..., 0] = 1; iv[..., C - 1] = W - 1; ta[..., 0] = 0; ta[..., C - 1] = W - 1
    gain = np.where(rng.random((N, 8, 16, W)) < 0.3, 0.125, 4.0)
    return pack(np.where(x == 1, 255, 16), gain, ta, iv, np.where(d == 1, 8160, 512))
def setup_inputs_corners(rng):
    x, ta, iv, d = parts(rng, [0.4, 0.3, 0.3]); z = rng.integers(24, 248, 16); junk = 16 + (z - 16 + 100) % 240
    k = np.arange(16); e = k % 2; nb = W // 64
    for q in range(N):
        for g in range(8):
            st = (2, 1, 3, 2)[(g + q) % 4]
            cs = rng.permutation(np.concatenate([np.array([0, C - 1]), 1 + rng.permutation(C - 2)[:nb - 2]]))
            b = 64 * rng.permutation(nb) - 1; on = (b[:, None] + st * k) % W; lt = (on + 1) % W
            mode = rng.integers(0, 9, (nb, 1)); state = rng.integers(0, 4, (nb, 16))
            for j, pat in enumerate((3 + 0 * k, 2 + 0 * k, e, (k == 15) * 1, (k == 0) * 1, 1 - e, 2 * e)):
                state = np.where(mode == j, pat[None, :], state)
            hc = np.zeros(W, bool); hc[on[(state & 1) > 0]] = True; hc[lt[(state & 2) > 0]] = True
            al = np.zeros(W, bool); al[on.reshape(-1)] = True; al[lt.reshape(-1)] = True
            rest = np.where(al[None, :], junk[:, None], x[q, g])
            far = np.argsort(rng.random((16, W)), axis=0) < rng.choice(np.array([0, 16 - HE, 17 - HE]), W, p=[0.7, 0.2, 0.1])[None, :]
            x[q, g] = np.where(hc[None, :] & ~far, z[:, None], rest)
            ta[q, g, cs] = (b - st) % W; iv[q, g][:, cs] = st
            pick = rng.choice(4, nb, p=[0.4, 0.25, 0.25, 0.1]); n1 = np.array([16, 16, HE, HE - 1])[pick]
            size = np.where(np.argsort(rng.random((16, nb)), axis=0) < n1[None, :], EPS, EPS + 1) * (pick > 0)[None, :]
            d[q, g][:, cs] = 32 * z[:, None] + rng.choice(np.array([-1, 1]), (16, nb)) * size
    return pack(x, gains(rng), ta, iv, d)
def setup_inputs_crowd(rng):
    x, ta, iv, d = parts(rng, [0.4, 0.3, 0.3]); z = rng.integers(24, 248, 16); junk = 16 + (z - 16 + 100) % 240
    hop = np.where(np.arange(16) % 2 == 0, W - 1, 1); o = rng.permutation(8)
    for q in range(N):
        for i in range(8):
            g = int(o[i]); v = int(rng.choice(np.array([0, W - 1, int(rng.integers(1, W - 1))]))); cs = rng.permutation(C)
            if i == 6: v = int(rng.integers(1, W // 2))
            n = (C, C, 16, 16, 16, 0, (64, 32, 96)[q % 3], 0)[i]; one = (0, 0, 1, 0, 0, 2, 1, 0)[i]; a = cs[:n]; s = cs[n:n + one]
            if i == 7:
                h = 19 + rng.permutation(45)[:7]; s = np.concatenate([np.arange(9, 19), h, 127 - h, rng.choice(np.array([0, C - 1]), 1)])
            x[q, g, :, (v - 1) % W] = junk; x[q, g, :, v] = z
            ta[q, g, a] = v; iv[q, g][:, a] = hop[:, None]; d[q, g][:, a] = 32 * z[:, None]
            ta[q, g, s] = (v - W // 32) % W; iv[q, g][:, s] = W // 32; d[q, g][:, s] = 32 * z[:, None]
            if i in (1, 4):
                iv[q, g, 15, a[-1]] = W // 2; x[q, g, :, (v - 1 + W // 2) % W] = z
    return pack(x, gains(rng), ta, iv, d)
def setup_inputs_long(rng):
    x, ta, iv, d = parts(rng, [0.4, 0.3, 0.3]); gain = gains(rng); z, z0 = rng.integers(24, 248, (2, 16)); g0 = int(rng.integers(0, 8)); base = int(rng.integers(0, W))
    wd = 16 * 2 ** VI; k = np.arange(16)
    for i in range(min(2, W // (wd * N)) * N):
        r = i % N; b = (base - wd * i) % W
        for g in range(8):
            if g != g0:
                c = int(rng.integers(0, CUT)) + CUT * ((i // N + r) % 2)
                ta[r, g, c] = b; iv[r, g, :, c] = W - 2; d[r, g, :, c] = 32 * z + rng.integers(-EPS, EPS + 1, 16)
        q = (r + VI - 1) % N
        for g in range(8):
            m = rng.integers(0, 3, 16); m[9] = 1; m[15] = 1
            x[q, g][:, ((b - 2 ** VI * (k + 1) + m) % W)[m < 2]] = z[:, None]
        for t in range(VI - 1):
            x[(r + t) % N][:, :, (b - 2 ** (t + 1) * (k[1::2] + 1)) % W] = z[:, None]
    nf = min(C, W // 16); sg = np.where(z0 < 136, 1, -1)
    for q in range(N):
        cs = rng.permutation(C)[:nf]; st = 2 * int(rng.integers(0, W // 2)) + 1; b = int(rng.integers(0, W))
        col = (b + st * (np.arange(16 * nf) + 1)) % W
        x[q, g0][:, col] = z0[:, None]; ta[q, g0, cs] = (b + 16 * st * np.arange(nf)) % W; iv[q, g0][:, cs] = st
        e = rng.integers(-EPS, EPS + 1, (16, nf)); far = np.argsort(rng.random((16, 8)), axis=0); near = EPS * rng.choice(np.array([-1, 1]), (16, 8))
        e[:, :8] = np.where(far < 2, 512 * sg[:, None], np.where(far < 16 - HE, 2080 * sg[:, None], near))
        d[q, g0][:, cs] = 32 * z0[:, None] + e
        gain[q, g0][:, col[:128]] = 4 * (VI - 2) * (0.75 + 0.5 * rng.random((16, 128)))
    return pack(x, gain * 0.25, ta, iv, d)
def check_ranges(d):
    bad = []
    for name, lo, hi in (("xs", 16, 255), ("gn", 0.125, 4), ("tau", 0, W - 1), ("iv", 1, W - 1), ("pf", 512, 8160)):
        a = np.asarray(d[name]).astype(np.float64)
        if not np.all(np.isfinite(a)) or np.min(a) < lo or np.max(a) > hi: bad.append("range of " + name)
        elif name != "gn" and np.any(a != np.floor(a)): bad.append(name + " is not whole")
    return bad
def go(a, t):
    return np.concatenate([a[..., :CUT], np.roll(a[..., CUT:], t, axis=0)], axis=-1)
def reference(xs, gn, tau, iv, pf):
    X = xs.astype(np.float32).astype(np.int32).reshape(N, 8, 16, W) * np.int32(32); GA = gn.astype(np.float64).reshape(N, 8, 16, W)
    I = iv.astype(np.int32).reshape(N, 8, 16, C); D = pf.astype(np.int32).reshape(N, 8, 16, C); ta = tau.astype(np.int32)
    y = np.zeros((N, 8, 16, C)); eight = np.arange(8)[:, None]; rows = np.arange(16)[None, :, None]
    for t in range(VI):
        for r in range(N):
            q = (r + t) % N
            T = go((ta[r][:, None, :] + np.add.accumulate(I[r], axis=1)) & (W - 1), t).transpose(0, 2, 1).reshape(8, 16 * C); T1 = (T + 1) & (W - 1)
            Ds = go(D[r], t); Dx = np.repeat(Ds, 16, axis=2)
            e0 = np.take_along_axis(X[q], T[:, None, :], 2) - Dx; e1 = np.take_along_axis(X[q], T1[:, None, :], 2) - Dx
            on = np.sum((np.abs(e0) <= EPS).astype(np.int32), axis=1) >= HE
            late = ~on & (np.sum((np.abs(e1) <= EPS).astype(np.int32), axis=1) >= HE); heard = on | late
            P = np.where(late, T1, T); E = np.where(late[:, None, :], e1, e0)
            cnt = np.zeros((8, W), np.int32); np.add.at(cnt, (eight, P), heard.astype(np.int32))
            taken = heard & (np.take_along_axis(cnt, P, 1) == 1)
            z = np.where(taken[:, None, :], np.take_along_axis(GA[q], P[:, None, :], 2) * np.exp(-0.00390625 * np.abs(E)), 0.0)
            y[r] += go(np.add.reduce(z.reshape(8, 16, C, 16), axis=3), -t)
            if t == VI - 1: continue
            S = np.add.reduce(np.where(taken[:, None, :], E, 0).reshape(8, 16, C, 16), axis=3)
            D[r] = go(Ds + (S >> 4), -t)
            X[q] = np.where((cnt == 1)[:, None, :], 0, X[q])
            a = go(taken.reshape(8, C, 16).transpose(0, 2, 1), -t); l = go((taken & late).reshape(8, C, 16).transpose(0, 2, 1), -t)
            J = I[r] + l; leave = np.zeros((8, 16, C), bool); leave[:, :15] = ~a[:, :15] & a[:, 1:]
            J[:, 1:] = J[:, 1:] + np.where(leave[:, :15], J[:, :15], 0)
            o = np.argsort(leave.astype(np.int32), axis=1, kind="stable"); n = 16 - np.sum(leave.astype(np.int32), axis=1)[:, None, :]
            src = np.take_along_axis(o, np.where(rows < n, rows, rows - n), 1)
            I[r] = np.take_along_axis(J, src, 1)
    return {"y": y.reshape(N, 128, C).astype(np.float32)}

def check_inputs(d):
    bad = list(check_ranges(d))
    if not bad:
        for name, y in reference(**d).items():
            for q in range(N):
                v = np.abs(np.asarray(y[q], np.float64)); s = np.sqrt(np.mean(v * v))
                if v.max() > 10 * s or s < 2.0 ** -1: bad.append('%s of rank %d is uneven or too small' % (name, q))
    return bad

@@ -1,0 +1,621 @@
+import numpy as np
+from concourse.mybir import AluOpType as Op, ActivationFunctionType as Fn
+
+N, W, C, VI = 8, 2048, 256, 3
+BIG = 12288.0
+SC = 113.0 / 16
+BIG32 = 1.5 * 2 ** 29
+B = 8192.0
+NA = 8
+NZ = 6
+NY = 7
+NF = 5
+HALVES = (True, False, False)
+ONV = [0, 2, 4]
+EB = (0, 1, 6, 5)
+
+S, P = "sbuf", "psum"
+SCRATCH = {
+    "x0": (S, [128, W], "bfloat16"), "x1": (S, [128, W], "bfloat16"), "x2": (S, [128, W], "bfloat16"),
+    "g0": (S, [128, W], "bfloat16"), "g1": (S, [128, W], "bfloat16"), "g2": (S, [128, W], "bfloat16"),
+    "tab0": (S, [128, W + 8], "float32"), "tab1": (S, [128, W + 8], "float32"),
+    "xu": (S, [128, W + 16], "bfloat16"), "zt": (S, [128, W + 8], "float32"), "wv": (S, [128, W], "float32"),
+    "xg": (S, [128, 4096], "bfloat16"), "xa": (S, [128, 2048], "bfloat16"), "zg": (S, [128, 2048], "float32"),
+    "ind0": (S, [128, 4096], "bfloat16"), "ind1": (S, [128, 4096], "bfloat16"),
+    "oa": (S, [128, 2, 8192], "bfloat16"), "ob": (S, [128, 2, 33 * 128], "bfloat16"),
+    "ivi": (S, [128, C], "int32"), "ivf": (S, [128, C], "float32"), "taui": (S, [128, C], "int32"), "tauf": (S, [128, C], "float32"),
+    "di": (S, [128, C], "int32"), "drot": (S, [128, C], "int32"), "kb": (S, [128, C], "float32"),
+    "kt0": (S, [128, 520], "float32"), "kt1": (S, [128, 520], "float32"),
+    "lo": (S, [128, C], "int32"), "hi": (S, [128, C], "int32"), "mb": (S, [128, C], "bfloat16"),
+    "tu": (S, [128, C], "int32"), "ti": (S, [128, C], "int32"), "th": (S, [128, C], "float16"),
+    "of0": (S, [128, C], "uint16"), "of1": (S, [128, C], "uint16"), "pl0": (S, [128, C], "uint16"), "pl1": (S, [128, C], "uint16"),
+    "thr": (S, [128, C], "float32"), "late": (S, [128, C], "float32"), "mx": (S, [128, C], "float32"), "pen": (S, [128, C], "float32"),
+    "p0": (S, [128, C], "int32"), "pw": (S, [128, C], "int32"), "pp": (S, [128, C], "float32"), "ph": (S, [128, C], "float16"),
+    "bi": (S, [128, C], "int32"), "aa": (S, [128, C], "bfloat16"), "bb": (S, [128, C], "bfloat16"),
+    "hs0": (S, [128, 4, 64], "float32"), "hs1": (S, [128, 4, 64], "float32"), "r0": (S, [128, C], "bfloat16"), "r1": (S, [128, C], "bfloat16"),
+    "uq": (S, [128, 128], "bfloat16"), "u0": (S, [128, 128], "bfloat16"), "u1": (S, [128, 128], "bfloat16"), "us": (S, [128, 128], "bfloat16"),
+    "ul1": (S, [128, 128], "bfloat16"), "ul2": (S, [128, 128], "bfloat16"),
+    "i1": (S, [128, 128], "float32"), "i2": (S, [128, 128], "float32"), "i3": (S, [128, 128], "float32"), "idx": (S, [128, 128], "uint16"),
+    "cb": (S, [128, C], "float32"), "tn": (S, [128, C], "float32"), "tnb": (S, [128, C], "bfloat16"), "lv": (S, [128, C], "float32"),
+    "zz": (S, [128, C], "float32"), "tk": (S, [128, C], "float32"),
+    "vv": (S, [128, 8, 32], "float32"), "acc": (S, [128, 8, 32], "int32"), "cl": (S, [128, 2048], "float32"), "b32": (S, [128, 8], "bfloat16"),
+    "e2": (S, [128, 16], "float32"), "er": (S, [128, 128], "float32"), "nw": (S, [128, 128], "int32"), "v2": (S, [128, 8, 16], "float32"),
+    "nt0": (S, [128, 16], "float32"), "nt1": (S, [128, 16], "float32"),
+    "ntp": (S, [128, C], "bfloat16"), "d1": (S, [128, C], "float32"), "d2": (S, [128, C], "float32"),
+    "ya": (S, [128, C], "float32"), "yb": (S, [128, C], "float32"), "ys": (S, [128, C], "float32"), "yin": (S, [128, C], "float32"),
+    "one": (S, [128, 128], "float32"), "tr1": (S, [128, 128], "float32"), "tri": (S, [128, 128], "float32"), "blf": (S, [128, 128], "float32"),
+    "e8": (S, [128, 128], "float32"),
+    "idf": (S, [128, 128], "float32"), "idb": (S, [128, 128], "bfloat16"), "idh": (S, [128, 128], "bfloat16"), "id7": (S, [128, 128], "bfloat16"),
+    "idm": (S, [128, 128], "bfloat16"), "i32": (S, [128, 128], "bfloat16"), "r32": (S, [128, 128], "bfloat16"),
+    "blk": (S, [128, 128], "bfloat16"), "blr": (S, [128, 128], "bfloat16"), "b16": (S, [128, 8], "bfloat16"),
+    "s3": (S, [128, 8, 48], "float16"), "c256": (S, [128, W], "bfloat16"), "sel": (S, [128, W], "bfloat16"),
+    "wc": (S, [128, 8], "bfloat16"), "seg": (S, [128, 128], "float32"),
+    "k1": (S, [128, 8], "int32"), "k2": (S, [128, 8], "int32"), "k3": (S, [128, 8], "float32"), "k4": (S, [128, 8], "float32"), "el": (S, [128, 8], "uint16"),
+}
+for _b in range(8):
+    SCRATCH["q%d" % _b] = (P, [128, 16, 32] if _b in (2, 3) else [128, 4, 128] if _b in (6, 7) else [128, 512], "float32")
+SHAPES = {"xs": [128, W], "gn": [128, W], "tau": [8, C], "iv": [128, C], "pf": [128, C], "y": [128, C]}
+ENG = ("pe", "act", "dve", "gp", "sp")
+SEMAPHORES = ["pe", "act", "dve", "gp"] + ["d%d" % i for i in range(30)] + ["l%d" % i for i in range(6)] + ["a%d" % i for i in range(6)]
+ALL = slice(None)
+MASKS = {}
+
+
+def build(g, core, T, topo, rank):
+    ops = []
+    nd = [0]
+    queue = {"pe": g.tensor, "act": g.scalar, "dve": g.vector, "gp": g, "sp": g.sync}
+
+    def A(name, *ix):
+        shape = SHAPES[name] if name in SHAPES else SCRATCH[name][1]
+        ix = list(ix) + [ALL] * (len(shape) - len(ix))
+        rs = [range(n)[s] if isinstance(s, slice) else range(s, s + 1) for s, n in zip(ix, shape)]
+        key = (shape[-1],) + tuple((r.start, r.stop, r.step) for r in rs[1:])
+        if key not in MASKS:
+            row = sum(1 << c for c in rs[-1])
+            MASKS[key] = row if len(shape) == 2 else sum(row << (b * shape[-1]) for b in rs[1])
+        return (T[name][tuple(ix)], [(name, rs[0][0], rs[0][-1], MASKS[key])])
+
+    def cols(name, a, b, s=1):
+        return A(name, ALL, slice(a, b, s))
+
+    def IND(win, off):
+        return (win[0].indirect(off[0]), win[1] + off[1])
+
+    def add(eng, call, outs, ins, sem=None, n=0, extra=None):
+        ops.append({"eng": eng, "call": call, "w": [b for o in outs for b in o[1]],
+                    "r": [b for i in ins if isinstance(i, tuple) for b in i[1]], "sem": sem, "n": n, "inc": False, "extra": extra})
+
+    def v(x):
+        return x[0] if isinstance(x, tuple) else x
+
+    def ts(out, in0, s1, op0, s2=None, op1=None):
+        if op1 is None:
+            add("dve", lambda: g.vector.tensor_scalar(out[0], in0[0], v(s1), None, op0), [out], [in0, s1])
+        else:
+            add("dve", lambda: g.vector.tensor_scalar(out[0], in0[0], v(s1), v(s2), op0, op1), [out], [in0, s1, s2])
+
+    def tt(out, a, b, op):
+        add("dve", lambda: g.vector.tensor_tensor(out[0], a[0], b[0], op), [out], [a, b])
+
+    def cp(out, a):
+        add("dve", lambda: g.vector.tensor_copy(out[0], a[0]), [out], [a])
+
+    def ms(out, c):
+        add("dve", lambda: g.vector.memset(out[0], c), [out], [])
+
+    def act(out, a, f, bias=0.0, scale=1.0):
+        add("act", lambda: g.scalar.activation(out[0], a[0], f, bias=float(bias), scale=float(scale)), [out], [a])
+
+    def mm(out, l, r, start=True, stop=True):
+        add("pe", lambda: g.tensor.matmul(out[0], l[0], r[0], start, stop), [out], [l, r])
+
+    def sel(out, a, pat, op, base, cm):
+        add("gp", lambda: g.affine_select(out[0], a[0], pat, op, 0.0, base, cm), [out], [a])
+
+    def iota(out, pat, base, cm, small):
+        if small:
+            add("gp", lambda: g.iota(out[0], pat, base, cm, allow_small_or_imprecise_dtypes=True), [out], [])
+        else:
+            add("gp", lambda: g.iota(out[0], pat, base, cm), [out], [])
+
+    def dma(eng, out, a):
+        nd[0] += 1
+        add(eng, lambda: queue[eng].dma_start(out[0], a[0]), [out], [a], sem="d%d" % (nd[0] - 1), n=16)
+
+    def send(k, back, dst, src):
+        to = T.cores[(rank - back) % N]
+        rid, pid = topo.addr(to)[:2]
+        mask = topo.mask(core, to)
+        n_out = len(topo.engines(core, to))
+        n_in = len(topo.engines(T.cores[(rank + back) % N], core))
+        add("gp", lambda: g.remote_dma(dst[0], src[0], T.sem["a%d" % k], T.sem["l%d" % k], pid, rid, mask), [], [src], sem="l%d" % k, n=n_out, extra="remote")
+        add(None, None, [dst], [], sem="a%d" % k, n=n_in)
+
+    def q(b, a=0, e=512, s=1):
+        shape = SCRATCH["q%d" % b][1]
+        if len(shape) == 2:
+            return cols("q%d" % b, a, e, s)
+        n = shape[2]
+        if a // n == (e - 1) // n:
+            return A("q%d" % b, ALL, a // n, slice(a % n, (e - 1) % n + 1, s))
+        return A("q%d" % b, ALL, slice(a // n, e // n))
+
+    dma("sp", A("ivi"), A("iv"))
+    dma("act", A("taui", slice(0, 8)), A("tau"))
+    dma("sp", cols("x0", 0, 1024), cols("xs", 0, 1024))
+    dma("act", A("di"), A("pf"))
+    dma("act", cols("x0", 1024, W), cols("xs", 1024, W))
+    dma("sp", A("g0"), A("gn"))
+
+    def rotate(dst, src, t, eng=("sp", "sp", "sp")):
+        s = (16 * t) % 128
+        dma(eng[0], cols(dst, 0, 128), cols(src, 0, 128))
+        dma(eng[1], A(dst, slice(s, 128), slice(128, C)), A(src, slice(0, 128 - s), slice(128, C)))
+        dma(eng[2], A(dst, slice(0, s), slice(128, C)), A(src, slice(128 - s, 128), slice(128, C)))
+
+    rotate("drot", "pf", 1)
+    ms(A("one"), 1.0)
+    ms(A("s3"), 0.0)
+    ms(A("c256"), 256.0)
+    ms(A("ob", ALL, ALL, slice(0, 128)), 1.0)
+    ms(A("ob", ALL, ALL, slice(32 * 128, 33 * 128)), -1.0)
+    for h in range(2):
+        for c in (0, 256, 512):
+            ms(cols("kt%d" % h, c, c + (8 if c == 512 else 128)), 1e9)
+    sel(A("tr1"), A("one"), [[-16, 8], [0, 16]], Op.is_ge, 0, 1)
+    sel(A("tri"), A("tr1"), [[1, 128]], Op.is_ge, 0, -1)
+    sel(A("e8"), A("one"), [[-1, 8], [0, 16]], Op.is_equal, 0, 1)
+    sel(A("idf"), A("one"), [[-1, 128]], Op.is_equal, 0, 1)
+    sel(A("blf"), A("tr1"), [[16, 8], [0, 16]], Op.is_ge, 15, -1)
+    cp(A("ivf"), A("ivi"))
+    cp(A("tauf", slice(0, 8)), A("taui", slice(0, 8)))
+    cp(A("s3", ALL, ALL, slice(16, 32)), A("idf"))
+    for h in range(2):
+        mm(q(4, h, C, 2), cols("ivf", 128 * h, 128 * h + 128), A("tri"), True, False)
+        mm(q(4, h, C, 2), A("tauf", slice(0, 8), slice(128 * h, 128 * h + 128)), A("e8", slice(0, 8)), False, True)
+    for h in range(2):
+        mm(q(7, h, 16, 2), A("tauf", slice(0, 8), slice(128 * h, 128 * h + 128)), A("e8", slice(0, 8), slice(0, 128, 16)))
+    send(0, 1, A("x1"), A("x0"))
+    send(1, 1, A("g1"), A("g0"))
+    cp(A("tu"), q(4, 0, C))
+    ts(A("ti"), A("tu"), W - 1, Op.bitwise_and)
+    cp(A("th"), A("ti"))
+
+    def to_list(src, bank):
+        for m in range(8):
+            for gp in range(4):
+                for e in range(2):
+                    gg = 2 * gp + e
+                    mm(A("q%d" % bank, slice(32 * gp, 32 * gp + 32), slice(m, C, 8)), A("s3", ALL, m, slice(16 - 16 * e, 48 - 16 * e)),
+                       cols(src, 32 * gg, 32 * gg + 32), e == 0, e == 1)
+
+    def profile(t):
+        if t == 0:
+            ts(A("kb"), A("di"), -SC / 32, Op.mult, BIG, Op.add)
+        ts(A("lo"), A("di"), 1.0 / 32, Op.mult, (15.5 - 144) / 32 - 256, Op.add)
+        ts(A("hi"), A("di"), 1.0 / 32, Op.mult, (144 - 15.5) / 32, Op.add)
+        tt(A("mb"), A("lo"), A("hi"), Op.add)
+
+    def time_lists(bank):
+        ts(A("of1"), q(bank, 0, C), 1.0, Op.add)
+        cp(A("of0"), q(bank, 0, C))
+
+    to_list("th", 5)
+    act(cols("tab0", 0, 1024), cols("x0", 0, 1024), Fn.Identity, scale=SC)
+    act(cols("tab0", W, W + 1), cols("x0", 0, 1), Fn.Identity, scale=SC)
+    act(cols("tab0", 1024, W), cols("x0", 1024, W), Fn.Identity, scale=SC)
+    profile(0)
+    ts(A("id7"), A("idf"), 7.0, Op.mult)
+    ts(A("idm"), A("idf"), -3.5, Op.mult)
+    cp(A("blk"), A("blf"))
+    ts(A("b16"), cols("blf", 0, 128, 16), 16.0, Op.mult)
+    time_lists(5)
+    iota(cols("wc", 0, 1), [[0, 1]], 128, 1, True)
+    iota(A("k1"), [[0, 8]], 0, 1, False)
+    iota(A("k3"), [[2, 8]], 0, 0, True)
+    sel(A("sel"), A("c256"), [[-1, 16], [-16, 8], [0, 16]], Op.is_equal, 0, 1)
+
+    def late_constants():
+        ms(cols("xu", W, W + 16), 0.0)
+        ms(cols("zt", W, W + 8), 0.0)
+        ms(A("seg"), 1.0)
+        ms(cols("seg", 0, 128, 16), 0.0)
+        ms(cols("lv", C - 2, C), 0.0)
+        ms(A("cb"), B)
+        ms(cols("cb", 30, C, 32), 0.0)
+        ms(cols("cb", 31, C, 32), 0.0)
+        ts(A("b32"), cols("blf", 0, 128, 16), 32.0, Op.mult)
+        ts(A("k2"), A("k1"), 1, Op.bitwise_and)
+        tt(A("k4"), A("k2"), A("k3"), Op.add)
+        cp(A("el"), A("k4"))
+
+    def act_constants():
+        act(A("idb"), A("idf"), Fn.Identity)
+        act(A("idh"), A("idf"), Fn.Identity, scale=0.5)
+        act(A("i32"), A("idf"), Fn.Identity, scale=32.0)
+        act(cols("r32", 16, 128), cols("idf", 0, 112), Fn.Identity, scale=32.0)
+        act(cols("r32", 0, 16), cols("idf", 112, 128), Fn.Identity, scale=32.0)
+        act(cols("blr", 16, 128), cols("blf", 0, 112), Fn.Identity)
+        act(cols("blr", 0, 16), cols("blf", 112, 128), Fn.Identity)
+        act(A("nt0"), q(7, 0, 16), Fn.Identity, bias=W, scale=-1.0)
+        act(cols("nt1", 0, 16, 2), cols("nt0", 0, 16, 2), Fn.Identity)
+        act(cols("nt1", 3, 16, 2), cols("nt0", 1, 14, 2), Fn.Identity)
+        act(cols("nt1", 1, 2), cols("nt0", 15, 16), Fn.Identity)
+
+    def hear(t):
+        tab = cols("tab%d" % (t % 2), 0, W + 1)
+        via_act = [(1, k) for k in range(0, 16, 2)] + [(0, k) for k in range(16 - NA, 16, 2)]
+        direct = list(range(0, 16 - NA, 2))
+        pend = []
+
+        def count(w, k):
+            for kk in (k, k + 1):
+                for h in range(2):
+                    a = kk * C + 128 * h
+                    mm(q(4, C * w + 2 * kk + h, C * w + C, 32), cols("ind%d" % w, a, a + 128), cols("blk", 0, 128, 16) if w else A("b16"))
+
+        def one_direct(k):
+            for kk in (k, k + 1):
+                tt(cols("ind0", kk * C, kk * C + C), IND(tab, cols("of0", 16 * kk, 16 * kk + 16)), A("kb"), Op.add)
+            o = cols("ind0", k * C, k * C + 2 * C)
+            ts(o, o, BIG, Op.is_equal)
+            pend.append((0, k))
+
+        def front(j):
+            w, k = via_act[j]
+            s = (j % 4) * 512
+            act(cols("xa", s, s + 512), IND(tab, cols("of%d" % w, 16 * k, 16 * k + 32)), Fn.Identity, scale=1.0 / SC)
+            for e in range(2):
+                o = q(j % 4, e * C, e * C + C)
+                mm(o, A("id7"), cols("xa", s + e * C, s + e * C + C), True, False)
+                mm(o, A("idm"), A("mb"), False, True)
+
+        nv, done = len(via_act), 0
+        front(0)
+        for j in range(nv):
+            while done < len(direct) and done * nv <= j * len(direct):
+                one_direct(direct[done]); done += 1
+            if j + 1 < nv:
+                front(j + 1)
+            while pend:
+                count(*pend.pop(0))
+            w, k = via_act[j]
+            ts(cols("ind%d" % w, k * C, k * C + 2 * C), q(j % 4), BIG32 - 896, Op.add, BIG32, Op.is_equal)
+            pend.append((w, k))
+        while pend:
+            count(*pend.pop(0))
+
+    def claims(t):
+        c0, c1 = q(4, 0, C), q(4, C, 2 * C)
+        ts(A("thr"), c0, -160.0, Op.add, 10.5, Op.max)
+        tt(A("late"), c1, A("thr"), Op.is_gt)
+        tt(A("mx"), c1, A("thr"), Op.max)
+        ts(c0, A("mx"), 10.5, Op.is_le, 4096.0, Op.mult)
+        tt(c1, c0, A("ti"), Op.add)
+        tt(A("p0"), c1, A("late"), Op.add)
+        ts(A("bi"), A("p0"), 31, Op.bitwise_and)
+        ts(A("pw"), A("p0"), 4096 + W - 1, Op.bitwise_and)
+        for h in range(2):
+            cp(cols("bb", 128 * h, 128 * h + 128), cols("bi", h, C, 2))
+            ts(cols("aa", 128 * h, 128 * h + 128), cols("pw", h, C, 2), 1.0 / 32, Op.mult, 160 - 15.5 / 32, Op.add)
+        ts(A("ph"), A("pw"), float(W), Op.min)
+        to_list("ph", 5)
+
+    def histogram(t, fill):
+        for h0, h1 in (((0, 1), (1, 2)) if HALVES[t] else ((0, 2),)):
+            for a in range(64):
+                if a % 2 == 0 and a > 0:
+                    b = a // 2
+                    act(A("ob", ALL, slice(h0, h1), slice(128 * b, 128 * b + 128)), cols("bb", 128 * h0, 128 * h1), Fn.Sign, bias=0.5 - b)
+                ts(A("oa", ALL, slice(h0, h1), slice(128 * a, 128 * a + 128)), cols("aa", 128 * h0, 128 * h1), 160.0 + a, Op.is_equal, cols("wc", 0, 1), Op.mult)
+            for h in range(h0, h1):
+                for gq in range(4):
+                    for k in range(16):
+                        o = 16 * gq + k
+                        mm(q(6 + h, 128 * gq, 128 * gq + 66), A("oa", ALL, h, slice(o, 8192, 64)), A("ob", ALL, h, slice(o, 33 * 128, 64)), k == 0, k == 15)
+        cp(A("pl%d" % (t % 2)), q(5, 0, C))
+        fill[0]()
+        for h in range(2):
+            act(A("hs%d" % h), A("q%d" % (6 + h), ALL, ALL, slice(2, 66)), Fn.Identity)
+            for b4 in range(2):
+                part = slice(32 * b4, 32 * b4 + 32)
+                tt(cols("r%d" % h, 128 * b4, 128 * b4 + 128), A("q%d" % (6 + h), ALL, ALL, part), A("hs%d" % h, ALL, ALL, part), Op.subtract)
+            if h == 0:
+                fill[1]()
+        for which in range(2):
+            for g2 in range(2):
+                for b4 in range(2):
+                    o = A("q5", slice(64 * g2, 64 * g2 + 64), slice(C + 128 * which + b4, C + 128 * which + 128, 2))
+                    for h in range(which, 2):
+                        mm(o, cols("r%d" % h, 128 * b4 + g2, 128 * b4 + 128, 2), cols("idh", g2, 128, 2), h == which, h == 1)
+
+    def flags(t):
+        ts(A("uq"), q(5, C, C + 128), 1.0 / 128, Op.mult, 192 - 191.5 / 128, Op.add)
+        ts(A("u%d" % t), A("uq"), 192.0, Op.is_equal)
+
+    def owners(t):
+        ts(A("i1"), q(5, C + 128, 2 * C), 128.0, Op.min, 2.0, Op.mult)
+        ts(A("i2"), q(5, C, C + 128), 256.0, Op.min)
+        tt(A("i3"), A("i1"), A("i2"), Op.add)
+        cp(A("idx"), A("i3"))
+
+    def keys(t):
+        for h in range(2):
+            act(cols("kt%d" % (t % 2), 128 + C * h, C + C * h), cols("kb", 128 * h, 128 * h + 128), Fn.Identity)
+
+    def spread(u, x, with_x, out, banks):
+        def place(i):
+            return q(banks[i // 4 % len(banks)], 128 * (i % 4), 128 * (i % 4) + 128)
+        for r in range(4 + len(banks) - 1):
+            for i in range(4 * r, 4 * r + 4):
+                if i < 16:
+                    if with_x(i):
+                        mm(place(i), A("idb"), cols(x, i, W, 16), True, False)
+                    mm(place(i), cols("sel", 128 * i, 128 * i + 128), A(u), not with_x(i), True)
+            for i in range(4 * (r - len(banks) + 1), 4 * (r - len(banks) + 2)):
+                if i >= 0:
+                    out(i, place(i))
+
+    def diffs(t, a, b):
+        tt(cols("wv", a, b), IND(cols("kt%d" % (t % 2), 0, 513), cols("idx", a // 16, b // 16)), cols("tab%d" % (t % 2), a, b), Op.add)
+
+    def weights(c):
+        o = cols("wv", 512 * c, 512 * c + 512)
+        act(o, o, Fn.Abs, bias=-BIG)
+        act(q(EB[c]), o, Fn.Exp, scale=-1.0 / (8 * SC))
+
+    def terms(t, c):
+        tt(cols("zt", 512 * c, 512 * c + 512), q(EB[c]), cols("g%d" % t, 512 * c, 512 * c + 512), Op.mult)
+
+    def summed_terms(t, n, bank):
+        for j in range(n):
+            k = 16 - n + j
+            o = cols("zg", C * j, C * j + C)
+            act(o, IND(cols("zt", 0, W + 1), cols("pl%d" % (t % 2), 16 * k, 16 * k + 16)), Fn.Identity)
+            mm(q(bank, 0, C), A("idf"), o, j == 0, j == n - 1)
+
+    def gather_terms(t, ks):
+        for k in ks:
+            src = IND(cols("zt", 0, W + 1), cols("pl%d" % (t % 2), 16 * k, 16 * k + 16))
+            o = A("yb" if k % 2 else "ya")
+            if k == 1 or (k == 0 and t == 0):
+                cp(o, src)
+            else:
+                tt(o, src, A("yin") if k == 0 else o, Op.add)
+
+    def close_terms():
+        tt(A("ys"), A("ya"), A("yb"), Op.add)
+        rotate("yin", "ys", 1)
+
+    def taken(t, on_dve):
+        win = cols("xu", 0, W + 1)
+        order = [k for k in range(0, 16, 2)]
+        for k in order:
+            o, src = cols("xg", k * C, k * C + 2 * C), IND(win, cols("pl%d" % (t % 2), 16 * k, 16 * k + 32))
+            if k in on_dve:
+                cp(o, src)
+            else:
+                act(o, src, Fn.Identity)
+        n = len(on_dve) // 1
+        seq = sorted(order, key=lambda k: (on_dve.index(k) if k in on_dve else [j for j in order if j not in on_dve].index(k)))
+        for k in seq:
+            for kk in (k, k + 1):
+                for h in range(2):
+                    a = kk * C + 128 * h
+                    mm(q(4, 2 * kk + h, C, 32), cols("xg", a, a + 128), A("b32"))
+            if k != seq[-1]:
+                sums(k, seq)
+        return seq
+
+    def sums(k, seq):
+        for kk in (k, k + 1):
+            for h in range(2):
+                a = kk * C + 128 * h
+                mm(q(5 + h, 0, 128), A("r32" if h else "i32"), cols("xg", a, a + 128), kk == seq[0], kk == seq[-1] + 1)
+
+    def tapes(t, seq):
+        sx = q(4, 0, C)
+        side = q(4, C, 2 * C)
+        act(A("tnb"), sx, Fn.Relu, bias=1.0, scale=-1.0)
+        tt(A("tn"), A("cb"), sx, Op.subtract)
+        tt(side, sx, A("late"), Op.min)
+        tt(cols("lv", 0, C - 2), q(4, 2, C), cols("tn", 0, C - 2), Op.min)
+        sums(seq[-1], seq)
+        for h in range(2):
+            mm(q(7, 128 * h, 128 * h + 128), cols("tnb", h, C, 2), A("idb"))
+        act(A("ntp"), q(7, 0, C), Fn.Identity)
+        for h in range(2):
+            mm(q(7, C + 128 * h, C + 128 * h + 128), A("blr" if h else "blk"), cols("ntp", 128 * h, 128 * h + 128))
+        next_table(t + 1)
+        weights(0)
+        weights(1)
+        tt(A("zz"), side, A("lv"), Op.max)
+        for h in range(2):
+            o, d = q(4, h, C, 2), cols("zz", h, C, 2)
+            add("dve", lambda o=o, d=d: g.vector.tensor_tensor_scan(o[0], T["seg"][:], d[0], 0.0, Op.mult, Op.add), [o], [d, A("seg")])
+        ts(side, A("zz"), B, Op.is_ge, -16 * B, Op.mult)
+        tt(A("tk"), side, A("ti"), Op.add)
+        tt(A("vv"), sx, A("tk"), Op.add)
+        at = [0]
+
+        def moves(src, spans, bank):
+            for j, (d, a, b, n) in enumerate(spans):
+                o = cols("cl", at[0], at[0] + 16 * n)
+                at[0] += 16 * n
+                ts(o, A(src, ALL, ALL, slice(2 * a, 2 * a + 2 * n)), d * B, Op.max, (d + 1) * B, Op.min)
+                mm(A(bank, ALL, slice(0, 8), slice(2 * b, 2 * b + 2 * n)), A("idf"), o, j == 0, j == len(spans) - 1)
+
+        moves("vv", [(0, 0, 0, 16)] + [(d, 2 * d - 1, d - 1, 17 - 2 * d) for d in range(1, 9)], "q3")
+        tt(A("e2"), A("vv", ALL, ALL, slice(30, 32)), A("nt%d" % t), Op.add)
+        tt(A("d1"), q(7, C, 2 * C), A("drot"), Op.mult)
+        cp(A("er"), IND(A("e2"), A("el")))
+        for h in range(2):
+            tt(cols("d2", 128 * h, 128 * h + 128), q(5 + h, 0, 128), cols("d1", 128 * h, 128 * h + 128), Op.add)
+        weights(2)
+        weights(3)
+        ts(A("di"), A("d2"), 1.0 / 16, Op.mult, -15.0 / 32, Op.add)
+        ts(A("kb"), A("di"), -SC / 32, Op.mult, BIG, Op.add)
+        cp(A("acc"), q(3, 0, C))
+        ts(A("nw"), A("acc", ALL, ALL, slice(0, 16)), W - 1, Op.bitwise_and)
+        tt(A("v2"), A("nw"), A("er"), Op.add)
+        moves("v2", [(e, 0, 16 - e, e) for e in range(8, 0, -1)], "q2")
+        terms(t, 0)
+        late = A("acc", ALL, ALL, slice(16, 32))
+        tt(late, A("q2", ALL, slice(0, 8), slice(16, 32)), late, Op.add)
+        ts(cols("ti", 0, C, 2), A("acc", ALL, ALL, slice(0, 32, 2)), W - 1, Op.bitwise_and)
+        ts(cols("ti", 33, C, 2), A("acc", ALL, slice(0, 7), slice(1, 32, 2)), W - 1, Op.bitwise_and)
+        ts(cols("ti", 1, 32, 2), A("acc", ALL, 7, slice(1, 32, 2)), W - 1, Op.bitwise_and)
+        cp(A("th"), A("ti"))
+        to_list("th", 4)
+        profile(t + 1)
+        terms(t, 1)
+        time_lists(4)
+        terms(t, 2)
+        terms(t, 3)
+        if t == 0:
+            rotate("drot", "di", 1)
+
+    def next_table(t):
+        tab = "tab%d" % (t % 2)
+
+        def out(i, ps):
+            act(cols(tab, i, W, 16), ps, Fn.Identity, scale=SC)
+            if i == 0:
+                act(cols(tab, W, W + 1), q(3, 0, 1), Fn.Identity, scale=SC)
+        spread("ul%d" % t, "x%d" % t, lambda i: True, out, [3, 2, 0, 1])
+
+    def early_terms(t):
+        gather_terms(t, range(0, NF))
+        tt(A("yb"), q(0, 0, C), A("yb"), Op.add)
+
+    def later_terms(t):
+        gather_terms(t, range(NF, 16 - NY))
+        close_terms()
+
+    def taken_columns(t):
+        x = "x%d" % t
+
+        def out(i, ps):
+            if i // 4 % 2:
+                act(cols("xu", i, W, 16), ps, Fn.Relu, bias=-256.0)
+            else:
+                tt(cols("xu", i, W, 16), ps, cols(x, i, W, 16), Op.min)
+        spread("u%d" % t, x, lambda i: i // 4 % 2 == 1, out, [0, 1, 2, 3])
+
+    for t in range(VI):
+        hear(t)
+        if t == 0:
+            act_constants()
+        else:
+            summed_terms(t - 1, NY, 0)
+        keys(t)
+        claims(t)
+        if t == 0:
+            histogram(t, [lambda: None, late_constants])
+        else:
+            histogram(t, [lambda: early_terms(t - 1), lambda: later_terms(t - 1)])
+        if t < VI - 1:
+            flags(t)
+            if t == 0:
+                send(2, 1, A("ul1"), A("u0"))
+                send(3, 2, A("x2"), A("x0"))
+                send(4, 2, A("g2"), A("g0"))
+                owners(t)
+                taken_columns(t)
+            else:
+                tt(A("us"), A("u1"), A("ul1"), Op.add)
+                send(5, 1, A("ul2"), A("us"))
+                owners(t)
+                taken_columns(t)
+            seq = taken(t, ONV)
+            diffs(t, 0, W)
+            tapes(t, seq)
+        else:
+            owners(t)
+            for c in range(4):
+                diffs(t, 512 * c, 512 * c + 512)
+                weights(c)
+            for c in range(4):
+                terms(t, c)
+            summed_terms(t, NZ, 4)
+            gather_terms(t, range(0, 15 - NZ))
+            o = A("yb" if NZ % 2 else "ya")
+            tt(o, q(4, 0, C), o, Op.add)
+            gather_terms(t, range(15 - NZ, 16 - NZ))
+            tt(A("ys"), A("ya"), A("yb"), Op.add)
+            rotate("y", "ys", -(VI - 1), ("sp", "act", "sp"))
+    emit(ops, queue, T)
+
+
+def emit(ops, queue, T):
+    seen = {}
+    for i, o in enumerate(ops):
+        dep = set()
+        for mine, write in ((o["w"], True), (o["r"], False)):
+            for (name, p0, p1, m) in mine:
+                bank = name in SCRATCH and SCRATCH[name][0] == P
+                for (j, wr, a0, a1, b) in seen.get(name, []):
+                    other = ops[j]
+                    same = other["eng"] == o["eng"] and other["sem"] is None and o["sem"] is None
+                    if same and o["eng"] == "pe":
+                        continue
+                    if (bank and not same) or ((wr or write) and a0 <= p1 and p0 <= a1 and b & m):
+                        dep.add(j)
+        o["dep"] = dep
+        for mine, write in ((o["r"], False), (o["w"], True)):
+            for (name, p0, p1, m) in mine:
+                keep = []
+                for e in seen.get(name, []):
+                    same = ops[e[0]]["eng"] == o["eng"] and ops[e[0]]["sem"] is None and o["sem"] is None
+                    if (write or (same and not e[1])) and p0 <= e[2] and e[3] <= p1 and (e[4] | m) == m:
+                        continue
+                    keep.append(e)
+                keep.append((i, write, p0, p1, m))
+                seen[name] = keep
+    known = {e: {} for e in ENG}
+    for i, o in enumerate(ops):
+        o["wait"] = []
+        if o["eng"] is None:
+            o["know"] = {o["sem"]: i}
+            continue
+        kn = known[o["eng"]]
+        for j in sorted(o["dep"], reverse=True):
+            key = ops[j]["sem"] or ops[j]["eng"]
+            if kn.get(key, -1) >= j:
+                continue
+            o["wait"].append(j)
+            ops[j]["inc"] = True
+            for k2, val in ops[j]["know"].items():
+                if kn.get(k2, -1) < val:
+                    kn[k2] = val
+        o["know"] = dict(kn)
+        o["know"][o["sem"] or o["eng"]] = i
+    cnt = {e: 0 for e in ENG}
+    waited = {}
+    for o in ops:
+        if o["eng"] is None:
+            continue
+        for j in o["wait"]:
+            p = ops[j]
+            key, val = (p["sem"], p["n"]) if p["sem"] else (p["eng"], p["val"])
+            queue[o["eng"]].wait_ge(T.sem[key], val)
+            waited[key] = max(waited.get(key, 0), val)
+        ins = o["call"]()
+        if o["sem"]:
+            if o["extra"] is None:
+                ins.then_inc(T.sem[o["sem"]], 16)
+        elif o["inc"]:
+            cnt[o["eng"]] += 1
+            o["val"] = cnt[o["eng"]]
+            ins.then_inc(T.sem[o["eng"]], 1)
+    for o in ops:
+        if o["sem"] and waited.get(o["sem"], 0) < o["n"]:
+            queue["gp"].wait_ge(T.sem[o["sem"]], o["n"])
+
+
+def rank_program(g, core, T, topo):
+    rank = T.rank_of(core)
+    if rank is None:
+        return
+    build(g, core, T, topo, rank)

@@ -1,64 +1,70 @@
-import numpy as np
 from concourse.mybir import AluOpType as Op, ActivationFunctionType as Fn
 
 N, W, C, VI = 8, 2048, 256, 3
-BIG = 12288.0
-SC = 113.0 / 16
-BIG32 = 1.5 * 2 ** 29
+BIG = 1.5 * 2 ** 29
+BIGH = 1.5 * 2 ** 13
+M32 = 1.5 * 2 ** 28
+M1 = 1.5 * 2 ** 23
+M512 = 1.5 * 2 ** 32
 B = 8192.0
-NA = 8
-NZ = 6
-NY = 7
-NF = 5
-HALVES = (True, False, False)
-ONV = [0, 2, 4]
-EB = (0, 1, 6, 5)
+HALF = (8.0, 8 + 3.0 / 128)
+COPIES = 4
+NONE = W + 2
+LEVELS = (3, 1)
+VIA_ACT = ((2, 3), (), ())
+HB = (2, 3, 0, 1)
+EXP_AT = (1, 3, 5, 7)
+LAST = (0, 256, 768, 1280, 1792, 2048)
+ASIDE = True
 
 S, P = "sbuf", "psum"
+X3 = [128, W + 16]
+H3 = [128, 16, 16]
 SCRATCH = {
-    "x0": (S, [128, W], "bfloat16"), "x1": (S, [128, W], "bfloat16"), "x2": (S, [128, W], "bfloat16"),
+    "x0": (S, X3, "bfloat16"), "x1": (S, X3, "bfloat16"), "x2": (S, X3, "bfloat16"),
     "g0": (S, [128, W], "bfloat16"), "g1": (S, [128, W], "bfloat16"), "g2": (S, [128, W], "bfloat16"),
-    "tab0": (S, [128, W + 8], "float32"), "tab1": (S, [128, W + 8], "float32"),
-    "xu": (S, [128, W + 16], "bfloat16"), "zt": (S, [128, W + 8], "float32"), "wv": (S, [128, W], "float32"),
-    "xg": (S, [128, 4096], "bfloat16"), "xa": (S, [128, 2048], "bfloat16"), "zg": (S, [128, 2048], "float32"),
+    "xu": (S, X3, "bfloat16"), "zt": (S, [128, W + 8], "float32"), "wv": (S, [128, W], "float32"),
+    "xg": (S, [128, 4096], "bfloat16"), "xa": (S, [128, 2048], "bfloat16"), "zg": (S, [128, 2, 2048], "float32"),
     "ind0": (S, [128, 4096], "bfloat16"), "ind1": (S, [128, 4096], "bfloat16"),
-    "oa": (S, [128, 2, 8192], "bfloat16"), "ob": (S, [128, 2, 33 * 128], "bfloat16"),
-    "ivi": (S, [128, C], "int32"), "ivf": (S, [128, C], "float32"), "taui": (S, [128, C], "int32"), "tauf": (S, [128, C], "float32"),
-    "di": (S, [128, C], "int32"), "drot": (S, [128, C], "int32"), "kb": (S, [128, C], "float32"),
-    "kt0": (S, [128, 520], "float32"), "kt1": (S, [128, 520], "float32"),
-    "lo": (S, [128, C], "int32"), "hi": (S, [128, C], "int32"), "mb": (S, [128, C], "bfloat16"),
-    "tu": (S, [128, C], "int32"), "ti": (S, [128, C], "int32"), "th": (S, [128, C], "float16"),
+    "oa": (S, [128, 2, 8192], "float16"), "ob": (S, [128, 2, 33 * 128], "float16"),
+    "ivi": (S, [128, C], "int32"), "ivh": (S, [128, C], "float16"), "taui": (S, [128, C], "int32"), "tauh": (S, [128, C], "float16"),
+    "di": (S, [128, C], "int32"), "df": (S, [128, C], "float32"), "dri": (S, [128, C], "int32"), "drf": (S, [128, C], "float32"),
+    "kt": (S, [128, 704], "float32"), "lo": (S, [128, C], "float32"), "mb": (S, [128, C], "bfloat16"),
+    "tu": (S, [128, C], "int32"), "ti": (S, H3, "int32"), "th": (S, H3, "float16"),
     "of0": (S, [128, C], "uint16"), "of1": (S, [128, C], "uint16"), "pl0": (S, [128, C], "uint16"), "pl1": (S, [128, C], "uint16"),
-    "thr": (S, [128, C], "float32"), "late": (S, [128, C], "float32"), "mx": (S, [128, C], "float32"), "pen": (S, [128, C], "float32"),
-    "p0": (S, [128, C], "int32"), "pw": (S, [128, C], "int32"), "pp": (S, [128, C], "float32"), "ph": (S, [128, C], "float16"),
-    "bi": (S, [128, C], "int32"), "aa": (S, [128, C], "bfloat16"), "bb": (S, [128, C], "bfloat16"),
-    "hs0": (S, [128, 4, 64], "float32"), "hs1": (S, [128, 4, 64], "float32"), "r0": (S, [128, C], "bfloat16"), "r1": (S, [128, C], "bfloat16"),
-    "uq": (S, [128, 128], "bfloat16"), "u0": (S, [128, 128], "bfloat16"), "u1": (S, [128, 128], "bfloat16"), "us": (S, [128, 128], "bfloat16"),
-    "ul1": (S, [128, 128], "bfloat16"), "ul2": (S, [128, 128], "bfloat16"),
-    "i1": (S, [128, 128], "float32"), "i2": (S, [128, 128], "float32"), "i3": (S, [128, 128], "float32"), "idx": (S, [128, 128], "uint16"),
-    "cb": (S, [128, C], "float32"), "tn": (S, [128, C], "float32"), "tnb": (S, [128, C], "bfloat16"), "lv": (S, [128, C], "float32"),
-    "zz": (S, [128, C], "float32"), "tk": (S, [128, C], "float32"),
-    "vv": (S, [128, 8, 32], "float32"), "acc": (S, [128, 8, 32], "int32"), "cl": (S, [128, 2048], "float32"), "b32": (S, [128, 8], "bfloat16"),
-    "e2": (S, [128, 16], "float32"), "er": (S, [128, 128], "float32"), "nw": (S, [128, 128], "int32"), "v2": (S, [128, 8, 16], "float32"),
+    "t0": (S, [128, C], "float32"), "ee": (S, H3, "bfloat16"),
+    "bi": (S, H3, "int32"), "aa": (S, [128, 2, 1024], "bfloat16"), "bb": (S, [128, 2, 512], "bfloat16"),
+    "rr": (S, [128, C], "float16"), "rw": (S, [128, 4, 32], "float16"),
+    "u0": (S, [128, 128], "bfloat16"), "u1": (S, [128, 128], "bfloat16"), "us": (S, [128, 128], "bfloat16"),
+    "ul1": (S, [128, 128], "bfloat16"), "ul2": (S, [128, 128], "bfloat16"), "idx": (S, [128, 128], "uint16"),
+    "tnb": (S, [128, C], "bfloat16"), "sl": (S, [128, 512], "float32"), "seg": (S, [128, 512], "float32"), "tk": (S, [128, C], "float32"),
+    "vv": (S, [128, 16, 17], "float32"), "acc": (S, H3, "int32"), "cl": (S, [128, 2048], "float32"), "c0": (S, [128, C], "float32"),
+    "e2": (S, [128, 16], "float32"), "er": (S, [128, 128], "float32"), "nw": (S, [128, 128], "int32"), "v2": (S, [128, 16, 8], "float32"),
     "nt0": (S, [128, 16], "float32"), "nt1": (S, [128, 16], "float32"),
     "ntp": (S, [128, C], "bfloat16"), "d1": (S, [128, C], "float32"), "d2": (S, [128, C], "float32"),
-    "ya": (S, [128, C], "float32"), "yb": (S, [128, C], "float32"), "ys": (S, [128, C], "float32"), "yin": (S, [128, C], "float32"),
+    "ya": (S, [128, 128], "float32"), "yb": (S, [128, 128], "float32"), "ys": (S, [128, C], "float32"), "yacc": (S, [128, C], "float32"),
     "one": (S, [128, 128], "float32"), "tr1": (S, [128, 128], "float32"), "tri": (S, [128, 128], "float32"), "blf": (S, [128, 128], "float32"),
-    "e8": (S, [128, 128], "float32"),
-    "idf": (S, [128, 128], "float32"), "idb": (S, [128, 128], "bfloat16"), "idh": (S, [128, 128], "bfloat16"), "id7": (S, [128, 128], "bfloat16"),
-    "idm": (S, [128, 128], "bfloat16"), "i32": (S, [128, 128], "bfloat16"), "r32": (S, [128, 128], "bfloat16"),
-    "blk": (S, [128, 128], "bfloat16"), "blr": (S, [128, 128], "bfloat16"), "b16": (S, [128, 8], "bfloat16"),
+    "e8": (S, [128, 128], "float32"), "trh": (S, [128, 128], "float16"), "e8h": (S, [128, 128], "float16"),
+    "idf": (S, [128, 128], "float32"), "idb": (S, [128, 128], "bfloat16"), "id7": (S, [128, 128], "bfloat16"), "idm": (S, [128, 128], "bfloat16"),
+    "idh": (S, [128, 128], "float16"), "ish": (S, [128, 128], "float16"), "i2": (S, [128, 128], "bfloat16"), "r2": (S, [128, 128], "bfloat16"),
+    "back1": (S, [128, 128], "float32"), "back2": (S, [128, 128], "float32"), "idn": (S, [128, 128], "bfloat16"),
+    "blk": (S, [128, 128], "bfloat16"), "blr": (S, [128, 128], "bfloat16"), "b4k": (S, [128, 8], "bfloat16"), "b3": (S, [128, 8, 3], "bfloat16"),
     "s3": (S, [128, 8, 48], "float16"), "c256": (S, [128, W], "bfloat16"), "sel": (S, [128, W], "bfloat16"),
-    "wc": (S, [128, 8], "bfloat16"), "seg": (S, [128, 128], "float32"),
-    "k1": (S, [128, 8], "int32"), "k2": (S, [128, 8], "int32"), "k3": (S, [128, 8], "float32"), "k4": (S, [128, 8], "float32"), "el": (S, [128, 8], "uint16"),
+    "cin": (S, [128, 512], "bfloat16"), "off": (S, [128, 128], "bfloat16"),
+    "wc": (S, [128, 2], "bfloat16"), "idu": (S, [128, 128], "float16"), "isu": (S, [128, 128], "float16"),
+    "k3": (S, [128, 8], "int32"), "k4": (S, [128, 8], "int32"), "el": (S, [128, 8], "uint16"),
 }
 for _b in range(8):
-    SCRATCH["q%d" % _b] = (P, [128, 16, 32] if _b in (2, 3) else [128, 4, 128] if _b in (6, 7) else [128, 512], "float32")
+    SCRATCH["q%d" % _b] = (P, [128, 16, 32] if _b == 4 else [128, 4, 128] if _b in (6, 7) else [128, 512] if _b < 2 else [128, 32, 16], "float32")
 SHAPES = {"xs": [128, W], "gn": [128, W], "tau": [8, C], "iv": [128, C], "pf": [128, C], "y": [128, C]}
 ENG = ("pe", "act", "dve", "gp", "sp")
 SEMAPHORES = ["pe", "act", "dve", "gp"] + ["d%d" % i for i in range(30)] + ["l%d" % i for i in range(6)] + ["a%d" % i for i in range(6)]
 ALL = slice(None)
 MASKS = {}
+ORDER = []
+CYC, PCYC, GATHER, VCALL, SCALL, WAKE, LOCAL, REMOTE, LRATE, RRATE = 0.83, 0.45, 1.4, 15, 65, 130, 2500, 4000, 150, 40
+ROUNDS = 6
+SPAN = []
 
 
 def build(g, core, T, topo, rank):
@@ -67,485 +73,507 @@ def build(g, core, T, topo, rank):
     queue = {"pe": g.tensor, "act": g.scalar, "dve": g.vector, "gp": g, "sp": g.sync}
 
     def A(name, *ix):
-        shape = SHAPES[name] if name in SHAPES else SCRATCH[name][1]
+        where, shape, dt = (None, SHAPES[name], "") if name in SHAPES else SCRATCH[name]
         ix = list(ix) + [ALL] * (len(shape) - len(ix))
         rs = [range(n)[s] if isinstance(s, slice) else range(s, s + 1) for s, n in zip(ix, shape)]
         key = (shape[-1],) + tuple((r.start, r.stop, r.step) for r in rs[1:])
         if key not in MASKS:
             row = sum(1 << c for c in rs[-1])
             MASKS[key] = row if len(shape) == 2 else sum(row << (b * shape[-1]) for b in rs[1])
-        return (T[name][tuple(ix)], [(name, rs[0][0], rs[0][-1], MASKS[key])])
+        return (T[name][tuple(ix)], [(name, rs[0][0], rs[0][-1], MASKS[key])], MASKS[key].bit_count(), 2 if "16" in dt else 4, where)
 
-    def cols(name, a, b, s=1):
-        return A(name, ALL, slice(a, b, s))
+    def cols(name, a, b, s=1, part=ALL):
+        shape = SHAPES[name] if name in SHAPES else SCRATCH[name][1]
+        if len(shape) == 2:
+            return A(name, part, slice(a, b, s))
+        n = shape[2]
+        if a // n == (b - 1) // n:
+            return A(name, part, a // n, slice(a % n, (b - 1) % n + 1, s))
+        return A(name, part, slice(a // n, b // n), slice(a % n, n, s))
+
+    def q(b, a=0, e=512, s=1, part=ALL):
+        return cols("q%d" % b, a, e, s, part)
 
     def IND(win, off):
-        return (win[0].indirect(off[0]), win[1] + off[1])
+        return (win[0].indirect(off[0]), win[1] + off[1], 16 * off[2], win[3], "gather")
 
-    def add(eng, call, outs, ins, sem=None, n=0, extra=None):
-        ops.append({"eng": eng, "call": call, "w": [b for o in outs for b in o[1]],
+    def add(eng, call, outs, ins, ns, sem=None, n=0, extra=None, wake=WAKE, after=()):
+        ops.append({"eng": eng, "call": call, "w": [b for o in outs for b in o[1]], "ns": ns, "wake": wake, "after": list(after),
                     "r": [b for i in ins if isinstance(i, tuple) for b in i[1]], "sem": sem, "n": n, "inc": False, "extra": extra})
+        return len(ops) - 1
 
     def v(x):
         return x[0] if isinstance(x, tuple) else x
 
+    def vtime(out, a, slow=False):
+        if a[4] == "gather":
+            return 50 + CYC * GATHER * out[2]
+        return VCALL + CYC * max(64, out[2] * (2 if slow else 0.5 if out[3] == a[3] == 2 else 1))
+
     def ts(out, in0, s1, op0, s2=None, op1=None):
         if op1 is None:
-            add("dve", lambda: g.vector.tensor_scalar(out[0], in0[0], v(s1), None, op0), [out], [in0, s1])
+            add("dve", lambda: g.vector.tensor_scalar(out[0], in0[0], v(s1), None, op0), [out], [in0, s1], vtime(out, in0))
         else:
-            add("dve", lambda: g.vector.tensor_scalar(out[0], in0[0], v(s1), v(s2), op0, op1), [out], [in0, s1, s2])
+            add("dve", lambda: g.vector.tensor_scalar(out[0], in0[0], v(s1), v(s2), op0, op1), [out], [in0, s1, s2], vtime(out, in0))
 
     def tt(out, a, b, op):
-        add("dve", lambda: g.vector.tensor_tensor(out[0], a[0], b[0], op), [out], [a, b])
+        add("dve", lambda: g.vector.tensor_tensor(out[0], a[0], b[0], op), [out], [a, b], vtime(out, a, a[4] == b[4] == S))
 
     def cp(out, a):
-        add("dve", lambda: g.vector.tensor_copy(out[0], a[0]), [out], [a])
+        add("dve", lambda: g.vector.tensor_copy(out[0], a[0]), [out], [a], vtime(out, a))
 
     def ms(out, c):
-        add("dve", lambda: g.vector.memset(out[0], c), [out], [])
+        add("dve", lambda: g.vector.memset(out[0], c), [out], [], vtime(out, out))
 
     def act(out, a, f, bias=0.0, scale=1.0):
-        add("act", lambda: g.scalar.activation(out[0], a[0], f, bias=float(bias), scale=float(scale)), [out], [a])
+        add("act", lambda: g.scalar.activation(out[0], a[0], f, bias=float(bias), scale=float(scale)), [out], [a],
+            SCALL + CYC * out[2] * (GATHER if a[4] == "gather" else 1))
 
     def mm(out, l, r, start=True, stop=True):
-        add("pe", lambda: g.tensor.matmul(out[0], l[0], r[0], start, stop), [out], [l, r])
+        add("pe", lambda: g.tensor.matmul(out[0], l[0], r[0], start, stop), [out], [l, r], PCYC * max(min(64, l[2]), r[2]) * (4 if l[3] == 4 else 1))
 
     def sel(out, a, pat, op, base, cm):
-        add("gp", lambda: g.affine_select(out[0], a[0], pat, op, 0.0, base, cm), [out], [a])
+        add("gp", lambda: g.affine_select(out[0], a[0], pat, op, 0.0, base, cm), [out], [a], 170 + 2 * CYC * out[2])
 
     def iota(out, pat, base, cm, small):
         if small:
-            add("gp", lambda: g.iota(out[0], pat, base, cm, allow_small_or_imprecise_dtypes=True), [out], [])
+            add("gp", lambda: g.iota(out[0], pat, base, cm, allow_small_or_imprecise_dtypes=True), [out], [], 130 + 2 * CYC * out[2])
         else:
-            add("gp", lambda: g.iota(out[0], pat, base, cm), [out], [])
+            add("gp", lambda: g.iota(out[0], pat, base, cm), [out], [], 130 + 2 * CYC * out[2])
 
     def dma(eng, out, a):
         nd[0] += 1
-        add(eng, lambda: queue[eng].dma_start(out[0], a[0]), [out], [a], sem="d%d" % (nd[0] - 1), n=16)
+        side = out if out[4] else a
+        add(eng, lambda: queue[eng].dma_start(out[0], a[0]), [out], [a], 50, sem="d%d" % (nd[0] - 1), n=16, wake=LOCAL + 128 * side[2] * side[3] / LRATE)
 
-    def send(k, back, dst, src):
+    def dma_add(out, a):
+        nd[0] += 1
+        add("gp", lambda: g.dma_start(out[0], a[0], accum_op=Op.add), [out], [a, out], 100, sem="d%d" % (nd[0] - 1), n=16, wake=LOCAL + 128 * out[2] * out[3] / LRATE)
+
+    def send(k, back, dst, src, after=()):
         to = T.cores[(rank - back) % N]
         rid, pid = topo.addr(to)[:2]
         mask = topo.mask(core, to)
         n_out = len(topo.engines(core, to))
         n_in = len(topo.engines(T.cores[(rank + back) % N], core))
-        add("gp", lambda: g.remote_dma(dst[0], src[0], T.sem["a%d" % k], T.sem["l%d" % k], pid, rid, mask), [], [src], sem="l%d" % k, n=n_out, extra="remote")
-        add(None, None, [dst], [], sem="a%d" % k, n=n_in)
-
-    def q(b, a=0, e=512, s=1):
-        shape = SCRATCH["q%d" % b][1]
-        if len(shape) == 2:
-            return cols("q%d" % b, a, e, s)
-        n = shape[2]
-        if a // n == (e - 1) // n:
-            return A("q%d" % b, ALL, a // n, slice(a % n, (e - 1) % n + 1, s))
-        return A("q%d" % b, ALL, slice(a // n, e // n))
+        ns = REMOTE + 128 * src[2] * src[3] / RRATE
+        i = add("gp", lambda: g.remote_dma(dst[0], src[0], T.sem["a%d" % k], T.sem["l%d" % k], pid, rid, mask), [], [src], 2000 if k == 0 else 300,
+                sem="l%d" % k, n=n_out, extra="remote", wake=ns, after=after)
+        add(None, None, [dst], [], ns, sem="a%d" % k, n=n_in, after=[i])
+        return i
 
     dma("sp", A("ivi"), A("iv"))
     dma("act", A("taui", slice(0, 8)), A("tau"))
-    dma("sp", cols("x0", 0, 1024), cols("xs", 0, 1024))
-    dma("act", A("di"), A("pf"))
-    dma("act", cols("x0", 1024, W), cols("xs", 1024, W))
+    dma("sp", A("di"), A("pf"))
+    dma("act", cols("x0", 0, 1024), cols("xs", 0, 1024))
+    dma("sp", cols("x0", 1024, W), cols("xs", 1024, W))
+    dma("act", cols("x0", W, W + 16), cols("xs", 0, 16))
     dma("sp", A("g0"), A("gn"))
 
-    def rotate(dst, src, t, eng=("sp", "sp", "sp")):
-        s = (16 * t) % 128
-        dma(eng[0], cols(dst, 0, 128), cols(src, 0, 128))
-        dma(eng[1], A(dst, slice(s, 128), slice(128, C)), A(src, slice(0, 128 - s), slice(128, C)))
-        dma(eng[2], A(dst, slice(0, s), slice(128, C)), A(src, slice(128 - s, 128), slice(128, C)))
+    def rotate(dst, src):
+        dma("sp", cols(dst, 0, 128), cols(src, 0, 128))
+        dma("sp", A(dst, slice(16, 128), slice(128, C)), A(src, slice(0, 112), slice(128, C)))
+        dma("sp", A(dst, slice(0, 16), slice(128, C)), A(src, slice(112, 128), slice(128, C)))
 
-    rotate("drot", "pf", 1)
+    def shifted(dst, src, s, scale):
+        act(cols(dst, s, 128), cols(src, 0, 128 - s), Fn.Identity, scale=scale)
+        act(cols(dst, 0, s), cols(src, 128 - s, 128), Fn.Identity, scale=scale)
+
+    rotate("dri", "pf")
     ms(A("one"), 1.0)
     ms(A("s3"), 0.0)
     ms(A("c256"), 256.0)
-    ms(A("ob", ALL, ALL, slice(0, 128)), 1.0)
-    ms(A("ob", ALL, ALL, slice(32 * 128, 33 * 128)), -1.0)
-    for h in range(2):
-        for c in (0, 256, 512):
-            ms(cols("kt%d" % h, c, c + (8 if c == 512 else 128)), 1e9)
+    ms(A("kt"), 1e9)
+    ms(A("rw", ALL, ALL, slice(2, 32)), 0.0)
+    ms(cols("xu", W, W + 16), 0.0)
+    ms(cols("zt", W, W + 8), 0.0)
+    ms(A("seg"), 1.0)
+    ms(cols("seg", 0, 512, 32), 0.0)
+    ms(A("vv", ALL, ALL, slice(16, 17)), 0.0)
     sel(A("tr1"), A("one"), [[-16, 8], [0, 16]], Op.is_ge, 0, 1)
     sel(A("tri"), A("tr1"), [[1, 128]], Op.is_ge, 0, -1)
     sel(A("e8"), A("one"), [[-1, 8], [0, 16]], Op.is_equal, 0, 1)
     sel(A("idf"), A("one"), [[-1, 128]], Op.is_equal, 0, 1)
     sel(A("blf"), A("tr1"), [[16, 8], [0, 16]], Op.is_ge, 15, -1)
-    cp(A("ivf"), A("ivi"))
-    cp(A("tauf", slice(0, 8)), A("taui", slice(0, 8)))
+    sel(A("sel"), A("c256"), [[-1, 16], [-16, 8], [0, 16]], Op.is_equal, 0, 1)
+    iota(A("wc"), [[0, 2]], 128, 1, True)
+    iota(A("k3"), [[2, 8]], 0, 0, False)
+    iota(A("k4"), [[0, 8]], 0, 1, False)
+    cp(A("trh"), A("tri"))
+    cp(A("e8h"), A("e8"))
     cp(A("s3", ALL, ALL, slice(16, 32)), A("idf"))
-    for h in range(2):
-        mm(q(4, h, C, 2), cols("ivf", 128 * h, 128 * h + 128), A("tri"), True, False)
-        mm(q(4, h, C, 2), A("tauf", slice(0, 8), slice(128 * h, 128 * h + 128)), A("e8", slice(0, 8)), False, True)
-    for h in range(2):
-        mm(q(7, h, 16, 2), A("tauf", slice(0, 8), slice(128 * h, 128 * h + 128)), A("e8", slice(0, 8), slice(0, 128, 16)))
-    send(0, 1, A("x1"), A("x0"))
-    send(1, 1, A("g1"), A("g0"))
-    cp(A("tu"), q(4, 0, C))
-    ts(A("ti"), A("tu"), W - 1, Op.bitwise_and)
-    cp(A("th"), A("ti"))
+    for same, on, scale in (("idh", "ish", 0.25), ("idu", "isu", 1537.0 / 4096)):
+        ts(A(same), A("idf"), scale, Op.mult)
+        cp(cols(on, 2, 128), cols(same, 0, 126))
+        cp(cols(on, 0, 2), cols(same, 126, 128))
+    ts(A("k4"), A("k4"), 8, Op.bitwise_and, 3, Op.logical_shift_right)
+    tt(A("k3"), A("k3"), A("k4"), Op.add)
+    cp(A("el"), A("k3"))
+    for name, scale in (("id7", 7.0), ("idm", -3.5 / 32), ("idb", 1.0), ("idn", -1.0 / 256), ("i2", 2.0)):
+        act(A(name), A("idf"), Fn.Identity, scale=scale)
+    act(A("b4k"), cols("blf", 0, 128, 16), Fn.Identity, scale=4096.0)
+    act(A("blk"), A("blf"), Fn.Identity, scale=1.0 / 16)
+    shifted("r2", "idf", 16, 2.0)
+    shifted("blr", "blf", 16, 1.0 / 16)
+    shifted("back1", "idf", 112, 1.0)
+    shifted("back2", "idf", 96, 1.0)
+    for j, w in enumerate((-512.0, 32.0, 8192.0)):
+        act(A("b3", ALL, ALL, j), cols("blf", 0, 128, 16), Fn.Identity, scale=w)
+    act(cols("cin", 0, 512, 2), cols("c256", 0, C), Fn.Identity, scale=0.0)
+    act(cols("cin", 1, 512, 2), cols("c256", 0, C), Fn.Identity, scale=16.0)
+    act(A("off"), A("one"), Fn.Identity, scale=-15.0 / 32)
 
-    def to_list(src, bank):
+    cp(A("ivh"), A("ivi"))
+    cp(A("tauh", slice(0, 8)), A("taui", slice(0, 8)))
+    cp(A("df"), A("di"))
+    for h in range(2):
+        o = A("q5", ALL, slice(16 + h, 32, 2))
+        mm(o, cols("ivh", 128 * h, 128 * h + 128), A("trh"), True, False)
+        mm(o, A("tauh", slice(0, 8), slice(128 * h, 128 * h + 128)), A("e8h", slice(0, 8)), False, True)
+    for h in range(2):
+        mm(q(7, h, 16, 2), A("tauh", slice(0, 8), slice(128 * h, 128 * h + 128)), A("e8h", slice(0, 8), slice(0, 128, 16)))
+    act(A("nt0"), q(7, 0, 16), Fn.Identity, bias=W, scale=-1.0)
+    act(cols("nt1", 0, 16, 2), cols("nt0", 0, 16, 2), Fn.Identity)
+    act(cols("nt1", 3, 16, 2), cols("nt0", 1, 14, 2), Fn.Identity)
+    act(cols("nt1", 1, 2), cols("nt0", 15, 16), Fn.Identity)
+    cp(A("tu"), q(5, C, 2 * C))
+    ts(A("ti"), A("tu"), W - 1, Op.bitwise_and)
+    send(0, 1, A("x1"), A("x0"))
+
+    def to_list(srcs, bank):
         for m in range(8):
             for gp in range(4):
                 for e in range(2):
-                    gg = 2 * gp + e
-                    mm(A("q%d" % bank, slice(32 * gp, 32 * gp + 32), slice(m, C, 8)), A("s3", ALL, m, slice(16 - 16 * e, 48 - 16 * e)),
-                       cols(src, 32 * gg, 32 * gg + 32), e == 0, e == 1)
+                    for src in srcs:
+                        a = 64 * gp + 32 * e
+                        mm(q(bank, m, C, 8, slice(32 * gp, 32 * gp + 32)), A("s3", ALL, m, slice(16 - 16 * e, 48 - 16 * e)),
+                           A(src, ALL, slice(a // 16, a // 16 + 2)),
+                           e == 0 and src == srcs[0], e == 1 and src == srcs[-1])
 
-    def profile(t):
-        if t == 0:
-            ts(A("kb"), A("di"), -SC / 32, Op.mult, BIG, Op.add)
-        ts(A("lo"), A("di"), 1.0 / 32, Op.mult, (15.5 - 144) / 32 - 256, Op.add)
-        ts(A("hi"), A("di"), 1.0 / 32, Op.mult, (144 - 15.5) / 32, Op.add)
-        tt(A("mb"), A("lo"), A("hi"), Op.add)
+    def centres(bank):
+        act(q(bank, C, 2 * C), A("df"), Fn.Identity, bias=M32, scale=1 + 2.0 ** -15)
+        act(A("lo"), A("df"), Fn.Identity, bias=-M32 - 8192, scale=1 - 2.0 ** -15)
+        tt(A("mb"), q(bank, C, 2 * C), A("lo"), Op.add)
 
-    def time_lists(bank):
-        ts(A("of1"), q(bank, 0, C), 1.0, Op.add)
+    def times(bank):
+        cp(A("th"), A("ti"))
+        to_list(["th"], bank)
         cp(A("of0"), q(bank, 0, C))
-
-    to_list("th", 5)
-    act(cols("tab0", 0, 1024), cols("x0", 0, 1024), Fn.Identity, scale=SC)
-    act(cols("tab0", W, W + 1), cols("x0", 0, 1), Fn.Identity, scale=SC)
-    act(cols("tab0", 1024, W), cols("x0", 1024, W), Fn.Identity, scale=SC)
-    profile(0)
-    ts(A("id7"), A("idf"), 7.0, Op.mult)
-    ts(A("idm"), A("idf"), -3.5, Op.mult)
-    cp(A("blk"), A("blf"))
-    ts(A("b16"), cols("blf", 0, 128, 16), 16.0, Op.mult)
-    time_lists(5)
-    iota(cols("wc", 0, 1), [[0, 1]], 128, 1, True)
-    iota(A("k1"), [[0, 8]], 0, 1, False)
-    iota(A("k3"), [[2, 8]], 0, 0, True)
-    sel(A("sel"), A("c256"), [[-1, 16], [-16, 8], [0, 16]], Op.is_equal, 0, 1)
-
-    def late_constants():
-        ms(cols("xu", W, W + 16), 0.0)
-        ms(cols("zt", W, W + 8), 0.0)
-        ms(A("seg"), 1.0)
-        ms(cols("seg", 0, 128, 16), 0.0)
-        ms(cols("lv", C - 2, C), 0.0)
-        ms(A("cb"), B)
-        ms(cols("cb", 30, C, 32), 0.0)
-        ms(cols("cb", 31, C, 32), 0.0)
-        ts(A("b32"), cols("blf", 0, 128, 16), 32.0, Op.mult)
-        ts(A("k2"), A("k1"), 1, Op.bitwise_and)
-        tt(A("k4"), A("k2"), A("k3"), Op.add)
-        cp(A("el"), A("k4"))
-
-    def act_constants():
-        act(A("idb"), A("idf"), Fn.Identity)
-        act(A("idh"), A("idf"), Fn.Identity, scale=0.5)
-        act(A("i32"), A("idf"), Fn.Identity, scale=32.0)
-        act(cols("r32", 16, 128), cols("idf", 0, 112), Fn.Identity, scale=32.0)
-        act(cols("r32", 0, 16), cols("idf", 112, 128), Fn.Identity, scale=32.0)
-        act(cols("blr", 16, 128), cols("blf", 0, 112), Fn.Identity)
-        act(cols("blr", 0, 16), cols("blf", 112, 128), Fn.Identity)
-        act(A("nt0"), q(7, 0, 16), Fn.Identity, bias=W, scale=-1.0)
-        act(cols("nt1", 0, 16, 2), cols("nt0", 0, 16, 2), Fn.Identity)
-        act(cols("nt1", 3, 16, 2), cols("nt0", 1, 14, 2), Fn.Identity)
-        act(cols("nt1", 1, 2), cols("nt0", 15, 16), Fn.Identity)
-
-    def hear(t):
-        tab = cols("tab%d" % (t % 2), 0, W + 1)
-        via_act = [(1, k) for k in range(0, 16, 2)] + [(0, k) for k in range(16 - NA, 16, 2)]
-        direct = list(range(0, 16 - NA, 2))
-        pend = []
-
-        def count(w, k):
-            for kk in (k, k + 1):
-                for h in range(2):
-                    a = kk * C + 128 * h
-                    mm(q(4, C * w + 2 * kk + h, C * w + C, 32), cols("ind%d" % w, a, a + 128), cols("blk", 0, 128, 16) if w else A("b16"))
-
-        def one_direct(k):
-            for kk in (k, k + 1):
-                tt(cols("ind0", kk * C, kk * C + C), IND(tab, cols("of0", 16 * kk, 16 * kk + 16)), A("kb"), Op.add)
-            o = cols("ind0", k * C, k * C + 2 * C)
-            ts(o, o, BIG, Op.is_equal)
-            pend.append((0, k))
-
-        def front(j):
-            w, k = via_act[j]
-            s = (j % 4) * 512
-            act(cols("xa", s, s + 512), IND(tab, cols("of%d" % w, 16 * k, 16 * k + 32)), Fn.Identity, scale=1.0 / SC)
-            for e in range(2):
-                o = q(j % 4, e * C, e * C + C)
-                mm(o, A("id7"), cols("xa", s + e * C, s + e * C + C), True, False)
-                mm(o, A("idm"), A("mb"), False, True)
-
-        nv, done = len(via_act), 0
-        front(0)
-        for j in range(nv):
-            while done < len(direct) and done * nv <= j * len(direct):
-                one_direct(direct[done]); done += 1
-            if j + 1 < nv:
-                front(j + 1)
-            while pend:
-                count(*pend.pop(0))
-            w, k = via_act[j]
-            ts(cols("ind%d" % w, k * C, k * C + 2 * C), q(j % 4), BIG32 - 896, Op.add, BIG32, Op.is_equal)
-            pend.append((w, k))
-        while pend:
-            count(*pend.pop(0))
-
-    def claims(t):
-        c0, c1 = q(4, 0, C), q(4, C, 2 * C)
-        ts(A("thr"), c0, -160.0, Op.add, 10.5, Op.max)
-        tt(A("late"), c1, A("thr"), Op.is_gt)
-        tt(A("mx"), c1, A("thr"), Op.max)
-        ts(c0, A("mx"), 10.5, Op.is_le, 4096.0, Op.mult)
-        tt(c1, c0, A("ti"), Op.add)
-        tt(A("p0"), c1, A("late"), Op.add)
-        ts(A("bi"), A("p0"), 31, Op.bitwise_and)
-        ts(A("pw"), A("p0"), 4096 + W - 1, Op.bitwise_and)
+        ts(A("of1"), q(bank, 0, C), 1.0, Op.add)
+        ts(A("bi"), A("ti"), 31, Op.bitwise_and)
         for h in range(2):
-            cp(cols("bb", 128 * h, 128 * h + 128), cols("bi", h, C, 2))
-            ts(cols("aa", 128 * h, 128 * h + 128), cols("pw", h, C, 2), 1.0 / 32, Op.mult, 160 - 15.5 / 32, Op.add)
-        ts(A("ph"), A("pw"), float(W), Op.min)
-        to_list("ph", 5)
+            ts(A("aa", ALL, h, slice(0, 128)), A("th", ALL, slice(h, 16, 2)), 1.0 / 32, Op.mult, 160 - 15.5 / 32, Op.add)
+        n = 1
+        while n < COPIES:
+            ts(A("aa", ALL, ALL, slice(128 * n, 256 * n)), A("aa", ALL, ALL, slice(0, 128 * n)), -float(n), Op.add)
+            n *= 2
+        for a in range(0, 64, n):
+            ts(A("oa", ALL, ALL, slice(128 * a, 128 * (a + n))), A("aa", ALL, ALL, slice(0, 128 * n)), 160.0 + a, Op.is_equal, cols("wc", 0, 1), Op.mult)
 
-    def histogram(t, fill):
-        for h0, h1 in (((0, 1), (1, 2)) if HALVES[t] else ((0, 2),)):
-            for a in range(64):
-                if a % 2 == 0 and a > 0:
-                    b = a // 2
-                    act(A("ob", ALL, slice(h0, h1), slice(128 * b, 128 * b + 128)), cols("bb", 128 * h0, 128 * h1), Fn.Sign, bias=0.5 - b)
-                ts(A("oa", ALL, slice(h0, h1), slice(128 * a, 128 * a + 128)), cols("aa", 128 * h0, 128 * h1), 160.0 + a, Op.is_equal, cols("wc", 0, 1), Op.mult)
-            for h in range(h0, h1):
-                for gq in range(4):
-                    for k in range(16):
-                        o = 16 * gq + k
-                        mm(q(6 + h, 128 * gq, 128 * gq + 66), A("oa", ALL, h, slice(o, 8192, 64)), A("ob", ALL, h, slice(o, 33 * 128, 64)), k == 0, k == 15)
-        cp(A("pl%d" % (t % 2)), q(5, 0, C))
-        fill[0]()
-        for h in range(2):
-            act(A("hs%d" % h), A("q%d" % (6 + h), ALL, ALL, slice(2, 66)), Fn.Identity)
-            for b4 in range(2):
-                part = slice(32 * b4, 32 * b4 + 32)
-                tt(cols("r%d" % h, 128 * b4, 128 * b4 + 128), A("q%d" % (6 + h), ALL, ALL, part), A("hs%d" % h, ALL, ALL, part), Op.subtract)
-            if h == 0:
-                fill[1]()
-        for which in range(2):
-            for g2 in range(2):
-                for b4 in range(2):
-                    o = A("q5", slice(64 * g2, 64 * g2 + 64), slice(C + 128 * which + b4, C + 128 * which + 128, 2))
-                    for h in range(which, 2):
-                        mm(o, cols("r%d" % h, 128 * b4 + g2, 128 * b4 + 128, 2), cols("idh", g2, 128, 2), h == which, h == 1)
-
-    def flags(t):
-        ts(A("uq"), q(5, C, C + 128), 1.0 / 128, Op.mult, 192 - 191.5 / 128, Op.add)
-        ts(A("u%d" % t), A("uq"), 192.0, Op.is_equal)
-
-    def owners(t):
-        ts(A("i1"), q(5, C + 128, 2 * C), 128.0, Op.min, 2.0, Op.mult)
-        ts(A("i2"), q(5, C, C + 128), 256.0, Op.min)
-        tt(A("i3"), A("i1"), A("i2"), Op.add)
-        cp(A("idx"), A("i3"))
-
-    def keys(t):
-        for h in range(2):
-            act(cols("kt%d" % (t % 2), 128 + C * h, C + C * h), cols("kb", 128 * h, 128 * h + 128), Fn.Identity)
-
-    def spread(u, x, with_x, out, banks):
-        def place(i):
-            return q(banks[i // 4 % len(banks)], 128 * (i % 4), 128 * (i % 4) + 128)
-        for r in range(4 + len(banks) - 1):
-            for i in range(4 * r, 4 * r + 4):
-                if i < 16:
-                    if with_x(i):
-                        mm(place(i), A("idb"), cols(x, i, W, 16), True, False)
-                    mm(place(i), cols("sel", 128 * i, 128 * i + 128), A(u), not with_x(i), True)
-            for i in range(4 * (r - len(banks) + 1), 4 * (r - len(banks) + 2)):
-                if i >= 0:
-                    out(i, place(i))
-
-    def diffs(t, a, b):
-        tt(cols("wv", a, b), IND(cols("kt%d" % (t % 2), 0, 513), cols("idx", a // 16, b // 16)), cols("tab%d" % (t % 2), a, b), Op.add)
-
-    def weights(c):
-        o = cols("wv", 512 * c, 512 * c + 512)
-        act(o, o, Fn.Abs, bias=-BIG)
-        act(q(EB[c]), o, Fn.Exp, scale=-1.0 / (8 * SC))
-
-    def terms(t, c):
-        tt(cols("zt", 512 * c, 512 * c + 512), q(EB[c]), cols("g%d" % t, 512 * c, 512 * c + 512), Op.mult)
-
-    def summed_terms(t, n, bank):
-        for j in range(n):
-            k = 16 - n + j
-            o = cols("zg", C * j, C * j + C)
-            act(o, IND(cols("zt", 0, W + 1), cols("pl%d" % (t % 2), 16 * k, 16 * k + 16)), Fn.Identity)
-            mm(q(bank, 0, C), A("idf"), o, j == 0, j == n - 1)
-
-    def gather_terms(t, ks):
-        for k in ks:
-            src = IND(cols("zt", 0, W + 1), cols("pl%d" % (t % 2), 16 * k, 16 * k + 16))
-            o = A("yb" if k % 2 else "ya")
-            if k == 1 or (k == 0 and t == 0):
-                cp(o, src)
+    def hear(t, aside):
+        tab = A("x%d" % t)
+        for j in range(16):
+            w, h, kq = j // 8, j // 4 % 2, j % 4
+            xa, bank, a = cols("xa", 512 * kq, 512 * kq + 512), HB[kq], 2048 * h + 512 * kq
+            act(xa, IND(tab, cols("of%d" % w, a // 16, a // 16 + 32)), Fn.Identity)
+            mm(q(bank), A("id7"), xa, True, False)
+            for i in range(4):
+                mm(q(bank, 128 * i, 128 * i + 128), A("idm"), cols("mb", 128 * h, 128 * h + 128), False, i == 3)
+            first = a
+            if j not in VIA_ACT[t]:
+                ts(cols("ind%d" % w, a, a + 512), q(bank), BIG - 896, Op.add, BIG, Op.not_equal)
             else:
-                tt(o, src, A("yin") if k == 0 else o, Op.add)
+                act(cols("ind%d" % w, a, a + 512), q(bank), Fn.Identity, bias=BIGH - 896)
+                if j % 2 == 0:
+                    continue
+                first = a - 512
+                ts(cols("ind%d" % w, first, a + 512), cols("ind%d" % w, first, a + 512), BIGH, Op.not_equal)
+            for b in range(first, a + 512, 128):
+                k = b // 128
+                mm(A("q7", ALL, slice(0, 2), slice(k, 128, 32)) if w else A("q4", ALL, slice(0, 8), k), cols("ind%d" % w, b, b + 128), A("b4k"))
+            if j == 7:
+                act(A("t0"), q(4, 0, C), Fn.Relu, bias=-5 * 4096.0)
+            if j in aside:
+                aside[j]()
 
-    def close_terms():
-        tt(A("ys"), A("ya"), A("yb"), Op.add)
-        rotate("yin", "ys", 1)
+    def claims():
+        c1 = q(7, 0, C)
+        ts(c1, c1, -5 * 4096.0, Op.add, 1.0, Op.max)
+        tt(A("ee"), c1, A("t0"), Op.min)
+        for h in range(2):
+            tt(A("bb", ALL, h, slice(0, 128)), A("ee", ALL, slice(h, 16, 2)), A("bi", ALL, slice(h, 16, 2)), Op.add)
+        ts(A("bb", ALL, ALL, slice(128, 256)), A("bb", ALL, ALL, slice(0, 128)), -16.0, Op.add)
+        ts(A("bb", ALL, ALL, slice(256, 512)), A("bb", ALL, ALL, slice(0, 256)), -1.0, Op.add)
 
-    def taken(t, on_dve):
-        win = cols("xu", 0, W + 1)
-        order = [k for k in range(0, 16, 2)]
-        for k in order:
-            o, src = cols("xg", k * C, k * C + 2 * C), IND(win, cols("pl%d" % (t % 2), 16 * k, 16 * k + 32))
-            if k in on_dve:
-                cp(o, src)
+    def histogram(t):
+        to_list(["th", "ee"], 5)
+        ts(A("pl%d" % (t % 2)), q(5, 0, C), float(NONE), Op.min)
+        for h in range(2):
+            ts(A("ob", ALL, h, slice(4096, 4096 + 128)), A("bb", ALL, h, slice(0, 128)), 32.0, Op.is_equal, HALF[h], Op.mult)
+            for i in range(8):
+                ts(A("ob", ALL, h, slice(512 * i, 512 * i + 512)), A("bb", ALL, h), 2.0 * i, Op.is_equal, HALF[h], Op.mult)
+            for gq, bank in enumerate((0, 1, 6, 7)):
+                for k in range(16):
+                    mm(q(bank, 0, 66), A("oa", ALL, h, slice(16 * gq + k, 8192, 64)), A("ob", ALL, h, slice(16 * gq + k, 33 * 128, 64)), h + k == 0, h + k == 16)
+                if h:
+                    ts(cols("rr", 64 * gq, 64 * gq + 64), q(bank, 0, 64), 4096.0, Op.min)
+                    ts(A("rw", ALL, gq, slice(0, 2)), q(bank, 64, 66), 4096.0, Op.min)
+
+        def by_column(bank, same, on):
+            for b4 in (1, 0):
+                for g2 in range(2):
+                    o = q(bank, C + b4, C + 128, 2, slice(64 * g2, 64 * g2 + 64))
+                    mm(o, cols("rr", 2 * b4 + g2, C, 4), cols(same, g2, 128, 2), True, b4 == 1)
+                    if b4 == 0:
+                        mm(o, cols("rw", g2, 128, 2), cols(on, g2, 128, 2), False, True)
+
+        if t < VI - 1:
+            by_column(4, "idu", "isu")
+            ts(A("u%d" % t), q(4, C, C + 128), M512, Op.add, M512 + 512, Op.is_equal)
+        by_column(5, "idh", "ish")
+        ts(A("idx"), q(5, C, C + 128), -0.2, Op.add, 700.0, Op.min)
+        for h in range(2):
+            act(cols("kt", C + h, 2 * C, 2), cols("df", 128 * h, 128 * h + 128), Fn.Identity, scale=-1.0 / 32)
+
+    def spread(u, j, bank, x=None, sign="idb"):
+        if x:
+            mm(q(bank), A(sign), cols(x, j, W, 4), True, False)
+        for i in range(4):
+            mm(q(bank, i, 512, 4), cols("sel", 128 * (4 * i + j), 128 * (4 * i + j) + 128), A(u), not x, i == 3 or not x)
+
+    def diffs(t, a, b, aside):
+        src = IND(A("kt"), cols("idx", a // 16, b // 16))
+        if aside:
+            act(cols("wv", a, b), src, Fn.Identity)
+            dma_add(cols("wv", a, b), cols("x%d" % t, a, b))
+        else:
+            tt(cols("wv", a, b), src, cols("x%d" % t, a, b), Op.add)
+
+    def terms(t, a, b, bank):
+        o = cols("wv", a, b)
+        act(o, o, Fn.Abs)
+        act(q(bank, 0, b - a), o, Fn.Exp, scale=-1.0 / 8)
+        tt(cols("zt", a, b), q(bank, 0, b - a), cols("g%d" % t, a, b), Op.mult)
+        if a == 0:
+            act(cols("zt", W, W + 1), cols("zt", 0, 1), Fn.Identity)
+
+    def gather_terms(t, parts):
+        for h, a, b in parts:
+            act(A("zg", ALL, h, slice(128 * a, 128 * b)), IND(A("zt"), cols("pl%d" % (t % 2), 128 * h + 8 * a, 128 * h + 8 * b)), Fn.Identity)
+
+    def halve_terms(t):
+        n = 2048
+        for _ in range(LEVELS[t]):
+            n //= 2
+            dma_add(A("zg", ALL, ALL, slice(0, n)), A("zg", ALL, ALL, slice(n, 2 * n)))
+
+    def home(t, h):
+        return A("back%d" % t if h and t else "idf")
+
+    def sum_terms(t, bank):
+        n = 16 >> LEVELS[t]
+        for h in range(2):
+            for k in range(n):
+                mm(q(bank, 128 * h, 128 * h + 128), home(t, h), A("zg", ALL, h, slice(128 * k, 128 * k + 128)), k == 0, k == n - 1)
+        if t == 0:
+            act(A("yacc"), q(bank, 0, C), Fn.Identity)
+        else:
+            tt(A("yacc"), q(bank, 0, C), A("yacc"), Op.add)
+
+    def taken_columns(t):
+        x = "x%d" % t
+        for j in range(4):
+            spread("u%d" % t, j, HB[j], x if j % 2 else None)
+            if j % 2:
+                act(cols("xu", j, W, 4), q(HB[j]), Fn.Relu, bias=-256.0)
             else:
-                act(o, src, Fn.Identity)
-        n = len(on_dve) // 1
-        seq = sorted(order, key=lambda k: (on_dve.index(k) if k in on_dve else [j for j in order if j not in on_dve].index(k)))
-        for k in seq:
-            for kk in (k, k + 1):
-                for h in range(2):
-                    a = kk * C + 128 * h
-                    mm(q(4, 2 * kk + h, C, 32), cols("xg", a, a + 128), A("b32"))
-            if k != seq[-1]:
-                sums(k, seq)
-        return seq
+                tt(cols("xu", j, W, 4), q(HB[j]), cols(x, j, W, 4), Op.min)
+        cp(cols("xu", W, W + 1), cols("xu", 0, 1))
 
-    def sums(k, seq):
-        for kk in (k, k + 1):
+    def taken(t):
+        mm(q(4), A("idb"), A("cin"), True, False)
+        for h in range(2):
+            mm(q(5 + h, 0, 128), A("idb"), A("off"), True, False)
+        for kq in range(4):
             for h in range(2):
-                a = kk * C + 128 * h
-                mm(q(5 + h, 0, 128), A("r32" if h else "i32"), cols("xg", a, a + 128), kk == seq[0], kk == seq[-1] + 1)
+                a = 2048 * h + 512 * kq
+                o, src = cols("xg", a, a + 512), IND(A("xu"), cols("pl%d" % (t % 2), a // 16, a // 16 + 32))
+                if h == 0:
+                    cp(o, src)
+                else:
+                    act(o, src, Fn.Identity)
+                for k in range(4 * kq, 4 * kq + 4):
+                    a, s = 2048 * h + 128 * k, int(k == 0)
+                    mm(A("q4", ALL, slice(h, 16, 2), slice(2 * k - 1 + s, 2 * k + 2)), cols("xg", a, a + 128), A("b3", ALL, ALL, slice(s, 3)), False, h + k == 16)
+                    mm(q(5 + h, 0, 128), A("r2" if h else "i2"), cols("xg", a, a + 128), False, k == 15)
 
-    def tapes(t, seq):
-        sx = q(4, 0, C)
-        side = q(4, C, 2 * C)
-        act(A("tnb"), sx, Fn.Relu, bias=1.0, scale=-1.0)
-        tt(A("tn"), A("cb"), sx, Op.subtract)
-        tt(side, sx, A("late"), Op.min)
-        tt(cols("lv", 0, C - 2), q(4, 2, C), cols("tn", 0, C - 2), Op.min)
-        sums(seq[-1], seq)
+    def next_table(t):
+        x = "x%d" % t
+        for j in range(4):
+            spread("ul%d" % t, j, (j + 1) % 2, x, "idn")
+            act(cols(x, j, W, 4), q((j + 1) % 2), Fn.Relu, scale=-256.0)
+        act(cols(x, W, W + 1), cols(x, 0, 1), Fn.Identity)
+
+    def profiles(t):
         for h in range(2):
-            mm(q(7, 128 * h, 128 * h + 128), cols("tnb", h, C, 2), A("idb"))
+            act(cols("tnb", 128 * h, 128 * h + 128), A("q4", ALL, slice(h, 16, 2), slice(0, 32, 2)), Fn.Relu, bias=1.0, scale=-1.0)
+        for h in range(2):
+            mm(q(7, 128 * h, 128 * h + 128), cols("tnb", 128 * h, 128 * h + 128), A("idb"))
         act(A("ntp"), q(7, 0, C), Fn.Identity)
         for h in range(2):
             mm(q(7, C + 128 * h, C + 128 * h + 128), A("blr" if h else "blk"), cols("ntp", 128 * h, 128 * h + 128))
-        next_table(t + 1)
-        weights(0)
-        weights(1)
-        tt(A("zz"), side, A("lv"), Op.max)
+        tt(A("d1"), q(7, C, 2 * C), A("dri" if t == 0 else "drf"), Op.mult)
         for h in range(2):
-            o, d = q(4, h, C, 2), cols("zz", h, C, 2)
-            add("dve", lambda o=o, d=d: g.vector.tensor_tensor_scan(o[0], T["seg"][:], d[0], 0.0, Op.mult, Op.add), [o], [d, A("seg")])
-        ts(side, A("zz"), B, Op.is_ge, -16 * B, Op.mult)
-        tt(A("tk"), side, A("ti"), Op.add)
-        tt(A("vv"), sx, A("tk"), Op.add)
+            tt(cols("d2", 128 * h, 128 * h + 128), q(5 + h, 0, 128), cols("d1", 128 * h, 128 * h + 128), Op.add)
+        ts(A("df"), A("d2"), M1, Op.add, -M1, Op.add)
+        centres(6)
+        if t == 0:
+            rotate("drf", "df")
+
+    def tapes(t):
+        sx, lx = q(4, 0, 512, 2), q(4, 1, 512, 2)
+        tt(cols("sl", 0, 512, 2), sx, A("ee"), Op.min)
+        ts(cols("sl", 1, 512, 2), lx, 0.0, Op.is_lt, B, Op.mult)
+        tt(A("tk"), lx, A("ti"), Op.min)
+        profiles(t)
+        o, d, seg = q(0), A("sl"), A("seg")
+        add("dve", lambda: g.vector.tensor_tensor_scan(o[0], seg[0], d[0], 0.0, Op.mult, Op.add), [o], [d, seg], vtime(o, d))
+        vv = A("vv", ALL, ALL, slice(0, 16))
+        tt(vv, q(0, 0, 512, 2), A("tk"), Op.add)
         at = [0]
 
         def moves(src, spans, bank):
             for j, (d, a, b, n) in enumerate(spans):
                 o = cols("cl", at[0], at[0] + 16 * n)
                 at[0] += 16 * n
-                ts(o, A(src, ALL, ALL, slice(2 * a, 2 * a + 2 * n)), d * B, Op.max, (d + 1) * B, Op.min)
-                mm(A(bank, ALL, slice(0, 8), slice(2 * b, 2 * b + 2 * n)), A("idf"), o, j == 0, j == len(spans) - 1)
+                ts(o, A(src, ALL, ALL, slice(a, a + n)), d * B, Op.max, (d + 1) * B, Op.min)
+                mm(A(bank, ALL, slice(0, 16), slice(b, b + n)), A("idf"), o, j == 0, j == len(spans) - 1)
 
-        moves("vv", [(0, 0, 0, 16)] + [(d, 2 * d - 1, d - 1, 17 - 2 * d) for d in range(1, 9)], "q3")
-        tt(A("e2"), A("vv", ALL, ALL, slice(30, 32)), A("nt%d" % t), Op.add)
-        tt(A("d1"), q(7, C, 2 * C), A("drot"), Op.mult)
-        cp(A("er"), IND(A("e2"), A("el")))
-        for h in range(2):
-            tt(cols("d2", 128 * h, 128 * h + 128), q(5 + h, 0, 128), cols("d1", 128 * h, 128 * h + 128), Op.add)
-        weights(2)
-        weights(3)
-        ts(A("di"), A("d2"), 1.0 / 16, Op.mult, -15.0 / 32, Op.add)
-        ts(A("kb"), A("di"), -SC / 32, Op.mult, BIG, Op.add)
-        cp(A("acc"), q(3, 0, C))
-        ts(A("nw"), A("acc", ALL, ALL, slice(0, 16)), W - 1, Op.bitwise_and)
+        moves("vv", [(1, 1, 0, 16)] + [(d, 2 * d - 1, d - 1, 17 - 2 * d) for d in range(2, 9)], "q3")
+        ts(A("c0"), vv, 0.0, Op.max, B, Op.min)
+        tt(A("e2"), A("vv", ALL, ALL, 15), A("nt%d" % t), Op.add)
+        act(A("er"), IND(A("e2"), A("el")), Fn.Identity)
+        tt(A("acc"), q(3, 0, C), A("c0"), Op.add)
+        ts(A("nw"), A("acc", ALL, ALL, slice(0, 8)), W - 1, Op.bitwise_and)
         tt(A("v2"), A("nw"), A("er"), Op.add)
         moves("v2", [(e, 0, 16 - e, e) for e in range(8, 0, -1)], "q2")
-        terms(t, 0)
-        late = A("acc", ALL, ALL, slice(16, 32))
-        tt(late, A("q2", ALL, slice(0, 8), slice(16, 32)), late, Op.add)
-        ts(cols("ti", 0, C, 2), A("acc", ALL, ALL, slice(0, 32, 2)), W - 1, Op.bitwise_and)
-        ts(cols("ti", 33, C, 2), A("acc", ALL, slice(0, 7), slice(1, 32, 2)), W - 1, Op.bitwise_and)
-        ts(cols("ti", 1, 32, 2), A("acc", ALL, 7, slice(1, 32, 2)), W - 1, Op.bitwise_and)
-        cp(A("th"), A("ti"))
-        to_list("th", 4)
-        profile(t + 1)
-        terms(t, 1)
-        time_lists(4)
-        terms(t, 2)
-        terms(t, 3)
-        if t == 0:
-            rotate("drot", "di", 1)
+        late = A("acc", ALL, ALL, slice(8, 16))
+        tt(late, A("q2", ALL, slice(0, 16), slice(8, 16)), late, Op.add)
+        ts(A("ti", ALL, slice(0, 16, 2)), A("acc", ALL, slice(0, 16, 2)), W - 1, Op.bitwise_and)
+        ts(A("ti", ALL, slice(3, 16, 2)), A("acc", ALL, slice(1, 14, 2)), W - 1, Op.bitwise_and)
+        ts(A("ti", ALL, 1), A("acc", ALL, 15), W - 1, Op.bitwise_and)
 
-    def next_table(t):
-        tab = "tab%d" % (t % 2)
-
-        def out(i, ps):
-            act(cols(tab, i, W, 16), ps, Fn.Identity, scale=SC)
-            if i == 0:
-                act(cols(tab, W, W + 1), q(3, 0, 1), Fn.Identity, scale=SC)
-        spread("ul%d" % t, "x%d" % t, lambda i: True, out, [3, 2, 0, 1])
-
-    def early_terms(t):
-        gather_terms(t, range(0, NF))
-        tt(A("yb"), q(0, 0, C), A("yb"), Op.add)
-
-    def later_terms(t):
-        gather_terms(t, range(NF, 16 - NY))
-        close_terms()
-
-    def taken_columns(t):
-        x = "x%d" % t
-
-        def out(i, ps):
-            if i // 4 % 2:
-                act(cols("xu", i, W, 16), ps, Fn.Relu, bias=-256.0)
+    def last_terms(t):
+        for c in range(len(LAST) - 1):
+            diffs(t, LAST[c], LAST[c + 1], False)
+            terms(t, LAST[c], LAST[c + 1], c % 4)
+        gather_terms(t, [(1, 0, 2), (1, 2, 6), (1, 6, 11), (1, 11, 16)])
+        for k in range(16):
+            mm(q(0, 0, 128), home(t, 1), A("zg", ALL, 1, slice(128 * k, 128 * k + 128)), k == 0, k == 15)
+        for k in range(16):
+            src, o = IND(A("zt"), cols("pl%d" % (t % 2), 8 * k, 8 * k + 8)), A("yb" if k % 2 else "ya")
+            if k == 1:
+                cp(o, src)
             else:
-                tt(cols("xu", i, W, 16), ps, cols(x, i, W, 16), Op.min)
-        spread("u%d" % t, x, lambda i: i // 4 % 2 == 1, out, [0, 1, 2, 3])
+                tt(o, src, cols("yacc", 0, 128) if k == 0 else o, Op.add)
+        tt(cols("ys", 0, 128), A("ya"), A("yb"), Op.add)
+        dma("sp", cols("y", 0, 128), cols("ys", 0, 128))
+        tt(cols("ys", 128, C), q(0, 0, 128), cols("yacc", 128, C), Op.add)
+        dma("act", cols("y", 128, C), cols("ys", 128, C))
 
+    centres(1)
+    times(5)
     for t in range(VI):
-        hear(t)
-        if t == 0:
-            act_constants()
-        else:
-            summed_terms(t - 1, NY, 0)
-        keys(t)
-        claims(t)
-        if t == 0:
-            histogram(t, [lambda: None, late_constants])
-        else:
-            histogram(t, [lambda: early_terms(t - 1), lambda: later_terms(t - 1)])
-        if t < VI - 1:
-            flags(t)
-            if t == 0:
-                send(2, 1, A("ul1"), A("u0"))
-                send(3, 2, A("x2"), A("x0"))
-                send(4, 2, A("g2"), A("g0"))
-                owners(t)
-                taken_columns(t)
-            else:
-                tt(A("us"), A("u1"), A("ul1"), Op.add)
-                send(5, 1, A("ul2"), A("us"))
-                owners(t)
-                taken_columns(t)
-            seq = taken(t, ONV)
-            diffs(t, 0, W)
-            tapes(t, seq)
-        else:
-            owners(t)
+        aside = {}
+        if t > 0:
             for c in range(4):
-                diffs(t, 512 * c, 512 * c + 512)
-                weights(c)
-            for c in range(4):
-                terms(t, c)
-            summed_terms(t, NZ, 4)
-            gather_terms(t, range(0, 15 - NZ))
-            o = A("yb" if NZ % 2 else "ya")
-            tt(o, q(4, 0, C), o, Op.add)
-            gather_terms(t, range(15 - NZ, 16 - NZ))
-            tt(A("ys"), A("ya"), A("yb"), Op.add)
-            rotate("y", "ys", -(VI - 1), ("sp", "act", "sp"))
-    emit(ops, queue, T)
+                aside[EXP_AT[c]] = lambda c=c: terms(t - 1, 512 * c, 512 * c + 512, 5 + c % 2)
+        if t == 2:
+            aside[11] = lambda: sum_terms(0, 6)
+        hear(t, aside)
+        if t > 0:
+            gather_terms(t - 1, [(h, a, a + 4) for a in (8, 0, 12, 4) for h in range(2)])
+            halve_terms(t - 1)
+        claims()
+        histogram(t)
+        if t == VI - 1:
+            sum_terms(t - 1, 4)
+            last_terms(t)
+            break
+        if t == 0:
+            i = send(1, 1, A("ul1"), A("u0"))
+            i = send(2, 2, A("x2"), A("x0"), [i])
+            send(3, 1, A("g1"), A("g0"), [i])
+        else:
+            tt(A("us"), A("u1"), A("ul1"), Op.add)
+            i = send(4, 1, A("ul2"), A("us"))
+            send(5, 2, A("g2"), A("g0"), [i])
+        taken_columns(t)
+        taken(t)
+        for a in (0, 1024):
+            diffs(t, a, a + 1024, ASIDE)
+        tapes(t)
+        next_table(t + 1)
+        times(4)
+    if not ORDER:
+        ORDER.extend(arrange(ops))
+    emit([ops[i] for i in ORDER], queue, T)
+
+
+def arrange(ops):
+    seen, last = {}, {}
+    before = []
+    for i, o in enumerate(ops):
+        dep = {j: 0 for j in o["after"]}
+        for mine, write in ((o["r"], False), (o["w"], True)):
+            for (name, p0, p1, m) in mine:
+                if name in SCRATCH and SCRATCH[name][0] == P:
+                    j = last.get(name, i)
+                    if j != i:
+                        dep[j] = max(dep.get(j, 0), ops[j]["wake"] if ops[j]["eng"] != o["eng"] else 0)
+                    last[name] = i
+                keep = []
+                for e in seen.get(name, []):
+                    j, wr, a0, a1, b = e
+                    if j != i and (wr or write) and a0 <= p1 and p0 <= a1 and b & m:
+                        dep[j] = 0 if ops[j]["eng"] == o["eng"] == "pe" else ops[j]["wake"]
+                    if not (write and p0 <= a0 and a1 <= p1 and (b | m) == m):
+                        keep.append(e)
+                seen[name] = keep + [(i, write, p0, p1, m)]
+        before.append(dep)
+    behind = [{} for o in ops]
+    for i, dep in enumerate(before):
+        for j, gap in dep.items():
+            behind[j][i] = gap
+
+    def place(turn, needs, lead):
+        end = [0.0] * len(ops)
+        busy = {e: [] for e in ENG}
+        for i in turn:
+            at, ns = max([end[j] + gap for j, gap in needs[i].items()] + [lead[i]]), ops[i]["ns"]
+            if ops[i]["eng"]:
+                line = busy[ops[i]["eng"]]
+                k = len(line)
+                while k and line[k - 1][1] > at:
+                    k -= 1
+                while k < len(line) and line[k][0] < at + ns:
+                    at = max(at, line[k][1])
+                    k += 1
+                line.insert(k, (at, at + ns))
+            end[i] = at + ns
+        return end
+
+    tail = [o["wake"] if o["sem"] else 0.0 for o in ops]
+    turn, best = list(range(len(ops))), None
+    for _ in range(ROUNDS):
+        end = place(turn, before, [0.0] * len(ops))
+        span = max(e + w for e, w in zip(end, tail))
+        if best is None or span < best[0]:
+            best = (span, sorted(turn, key=lambda i: end[i] - ops[i]["ns"]))
+        end = place(sorted(turn[::-1], key=lambda i: -end[i] - tail[i]), behind, tail)
+        turn = sorted(turn, key=lambda i: -end[i])
+    SPAN.append(best[0])
+    return best[1]
 
 
 def emit(ops, queue, T):

@@ -8,33 +8,35 @@ M1 = 1.5 * 2 ** 23
 M512 = 1.5 * 2 ** 32
 B = 8192.0
 HALF = (8.0, 8 + 3.0 / 128)
-COPIES = 4
 NONE = W + 2
+COPIES = 4
+PIECES = ((0, 32, 7), (32, 48, 0), (48, 64, 1))
 LEVELS = (3, 1)
-VIA_ACT = ((2, 3), (), ())
+VIA_ACT = ((2, 3, 6, 7), (2, 3, 6, 7), (2, 3, 6, 7))
 HB = (2, 3, 0, 1)
-EXP_AT = (1, 3, 5, 7)
+XG_DVE = ((0, 0), (0, 1), (0, 2), (0, 3))
+STEP = 256
 LAST = (0, 256, 768, 1280, 1792, 2048)
-ASIDE = True
 
 S, P = "sbuf", "psum"
 X3 = [128, W + 16]
 H3 = [128, 16, 16]
 SCRATCH = {
     "x0": (S, X3, "bfloat16"), "x1": (S, X3, "bfloat16"), "x2": (S, X3, "bfloat16"),
-    "g0": (S, [128, W], "bfloat16"), "g1": (S, [128, W], "bfloat16"), "g2": (S, [128, W], "bfloat16"),
+    "g0": (S, [128, W], "bfloat16"), "g2": (S, [128, W], "bfloat16"), "lg0": (S, [128, W], "float32"), "lg1": (S, [128, W], "float32"),
     "xu": (S, X3, "bfloat16"), "zt": (S, [128, W + 8], "float32"), "wv": (S, [128, W], "float32"),
     "xg": (S, [128, 4096], "bfloat16"), "xa": (S, [128, 2048], "bfloat16"), "zg": (S, [128, 2, 2048], "float32"),
     "ind0": (S, [128, 4096], "bfloat16"), "ind1": (S, [128, 4096], "bfloat16"),
-    "oa": (S, [128, 2, 8192], "float16"), "ob": (S, [128, 2, 33 * 128], "float16"),
+    "oa": (S, [128, 2, 8192], "float16"), "ob0": (S, [128, 66, 64], "float16"), "ob1": (S, [128, 66, 64], "float16"),
     "ivi": (S, [128, C], "int32"), "ivh": (S, [128, C], "float16"), "taui": (S, [128, C], "int32"), "tauh": (S, [128, C], "float16"),
     "di": (S, [128, C], "int32"), "df": (S, [128, C], "float32"), "dri": (S, [128, C], "int32"), "drf": (S, [128, C], "float32"),
     "kt": (S, [128, 704], "float32"), "lo": (S, [128, C], "float32"), "mb": (S, [128, C], "bfloat16"),
     "tu": (S, [128, C], "int32"), "ti": (S, H3, "int32"), "th": (S, H3, "float16"),
     "of0": (S, [128, C], "uint16"), "of1": (S, [128, C], "uint16"), "pl0": (S, [128, C], "uint16"), "pl1": (S, [128, C], "uint16"),
-    "t0": (S, [128, C], "float32"), "ee": (S, H3, "bfloat16"),
-    "bi": (S, H3, "int32"), "aa": (S, [128, 2, 1024], "bfloat16"), "bb": (S, [128, 2, 512], "bfloat16"),
-    "rr": (S, [128, C], "float16"), "rw": (S, [128, 4, 32], "float16"),
+    "t0": (S, H3, "float32"), "ee": (S, H3, "bfloat16"), "bi": (S, H3, "int32"),
+    "aa": (S, [128, 2, 1024], "bfloat16"), "bb0": (S, [128, 8, 64], "bfloat16"), "bb1": (S, [128, 8, 64], "bfloat16"),
+    "rr0": (S, [128, C], "float16"), "rw0": (S, [128, 4, 32], "float16"), "rr1": (S, [128, C], "float16"), "rw1": (S, [128, 4, 32], "float16"),
+    "ef0": (S, [128, C], "float32"), "ev": (S, [128, C], "float32"), "ef1": (S, [128, C], "float32"), "zero": (S, [128, C], "bfloat16"),
     "u0": (S, [128, 128], "bfloat16"), "u1": (S, [128, 128], "bfloat16"), "us": (S, [128, 128], "bfloat16"),
     "ul1": (S, [128, 128], "bfloat16"), "ul2": (S, [128, 128], "bfloat16"), "idx": (S, [128, 128], "uint16"),
     "tnb": (S, [128, C], "bfloat16"), "sl": (S, [128, 512], "float32"), "seg": (S, [128, 512], "float32"), "tk": (S, [128, C], "float32"),
@@ -46,24 +48,24 @@ SCRATCH = {
     "one": (S, [128, 128], "float32"), "tr1": (S, [128, 128], "float32"), "tri": (S, [128, 128], "float32"), "blf": (S, [128, 128], "float32"),
     "e8": (S, [128, 128], "float32"), "trh": (S, [128, 128], "float16"), "e8h": (S, [128, 128], "float16"),
     "idf": (S, [128, 128], "float32"), "idb": (S, [128, 128], "bfloat16"), "id7": (S, [128, 128], "bfloat16"), "idm": (S, [128, 128], "bfloat16"),
-    "idh": (S, [128, 128], "float16"), "ish": (S, [128, 128], "float16"), "i2": (S, [128, 128], "bfloat16"), "r2": (S, [128, 128], "bfloat16"),
+    "idh": (S, [128, 128], "float16"), "ish": (S, [128, 128], "float16"), "idu": (S, [128, 128], "float16"), "isu": (S, [128, 128], "float16"),
+    "i2": (S, [128, 128], "bfloat16"), "r2": (S, [128, 128], "bfloat16"),
     "back1": (S, [128, 128], "float32"), "back2": (S, [128, 128], "float32"), "idn": (S, [128, 128], "bfloat16"),
     "blk": (S, [128, 128], "bfloat16"), "blr": (S, [128, 128], "bfloat16"), "b4k": (S, [128, 8], "bfloat16"), "b3": (S, [128, 8, 3], "bfloat16"),
     "s3": (S, [128, 8, 48], "float16"), "c256": (S, [128, W], "bfloat16"), "sel": (S, [128, W], "bfloat16"),
-    "cin": (S, [128, 512], "bfloat16"), "off": (S, [128, 128], "bfloat16"),
-    "wc": (S, [128, 2], "bfloat16"), "idu": (S, [128, 128], "float16"), "isu": (S, [128, 128], "float16"),
+    "cin": (S, [128, 512], "bfloat16"), "off": (S, [128, 128], "bfloat16"), "wc": (S, [128, 2], "bfloat16"),
     "k3": (S, [128, 8], "int32"), "k4": (S, [128, 8], "int32"), "el": (S, [128, 8], "uint16"),
 }
 for _b in range(8):
     SCRATCH["q%d" % _b] = (P, [128, 16, 32] if _b == 4 else [128, 4, 128] if _b in (6, 7) else [128, 512] if _b < 2 else [128, 32, 16], "float32")
 SHAPES = {"xs": [128, W], "gn": [128, W], "tau": [8, C], "iv": [128, C], "pf": [128, C], "y": [128, C]}
 ENG = ("pe", "act", "dve", "gp", "sp")
-SEMAPHORES = ["pe", "act", "dve", "gp"] + ["d%d" % i for i in range(30)] + ["l%d" % i for i in range(6)] + ["a%d" % i for i in range(6)]
+SEMAPHORES = ["pe", "act", "dve", "gp"] + ["d%d" % i for i in range(40)] + ["l%d" % i for i in range(6)] + ["a%d" % i for i in range(6)]
 ALL = slice(None)
 MASKS = {}
 ORDER = []
 CYC, PCYC, GATHER, VCALL, SCALL, WAKE, LOCAL, REMOTE, LRATE, RRATE = 0.83, 0.45, 1.4, 15, 65, 130, 2500, 4000, 150, 40
-ROUNDS = 6
+ROUNDS, PATIENCE = 3, 30
 SPAN = []
 
 
@@ -112,22 +114,21 @@ def build(g, core, T, topo, rank):
 
     def ts(out, in0, s1, op0, s2=None, op1=None):
         if op1 is None:
-            add("dve", lambda: g.vector.tensor_scalar(out[0], in0[0], v(s1), None, op0), [out], [in0, s1], vtime(out, in0))
-        else:
-            add("dve", lambda: g.vector.tensor_scalar(out[0], in0[0], v(s1), v(s2), op0, op1), [out], [in0, s1, s2], vtime(out, in0))
+            return add("dve", lambda: g.vector.tensor_scalar(out[0], in0[0], v(s1), None, op0), [out], [in0, s1], vtime(out, in0))
+        return add("dve", lambda: g.vector.tensor_scalar(out[0], in0[0], v(s1), v(s2), op0, op1), [out], [in0, s1, s2], vtime(out, in0))
 
     def tt(out, a, b, op):
-        add("dve", lambda: g.vector.tensor_tensor(out[0], a[0], b[0], op), [out], [a, b], vtime(out, a, a[4] == b[4] == S))
+        return add("dve", lambda: g.vector.tensor_tensor(out[0], a[0], b[0], op), [out], [a, b], vtime(out, a, a[4] == b[4] == S))
 
     def cp(out, a):
-        add("dve", lambda: g.vector.tensor_copy(out[0], a[0]), [out], [a], vtime(out, a))
+        return add("dve", lambda: g.vector.tensor_copy(out[0], a[0]), [out], [a], vtime(out, a))
 
     def ms(out, c):
         add("dve", lambda: g.vector.memset(out[0], c), [out], [], vtime(out, out))
 
-    def act(out, a, f, bias=0.0, scale=1.0):
-        add("act", lambda: g.scalar.activation(out[0], a[0], f, bias=float(bias), scale=float(scale)), [out], [a],
-            SCALL + CYC * out[2] * (GATHER if a[4] == "gather" else 1))
+    def act(out, a, f, bias=0.0, scale=1.0, load=0, after=()):
+        return add("act", lambda: g.scalar.activation(out[0], a[0], f, bias=float(bias), scale=float(scale)), [out], [a],
+                   load + SCALL + CYC * out[2] * (GATHER if a[4] == "gather" else 1), after=after)
 
     def mm(out, l, r, start=True, stop=True):
         add("pe", lambda: g.tensor.matmul(out[0], l[0], r[0], start, stop), [out], [l, r], PCYC * max(min(64, l[2]), r[2]) * (4 if l[3] == 4 else 1))
@@ -148,17 +149,19 @@ def build(g, core, T, topo, rank):
 
     def dma_add(out, a):
         nd[0] += 1
-        add("gp", lambda: g.dma_start(out[0], a[0], accum_op=Op.add), [out], [a, out], 100, sem="d%d" % (nd[0] - 1), n=16, wake=LOCAL + 128 * out[2] * out[3] / LRATE)
+        return add("gp", lambda: g.dma_start(out[0], a[0], accum_op=Op.add), [out], [a, out], 100, sem="d%d" % (nd[0] - 1), n=16,
+                   wake=LOCAL + 128 * out[2] * out[3] / LRATE)
 
     def send(k, back, dst, src, after=()):
         to = T.cores[(rank - back) % N]
         rid, pid = topo.addr(to)[:2]
-        mask = topo.mask(core, to)
-        n_out = len(topo.engines(core, to))
-        n_in = len(topo.engines(T.cores[(rank + back) % N], core))
+        share = lambda es: es[len(es) // 2:] if src[2] < W else es[:len(es) // 2]
+        mine = share(topo.engines(core, to))
+        mask = sum(1 << e for e in mine)
+        n_in = len(share(topo.engines(T.cores[(rank + back) % N], core)))
         ns = REMOTE + 128 * src[2] * src[3] / RRATE
         i = add("gp", lambda: g.remote_dma(dst[0], src[0], T.sem["a%d" % k], T.sem["l%d" % k], pid, rid, mask), [], [src], 2000 if k == 0 else 300,
-                sem="l%d" % k, n=n_out, extra="remote", wake=ns, after=after)
+                sem="l%d" % k, n=len(mine), extra="remote", wake=ns, after=after)
         add(None, None, [dst], [], ns, sem="a%d" % k, n=n_in, after=[i])
         return i
 
@@ -170,25 +173,21 @@ def build(g, core, T, topo, rank):
     dma("act", cols("x0", W, W + 16), cols("xs", 0, 16))
     dma("sp", A("g0"), A("gn"))
 
-    def rotate(dst, src):
+    def rotate(dst, src, s=16):
         dma("sp", cols(dst, 0, 128), cols(src, 0, 128))
-        dma("sp", A(dst, slice(16, 128), slice(128, C)), A(src, slice(0, 112), slice(128, C)))
-        dma("sp", A(dst, slice(0, 16), slice(128, C)), A(src, slice(112, 128), slice(128, C)))
+        dma("sp", A(dst, slice(s, 128), slice(128, C)), A(src, slice(0, 128 - s), slice(128, C)))
+        dma("sp", A(dst, slice(0, s), slice(128, C)), A(src, slice(128 - s, 128), slice(128, C)))
 
     def shifted(dst, src, s, scale):
         act(cols(dst, s, 128), cols(src, 0, 128 - s), Fn.Identity, scale=scale)
         act(cols(dst, 0, s), cols(src, 128 - s, 128), Fn.Identity, scale=scale)
 
     rotate("dri", "pf")
-    ms(A("one"), 1.0)
-    ms(A("s3"), 0.0)
-    ms(A("c256"), 256.0)
-    ms(A("kt"), 1e9)
-    ms(A("rw", ALL, ALL, slice(2, 32)), 0.0)
+    for name, value in (("one", 1.0), ("s3", 0.0), ("c256", 256.0), ("kt", 1e9), ("rw0", 0.0), ("rw1", 0.0), ("zero", 0.0), ("seg", 1.0)):
+        ms(A(name), value)
+    ms(cols("seg", 0, 512, 32), 0.0)
     ms(cols("xu", W, W + 16), 0.0)
     ms(cols("zt", W, W + 8), 0.0)
-    ms(A("seg"), 1.0)
-    ms(cols("seg", 0, 512, 32), 0.0)
     ms(A("vv", ALL, ALL, slice(16, 17)), 0.0)
     sel(A("tr1"), A("one"), [[-16, 8], [0, 16]], Op.is_ge, 0, 1)
     sel(A("tri"), A("tr1"), [[1, 128]], Op.is_ge, 0, -1)
@@ -238,17 +237,15 @@ def build(g, core, T, topo, rank):
     act(cols("nt1", 1, 2), cols("nt0", 15, 16), Fn.Identity)
     cp(A("tu"), q(5, C, 2 * C))
     ts(A("ti"), A("tu"), W - 1, Op.bitwise_and)
-    send(0, 1, A("x1"), A("x0"))
+    send(1, 2, A("x2"), A("x0"), [send(0, 1, A("x1"), A("x0"))])
 
-    def to_list(srcs, bank):
+    def to_list(src, bank, alone=True, last=True):
         for m in range(8):
             for gp in range(4):
                 for e in range(2):
-                    for src in srcs:
-                        a = 64 * gp + 32 * e
-                        mm(q(bank, m, C, 8, slice(32 * gp, 32 * gp + 32)), A("s3", ALL, m, slice(16 - 16 * e, 48 - 16 * e)),
-                           A(src, ALL, slice(a // 16, a // 16 + 2)),
-                           e == 0 and src == srcs[0], e == 1 and src == srcs[-1])
+                    a = 4 * gp + 2 * e
+                    mm(q(bank, m, C, 8, slice(32 * gp, 32 * gp + 32)), A("s3", ALL, m, slice(16 - 16 * e, 48 - 16 * e)), A(src, ALL, slice(a, a + 2)),
+                       alone and e == 0, e == 1 if alone else last and (m, e) == (7, 1))
 
     def centres(bank):
         act(q(bank, C, 2 * C), A("df"), Fn.Identity, bias=M32, scale=1 + 2.0 ** -15)
@@ -257,7 +254,7 @@ def build(g, core, T, topo, rank):
 
     def times(bank):
         cp(A("th"), A("ti"))
-        to_list(["th"], bank)
+        to_list("th", bank)
         cp(A("of0"), q(bank, 0, C))
         ts(A("of1"), q(bank, 0, C), 1.0, Op.add)
         ts(A("bi"), A("ti"), 31, Op.bitwise_and)
@@ -267,13 +264,14 @@ def build(g, core, T, topo, rank):
         while n < COPIES:
             ts(A("aa", ALL, ALL, slice(128 * n, 256 * n)), A("aa", ALL, ALL, slice(0, 128 * n)), -float(n), Op.add)
             n *= 2
-        for a in range(0, 64, n):
-            ts(A("oa", ALL, ALL, slice(128 * a, 128 * (a + n))), A("aa", ALL, ALL, slice(0, 128 * n)), 160.0 + a, Op.is_equal, cols("wc", 0, 1), Op.mult)
+        for h in range(2):
+            for a in range(0, 64, n):
+                ts(A("oa", ALL, h, slice(128 * a, 128 * (a + n))), A("aa", ALL, h, slice(0, 128 * n)), 160.0 + a, Op.is_equal, cols("wc", 0, 1), Op.mult)
 
-    def hear(t, aside):
+    def hear(t, h):
         tab = A("x%d" % t)
-        for j in range(16):
-            w, h, kq = j // 8, j // 4 % 2, j % 4
+        for j in range(8 * h, 8 * h + 8):
+            w, kq = j // 4 % 2, j % 4
             xa, bank, a = cols("xa", 512 * kq, 512 * kq + 512), HB[kq], 2048 * h + 512 * kq
             act(xa, IND(tab, cols("of%d" % w, a // 16, a // 16 + 32)), Fn.Identity)
             mm(q(bank), A("id7"), xa, True, False)
@@ -289,51 +287,47 @@ def build(g, core, T, topo, rank):
                 first = a - 512
                 ts(cols("ind%d" % w, first, a + 512), cols("ind%d" % w, first, a + 512), BIGH, Op.not_equal)
             for b in range(first, a + 512, 128):
-                k = b // 128
-                mm(A("q7", ALL, slice(0, 2), slice(k, 128, 32)) if w else A("q4", ALL, slice(0, 8), k), cols("ind%d" % w, b, b + 128), A("b4k"))
-            if j == 7:
-                act(A("t0"), q(4, 0, C), Fn.Relu, bias=-5 * 4096.0)
-            if j in aside:
-                aside[j]()
+                mm(A("q4", ALL, slice(8 * w, 8 * w + 8), b // 128), cols("ind%d" % w, b, b + 128), A("b4k"))
+            if j % 8 == 3:
+                act(A("t0", ALL, slice(h, 16, 2)), A("q4", ALL, slice(0, 8), slice(16 * h, 16 * h + 16)), Fn.Relu, bias=-5 * 4096.0)
 
-    def claims():
-        c1 = q(7, 0, C)
+    def claims(h):
+        c1, rows, bb = A("q4", ALL, slice(8, 16), slice(16 * h, 16 * h + 16)), slice(h, 16, 2), "bb%d" % h
         ts(c1, c1, -5 * 4096.0, Op.add, 1.0, Op.max)
-        tt(A("ee"), c1, A("t0"), Op.min)
-        for h in range(2):
-            tt(A("bb", ALL, h, slice(0, 128)), A("ee", ALL, slice(h, 16, 2)), A("bi", ALL, slice(h, 16, 2)), Op.add)
-        ts(A("bb", ALL, ALL, slice(128, 256)), A("bb", ALL, ALL, slice(0, 128)), -16.0, Op.add)
-        ts(A("bb", ALL, ALL, slice(256, 512)), A("bb", ALL, ALL, slice(0, 256)), -1.0, Op.add)
+        tt(A("ee", ALL, rows), c1, A("t0", ALL, rows), Op.min)
+        tt(A(bb, ALL, slice(0, 2)), A("ee", ALL, rows), A("bi", ALL, rows), Op.add)
+        ts(A(bb, ALL, slice(2, 4)), A(bb, ALL, slice(0, 2)), -16.0, Op.add)
+        ts(A(bb, ALL, slice(4, 8)), A(bb, ALL, slice(0, 4)), -1.0, Op.add)
 
-    def histogram(t):
-        to_list(["th", "ee"], 5)
-        ts(A("pl%d" % (t % 2)), q(5, 0, C), float(NONE), Op.min)
-        for h in range(2):
-            ts(A("ob", ALL, h, slice(4096, 4096 + 128)), A("bb", ALL, h, slice(0, 128)), 32.0, Op.is_equal, HALF[h], Op.mult)
+    def histogram(h):
+        ob, bb = "ob%d" % h, "bb%d" % h
+        ts(A(ob, ALL, slice(64, 66)), A(bb, ALL, slice(0, 2)), 32.0, Op.is_equal, HALF[h], Op.mult)
+        for a, b, bank in (PIECES if h else ((0, 64, 6),)):
             for i in range(8):
-                ts(A("ob", ALL, h, slice(512 * i, 512 * i + 512)), A("bb", ALL, h), 2.0 * i, Op.is_equal, HALF[h], Op.mult)
-            for gq, bank in enumerate((0, 1, 6, 7)):
-                for k in range(16):
-                    mm(q(bank, 0, 66), A("oa", ALL, h, slice(16 * gq + k, 8192, 64)), A("ob", ALL, h, slice(16 * gq + k, 33 * 128, 64)), h + k == 0, h + k == 16)
-                if h:
-                    ts(cols("rr", 64 * gq, 64 * gq + 64), q(bank, 0, 64), 4096.0, Op.min)
-                    ts(A("rw", ALL, gq, slice(0, 2)), q(bank, 64, 66), 4096.0, Op.min)
+                ts(A(ob, ALL, slice(8 * i, 8 * i + 8), slice(a, b)), A(bb, ALL, ALL, slice(a, b)), 2.0 * i, Op.is_equal, HALF[h], Op.mult)
+            for o in range(a, b):
+                at = 128 * ((o - a) // 16)
+                mm(q(bank, at, at + 66), A("oa", ALL, h, slice(o, 8192, 64)), A(ob, ALL, ALL, o), o % 16 == 0, o % 16 == 15)
+            n = (b - a) // 16
+            part = lambda c, d: q(bank, c, d) if n == 1 else A("q%d" % bank, ALL, slice(0, n), slice(c, d))
+            ts(cols("rr%d" % h, 4 * a, 4 * b), part(0, 64), 4096.0, Op.min)
+            ts(A("rw%d" % h, ALL, slice(a // 16, b // 16), slice(0, 2)), part(64, 66), 4096.0, Op.min)
 
-        def by_column(bank, same, on):
-            for b4 in (1, 0):
-                for g2 in range(2):
-                    o = q(bank, C + b4, C + 128, 2, slice(64 * g2, 64 * g2 + 64))
-                    mm(o, cols("rr", 2 * b4 + g2, C, 4), cols(same, g2, 128, 2), True, b4 == 1)
-                    if b4 == 0:
-                        mm(o, cols("rw", g2, 128, 2), cols(on, g2, 128, 2), False, True)
-
-        if t < VI - 1:
-            by_column(4, "idu", "isu")
-            ts(A("u%d" % t), q(4, C, C + 128), M512, Op.add, M512 + 512, Op.is_equal)
-        by_column(5, "idh", "ish")
-        ts(A("idx"), q(5, C, C + 128), -0.2, Op.add, 700.0, Op.min)
+    def owners(t):
+        mm(q(4, 0, C), A("idb"), A("zero"), True, False)
         for h in range(2):
-            act(cols("kt", C + h, 2 * C, 2), cols("df", 128 * h, 128 * h + 128), Fn.Identity, scale=-1.0 / 32)
+            for at, same, on in [(0, "idu", "isu"), (128, "idh", "ish")][t == VI - 1:]:
+                for b4 in (1, 0):
+                    for g2 in range(2):
+                        o = q(4, at + b4, at + 128, 2, slice(64 * g2, 64 * g2 + 64))
+                        mm(o, cols("rr%d" % h, 2 * b4 + g2, C, 4), cols(same, g2, 128, 2), False, False)
+                        if b4 == 0:
+                            mm(o, cols("rw%d" % h, g2, 128, 2), cols(on, g2, 128, 2), False, (h, at) == (1, 128))
+        if t < VI - 1:
+            ts(A("u%d" % t), q(4, 0, 128), M512, Op.add, M512 + 512, Op.is_equal)
+        ts(A("idx"), q(4, 128, C), -0.2, Op.add, 700.0, Op.min)
+        for h in range(2):
+            act(cols("kt", C + h, 2 * C, 2), cols("df", 128 * h, 128 * h + 128), Fn.Identity, scale=1.0 / 32)
 
     def spread(u, j, bank, x=None, sign="idb"):
         if x:
@@ -341,29 +335,38 @@ def build(g, core, T, topo, rank):
         for i in range(4):
             mm(q(bank, i, 512, 4), cols("sel", 128 * (4 * i + j), 128 * (4 * i + j) + 128), A(u), not x, i == 3 or not x)
 
-    def diffs(t, a, b, aside):
-        src = IND(A("kt"), cols("idx", a // 16, b // 16))
-        if aside:
-            act(cols("wv", a, b), src, Fn.Identity)
-            dma_add(cols("wv", a, b), cols("x%d" % t, a, b))
-        else:
-            tt(cols("wv", a, b), src, cols("x%d" % t, a, b), Op.add)
+    def logs():
+        parts = [(a, a + 512) for a in range(0, W, 512)]
+        for a, b in parts:
+            i = act(cols("lg0", a, b), cols("g0", a, b), Fn.Ln, load=1300 * (a == 0))
+        act(A("ef0"), A("df"), Fn.Exp, scale=1.0 / 256, load=1500, after=range(i - 3, i + 1))
+        for a, b in parts:
+            act(cols("lg0", a, b), cols("lg0", a, b), Fn.Identity, scale=-4.0)
+            act(cols("xa", a, b), cols("x0", a, b), Fn.Identity, scale=-0.5)
+        dma_add(A("lg0"), A("xa"))
 
-    def terms(t, a, b, bank):
-        o = cols("wv", a, b)
-        act(o, o, Fn.Abs)
-        act(q(bank, 0, b - a), o, Fn.Exp, scale=-1.0 / 8)
-        tt(cols("zt", a, b), q(bank, 0, b - a), cols("g%d" % t, a, b), Op.mult)
-        if a == 0:
+    def terms(t, a, b):
+        tt(cols("wv", a, b), IND(A("kt"), cols("idx", a // 16, b // 16)), cols("x%d" % t, a, b), Op.max)
+        if b % 1024 == 0:
+            i = dma_add(cols("wv", b - 1024, b), cols("lg%d" % t, b - 1024, b))
+            if (t, b) == (0, W):
+                send(3, 1, A("lg1"), A("lg0"), [i])
+            for c in range(b - 1024, b, 512):
+                act(cols("zt", c, c + 512), cols("wv", c, c + 512), Fn.Exp, scale=-0.25)
+        if b == 1024:
             act(cols("zt", W, W + 1), cols("zt", 0, 1), Fn.Identity)
 
-    def gather_terms(t, parts):
+    def gather_terms(t, parts, to=None):
         for h, a, b in parts:
-            act(A("zg", ALL, h, slice(128 * a, 128 * b)), IND(A("zt"), cols("pl%d" % (t % 2), 128 * h + 8 * a, 128 * h + 8 * b)), Fn.Identity)
+            act(A("zg", ALL, h if to is None else to, slice(128 * a, 128 * b)), IND(A("zt"), cols("pl%d" % (t % 2), 128 * h + 8 * a, 128 * h + 8 * b)), Fn.Identity)
 
     def halve_terms(t):
-        n = 2048
-        for _ in range(LEVELS[t]):
+        for h in range(2):
+            for a in (0, 4):
+                gather_terms(t, [(h, a + 8, a + 12), (h, a, a + 4)])
+                dma_add(A("zg", ALL, h, slice(128 * a, 128 * a + 512)), A("zg", ALL, h, slice(128 * a + 1024, 128 * a + 1536)))
+        n = 1024
+        for _ in range(LEVELS[t] - 1):
             n //= 2
             dma_add(A("zg", ALL, ALL, slice(0, n)), A("zg", ALL, ALL, slice(n, 2 * n)))
 
@@ -376,8 +379,9 @@ def build(g, core, T, topo, rank):
             for k in range(n):
                 mm(q(bank, 128 * h, 128 * h + 128), home(t, h), A("zg", ALL, h, slice(128 * k, 128 * k + 128)), k == 0, k == n - 1)
         if t == 0:
-            act(A("yacc"), q(bank, 0, C), Fn.Identity)
+            tt(A("yacc"), q(bank, 0, C), A("ef0"), Op.mult)
         else:
+            tt(q(bank, 0, C), q(bank, 0, C), A("ef1"), Op.mult)
             tt(A("yacc"), q(bank, 0, C), A("yacc"), Op.add)
 
     def taken_columns(t):
@@ -398,7 +402,7 @@ def build(g, core, T, topo, rank):
             for h in range(2):
                 a = 2048 * h + 512 * kq
                 o, src = cols("xg", a, a + 512), IND(A("xu"), cols("pl%d" % (t % 2), a // 16, a // 16 + 32))
-                if h == 0:
+                if (h, kq) in XG_DVE:
                     cp(o, src)
                 else:
                     act(o, src, Fn.Identity)
@@ -465,11 +469,17 @@ def build(g, core, T, topo, rank):
 
     def last_terms(t):
         for c in range(len(LAST) - 1):
-            diffs(t, LAST[c], LAST[c + 1], False)
-            terms(t, LAST[c], LAST[c + 1], c % 4)
-        gather_terms(t, [(1, 0, 2), (1, 2, 6), (1, 6, 11), (1, 11, 16)])
+            a, b = LAST[c], LAST[c + 1]
+            o = cols("wv", a, b)
+            tt(o, IND(A("kt"), cols("idx", a // 16, b // 16)), cols("x%d" % t, a, b), Op.subtract)
+            act(o, o, Fn.Abs)
+            act(q(c % 4, 0, b - a), o, Fn.Exp, scale=-1.0 / 8)
+            tt(cols("zt", a, b), q(c % 4, 0, b - a), cols("g%d" % t, a, b), Op.mult)
+            if a == 0:
+                act(cols("zt", W, W + 1), cols("zt", 0, 1), Fn.Identity)
+        gather_terms(t, [(1, 0, 1), (1, 1, 4), (1, 4, 10), (1, 10, 16)], 0)
         for k in range(16):
-            mm(q(0, 0, 128), home(t, 1), A("zg", ALL, 1, slice(128 * k, 128 * k + 128)), k == 0, k == 15)
+            mm(q(0, 0, 128), home(t, 1), A("zg", ALL, 0, slice(128 * k, 128 * k + 128)), k == 0, k == 15)
         for k in range(16):
             src, o = IND(A("zt"), cols("pl%d" % (t % 2), 8 * k, 8 * k + 8)), A("yb" if k % 2 else "ya")
             if k == 1:
@@ -484,34 +494,35 @@ def build(g, core, T, topo, rank):
     centres(1)
     times(5)
     for t in range(VI):
-        aside = {}
-        if t > 0:
-            for c in range(4):
-                aside[EXP_AT[c]] = lambda c=c: terms(t - 1, 512 * c, 512 * c + 512, 5 + c % 2)
+        mm(q(5, 0, C), A("idb"), A("zero"), True, False)
+        to_list("th", 5, False, False)
         if t == 2:
-            aside[11] = lambda: sum_terms(0, 6)
-        hear(t, aside)
+            sum_terms(0, 7)
+        for h in range(2):
+            hear(t, h)
+            claims(h)
+            histogram(h)
+        to_list("ee", 5, False)
+        ts(A("pl%d" % (t % 2)), q(5, 0, C), float(NONE), Op.min)
         if t > 0:
-            gather_terms(t - 1, [(h, a, a + 4) for a in (8, 0, 12, 4) for h in range(2)])
             halve_terms(t - 1)
-        claims()
-        histogram(t)
+        owners(t)
         if t == VI - 1:
-            sum_terms(t - 1, 4)
+            sum_terms(t - 1, 5)
             last_terms(t)
             break
         if t == 0:
-            i = send(1, 1, A("ul1"), A("u0"))
-            i = send(2, 2, A("x2"), A("x0"), [i])
-            send(3, 1, A("g1"), A("g0"), [i])
+            logs()
+            send(2, 1, A("ul1"), A("u0"))
         else:
+            act(A("ev"), A("df"), Fn.Exp, scale=1.0 / 256)
+            rotate("ef1", "ev", 112)
             tt(A("us"), A("u1"), A("ul1"), Op.add)
-            i = send(4, 1, A("ul2"), A("us"))
-            send(5, 2, A("g2"), A("g0"), [i])
+            send(5, 2, A("g2"), A("g0"), [send(4, 1, A("ul2"), A("us"))])
         taken_columns(t)
         taken(t)
-        for a in (0, 1024):
-            diffs(t, a, a + 1024, ASIDE)
+        for a in range(0, W, STEP):
+            terms(t, a, a + STEP)
         tapes(t)
         next_table(t + 1)
         times(4)
@@ -546,7 +557,7 @@ def arrange(ops):
         for j, gap in dep.items():
             behind[j][i] = gap
 
-    def place(turn, needs, lead):
+    def fit(turn, needs, lead):
         end = [0.0] * len(ops)
         busy = {e: [] for e in ENG}
         for i in turn:
@@ -563,14 +574,37 @@ def arrange(ops):
             end[i] = at + ns
         return end
 
+    def place(turn, needs, lead):
+        rank = {i: n for n, i in enumerate(turn)}
+        users = behind if needs is before else before
+        left, at, end = [len(d) for d in needs], list(lead), [0.0] * len(ops)
+        ready = {e: [i for i in turn if not left[i] and ops[i]["eng"] == e] for e in ENG + (None,)}
+        free = {e: 0.0 for e in ready}
+        for _ in ops:
+            now, e = min(((max(free[e], min(at[i] for i in ready[e])), e) for e in ready if ready[e]), key=lambda x: x[0])
+            i = min((j for j in ready[e] if at[j] <= now + PATIENCE), key=rank.get)
+            ready[e].remove(i)
+            end[i] = max(now, at[i]) + ops[i]["ns"]
+            free[e] = end[i] if e else 0.0
+            for j, gap in users[i].items():
+                at[j] = max(at[j], end[i] + gap)
+                left[j] -= 1
+                if not left[j]:
+                    ready[ops[j]["eng"]].append(j)
+        return end
+
     tail = [o["wake"] if o["sem"] else 0.0 for o in ops]
-    turn, best = list(range(len(ops))), None
-    for _ in range(ROUNDS):
-        end = place(turn, before, [0.0] * len(ops))
+    chain = [o["ns"] + w for o, w in zip(ops, tail)]
+    for i in range(len(ops) - 1, -1, -1):
+        for j, gap in before[i].items():
+            chain[j] = max(chain[j], ops[j]["ns"] + gap + chain[i])
+    turn, best = sorted(range(len(ops)), key=lambda i: -chain[i]), None
+    for how in (place, fit, fit) * ROUNDS:
+        end = how(turn, before, [0.0] * len(ops))
         span = max(e + w for e, w in zip(end, tail))
         if best is None or span < best[0]:
             best = (span, sorted(turn, key=lambda i: end[i] - ops[i]["ns"]))
-        end = place(sorted(turn[::-1], key=lambda i: -end[i] - tail[i]), behind, tail)
+        end = how(sorted(turn[::-1], key=lambda i: -end[i] - tail[i]), behind, tail)
         turn = sorted(turn, key=lambda i: -end[i])
     SPAN.append(best[0])
     return best[1]

@@ -1,77 +1,107 @@
+from concourse.bass import DstId, RemoteDMATransfer
 from concourse.mybir import AluOpType as Op, ActivationFunctionType as Fn
 
 N, W, C, VI = 8, 2048, 256, 3
-BIG = 1.5 * 2 ** 29
 BIGH = 1.5 * 2 ** 13
-M32 = 1.5 * 2 ** 28
 M1 = 1.5 * 2 ** 23
 M512 = 1.5 * 2 ** 32
+MID = 945.0
 B = 8192.0
 HALF = (8.0, 8 + 3.0 / 128)
 NONE = W + 2
 COPIES = 4
-PIECES = ((0, 32, 7), (32, 48, 0), (48, 64, 1))
-LEVELS = (3, 1)
-VIA_ACT = ((2, 3, 6, 7), (2, 3, 6, 7), (2, 3, 6, 7))
-HB = (2, 3, 0, 1)
-XG_DVE = ((0, 0), (0, 1), (0, 2), (0, 3))
+PIECES = ((0, 32, 1), (32, 48, 3), (48, 64, 4))
+LEVELS = ((2, 2), (1, 1))
+PIECE = 1024
+FUSED = ((), (), ())
+XB = (5, 6, 0, 2)
+XU_DVE = (3,)
+XG_DVE = ((0, 0), (0, 2))
+HOLD = 1
+BY_DMA = 512
+TAIL = 13
 STEP = 256
 LAST = (0, 256, 768, 1280, 1792, 2048)
+TA, TB, TC = (5, 6), (1, 3), (0, 2)
 
 S, P = "sbuf", "psum"
 X3 = [128, W + 16]
 H3 = [128, 16, 16]
 SCRATCH = {
-    "x0": (S, X3, "bfloat16"), "x1": (S, X3, "bfloat16"), "x2": (S, X3, "bfloat16"),
+    "x0": (S, [128, W], "bfloat16"), "x1": (S, [128, W], "bfloat16"), "x2": (S, [128, W], "bfloat16"),
+    "st0": (S, X3, "bfloat16"), "st1": (S, X3, "bfloat16"), "st2": (S, X3, "bfloat16"),
     "g0": (S, [128, W], "bfloat16"), "g2": (S, [128, W], "bfloat16"), "lg0": (S, [128, W], "float32"), "lg1": (S, [128, W], "float32"),
     "xu": (S, X3, "bfloat16"), "zt": (S, [128, W + 8], "float32"), "wv": (S, [128, W], "float32"),
-    "xg": (S, [128, 4096], "bfloat16"), "xa": (S, [128, 2048], "bfloat16"), "zg": (S, [128, 2, 2048], "float32"),
+    "xg": (S, [128, 4096], "bfloat16"), "zg": (S, [128, 2, 2048], "float32"),
     "ind0": (S, [128, 4096], "bfloat16"), "ind1": (S, [128, 4096], "bfloat16"),
     "oa": (S, [128, 2, 8192], "float16"), "ob0": (S, [128, 66, 64], "float16"), "ob1": (S, [128, 66, 64], "float16"),
     "ivi": (S, [128, C], "int32"), "ivh": (S, [128, C], "float16"), "taui": (S, [128, C], "int32"), "tauh": (S, [128, C], "float16"),
-    "di": (S, [128, C], "int32"), "df": (S, [128, C], "float32"), "dri": (S, [128, C], "int32"), "drf": (S, [128, C], "float32"),
-    "kt": (S, [128, 704], "float32"), "lo": (S, [128, C], "float32"), "mb": (S, [128, C], "bfloat16"),
-    "tu": (S, [128, C], "int32"), "ti": (S, H3, "int32"), "th": (S, H3, "float16"),
+    "di": (S, [128, C], "int32"), "df": (S, [128, C], "float32"), "dri": (S, [128, 128], "int32"), "drf": (S, [128, 128], "float32"),
+    "kt": (S, [128, 704], "float32"), "mb": (S, [128, C], "bfloat16"), "hi": (S, [128, C], "float16"), "at": (S, [128, 2, PIECE], "float32"),
+    "tu": (S, [128, C], "int32"), "ti": (S, H3, "int32"), "th": (S, H3, "float16"), "ph": (S, H3, "float16"),
     "of0": (S, [128, C], "uint16"), "of1": (S, [128, C], "uint16"), "pl0": (S, [128, C], "uint16"), "pl1": (S, [128, C], "uint16"),
-    "t0": (S, H3, "float32"), "ee": (S, H3, "bfloat16"), "bi": (S, H3, "int32"),
-    "aa": (S, [128, 2, 1024], "bfloat16"), "bb0": (S, [128, 8, 64], "bfloat16"), "bb1": (S, [128, 8, 64], "bfloat16"),
-    "rr0": (S, [128, C], "float16"), "rw0": (S, [128, 4, 32], "float16"), "rr1": (S, [128, C], "float16"), "rw1": (S, [128, 4, 32], "float16"),
-    "ef0": (S, [128, C], "float32"), "ev": (S, [128, C], "float32"), "ef1": (S, [128, C], "float32"), "zero": (S, [128, C], "bfloat16"),
-    "u0": (S, [128, 128], "bfloat16"), "u1": (S, [128, 128], "bfloat16"), "us": (S, [128, 128], "bfloat16"),
+    "t0": (S, [128, C], "float32"), "ee": (S, H3, "bfloat16"),
+    "aa": (S, [128, 2, 128 * COPIES], "bfloat16"), "bb0": (S, [128, 8, 64], "bfloat16"), "bb1": (S, [128, 8, 64], "bfloat16"),
+    "rr": (S, [128, C], "float16"), "rw": (S, [128, 4, 32], "float16"),
+    "ef0": (S, [128, C], "float32"), "ev": (S, [128, 128], "float32"), "ef1": (S, [128, C], "float32"), "zero": (S, [128, C], "bfloat16"),
+    "u0": (S, [128, 128], "bfloat16"), "u1": (S, [128, 128], "bfloat16"),
     "ul1": (S, [128, 128], "bfloat16"), "ul2": (S, [128, 128], "bfloat16"), "idx": (S, [128, 128], "uint16"),
-    "tnb": (S, [128, C], "bfloat16"), "sl": (S, [128, 512], "float32"), "seg": (S, [128, 512], "float32"), "tk": (S, [128, C], "float32"),
-    "vv": (S, [128, 16, 17], "float32"), "acc": (S, H3, "int32"), "cl": (S, [128, 2048], "float32"), "c0": (S, [128, C], "float32"),
-    "e2": (S, [128, 16], "float32"), "er": (S, [128, 128], "float32"), "nw": (S, [128, 128], "int32"), "v2": (S, [128, 16, 8], "float32"),
+    "tnb": (S, [128, C], "bfloat16"), "sl": (S, [128, 2, C], "float32"), "seg": (S, [128, C], "float32"), "sc": (S, [128, 2, C], "float32"),
+    "vv": (S, [128, 16, 17], "float32"), "acc": (S, H3, "int32"), "cl": (S, [128, 2, 808], "float32"), "c0": (S, [128, C], "float32"),
+    "e2": (S, [128, 16], "float32"), "nw": (S, [128, 128], "int32"), "er": (S, [128, 128], "float32"), "v2": (S, [128, 16, 8], "float32"),
     "nt0": (S, [128, 16], "float32"), "nt1": (S, [128, 16], "float32"),
     "ntp": (S, [128, C], "bfloat16"), "d1": (S, [128, C], "float32"), "d2": (S, [128, C], "float32"),
     "ya": (S, [128, 128], "float32"), "yb": (S, [128, 128], "float32"), "ys": (S, [128, C], "float32"), "yacc": (S, [128, C], "float32"),
     "one": (S, [128, 128], "float32"), "tr1": (S, [128, 128], "float32"), "tri": (S, [128, 128], "float32"), "blf": (S, [128, 128], "float32"),
     "e8": (S, [128, 128], "float32"), "trh": (S, [128, 128], "float16"), "e8h": (S, [128, 128], "float16"),
-    "idf": (S, [128, 128], "float32"), "idb": (S, [128, 128], "bfloat16"), "id7": (S, [128, 128], "bfloat16"), "idm": (S, [128, 128], "bfloat16"),
+    "idf": (S, [128, 128], "float32"), "idb": (S, [128, 128], "bfloat16"), "i32": (S, [128, 128], "bfloat16"), "h32": (S, [128, 128], "float16"),
+    "n32": (S, [128, 128], "bfloat16"), "i20": (S, [128, 128], "bfloat16"), "i16": (S, [128, 128], "float16"),
     "idh": (S, [128, 128], "float16"), "ish": (S, [128, 128], "float16"), "idu": (S, [128, 128], "float16"), "isu": (S, [128, 128], "float16"),
     "i2": (S, [128, 128], "bfloat16"), "r2": (S, [128, 128], "bfloat16"),
     "back1": (S, [128, 128], "float32"), "back2": (S, [128, 128], "float32"), "idn": (S, [128, 128], "bfloat16"),
     "blk": (S, [128, 128], "bfloat16"), "blr": (S, [128, 128], "bfloat16"), "b4k": (S, [128, 8], "bfloat16"), "b3": (S, [128, 8, 3], "bfloat16"),
-    "s3": (S, [128, 8, 48], "float16"), "c256": (S, [128, W], "bfloat16"), "sel": (S, [128, W], "bfloat16"),
-    "cin": (S, [128, 512], "bfloat16"), "off": (S, [128, 128], "bfloat16"), "wc": (S, [128, 2], "bfloat16"),
+    "s3": (S, [128, 8, 48], "float16"), "c256": (S, [128, C], "bfloat16"), "sel": (S, [128, W], "bfloat16"),
+    "cin": (S, [128, 384], "bfloat16"), "wc": (S, [128, 2], "bfloat16"),
     "k3": (S, [128, 8], "int32"), "k4": (S, [128, 8], "int32"), "el": (S, [128, 8], "uint16"),
 }
 for _b in range(8):
-    SCRATCH["q%d" % _b] = (P, [128, 16, 32] if _b == 4 else [128, 4, 128] if _b in (6, 7) else [128, 512] if _b < 2 else [128, 32, 16], "float32")
+    SCRATCH["q%d" % _b] = (P, [128, 16, 32] if _b in TA else [128, 32, 16] if _b in TC else [128, 4, 128], "float32")
 SHAPES = {"xs": [128, W], "gn": [128, W], "tau": [8, C], "iv": [128, C], "pf": [128, C], "y": [128, C]}
-ENG = ("pe", "act", "dve", "gp", "sp")
-SEMAPHORES = ["pe", "act", "dve", "gp"] + ["d%d" % i for i in range(40)] + ["l%d" % i for i in range(6)] + ["a%d" % i for i in range(6)]
+ENG = ("pe", "act", "dve", "gp", "sp", "dm")
+LONG = (("x0", 1, "x1", 0), ("x0", 2, "x2", 0), ("g0", 2, "g2", 1), ("lg0", 1, "lg1", 0))
+SEMAPHORES = (["pe", "act", "dve", "gp"] + ["d%d" % i for i in range(70)] + ["l%d" % i for i in range(6)] + ["a%d" % i for i in range(6)]
+              + ["hx0", "hg0", "hlg0"])
 ALL = slice(None)
 MASKS = {}
 ORDER = []
-CYC, PCYC, GATHER, VCALL, SCALL, WAKE, LOCAL, REMOTE, LRATE, RRATE = 0.83, 0.45, 1.4, 15, 65, 130, 2500, 4000, 150, 40
-ROUNDS, PATIENCE = 3, 30
+CYC, PCYC, GATHER, VCALL, SCALL, WAKE, LOCAL, REMOTE, ISSUE, ROW, LRATE, RRATE = 0.83, 0.45, 1.4, 15, 65, 130, 2200, 3000, 700, 50, 38, 60
+ADDS = 1.5
+ROUNDS, PATIENCE, TRIALS, NOISE, SLOW, MOVES, SLACK = 3, 30, 20, 300, (0.8, 1.15), 8000, 20
 SPAN = []
+
+
+def helpers(topo, cores, rank):
+    core = cores[rank]
+    free = [c for c in topo.cores_of(core) if c not in cores]
+    far = [c for c in free if topo.die(c) != topo.die(core) and topo.may_write(c, cores[(rank - 1) % N])]
+    near = [c for c in free if topo.die(c) == topo.die(core) and topo.may_write(c, cores[(rank - 2) % N])]
+    return [far[0], near[0]]
+
+
+def pass_on(g, core, T, topo, rank, me):
+    mine = [(k, src, dst, T.cores[(rank - back) % N]) for k, (src, back, dst, by) in enumerate(LONG) if by == me]
+    for k, src, dst, to in mine:
+        rid, pid = topo.addr(to)[:2]
+        g.wait_ge(T.sem["h" + src], len(topo.engines(T.cores[rank], core)))
+        g.remote_dma(T[dst][:], T[src][:], T.sem["a%d" % k], T.sem["l%d" % k], pid, rid, topo.mask(core, to))
+    for k, src, dst, to in mine:
+        g.wait_ge(T.sem["l%d" % k], len(topo.engines(core, to)))
 
 
 def build(g, core, T, topo, rank):
     ops = []
     nd = [0]
+    heard, added, copies = [], [], []
     queue = {"pe": g.tensor, "act": g.scalar, "dve": g.vector, "gp": g, "sp": g.sync}
 
     def A(name, *ix):
@@ -93,14 +123,21 @@ def build(g, core, T, topo, rank):
             return A(name, part, a // n, slice(a % n, (b - 1) % n + 1, s))
         return A(name, part, slice(a // n, b // n), slice(a % n, n, s))
 
+    def half(name, h):
+        return cols(name, 128 * h, 128 * h + 128)
+
     def q(b, a=0, e=512, s=1, part=ALL):
         return cols("q%d" % b, a, e, s, part)
+
+    def q3(b, a, e, c, d, s=1):
+        return A("q%d" % b, ALL, slice(a, e), slice(c, d, s))
 
     def IND(win, off):
         return (win[0].indirect(off[0]), win[1] + off[1], 16 * off[2], win[3], "gather")
 
-    def add(eng, call, outs, ins, ns, sem=None, n=0, extra=None, wake=WAKE, after=()):
-        ops.append({"eng": eng, "call": call, "w": [b for o in outs for b in o[1]], "ns": ns, "wake": wake, "after": list(after),
+    def add(eng, call, outs, ins, ns, sem=None, n=0, extra=None, wake=WAKE, after=(), move=0.0):
+        ops.append({"eng": eng, "call": call, "w": [b for o in outs for b in o[1]], "ns": ns, "wake": wake, "after": list(after), "move": move,
+                    "more": sum(CYC * GATHER * i[2] for i in ins if isinstance(i, tuple) and i[4] == "gather"),
                     "r": [b for i in ins if isinstance(i, tuple) for b in i[1]], "sem": sem, "n": n, "inc": False, "extra": extra})
         return len(ops) - 1
 
@@ -130,11 +167,22 @@ def build(g, core, T, topo, rank):
         return add("act", lambda: g.scalar.activation(out[0], a[0], f, bias=float(bias), scale=float(scale)), [out], [a],
                    load + SCALL + CYC * out[2] * (GATHER if a[4] == "gather" else 1), after=after)
 
-    def mm(out, l, r, start=True, stop=True):
+    def mm(out, l, r, start=True, stop=True, joined=False):
         add("pe", lambda: g.tensor.matmul(out[0], l[0], r[0], start, stop), [out], [l, r], PCYC * max(min(64, l[2]), r[2]) * (4 if l[3] == 4 else 1))
+        if joined:
+            b = ops.pop()
+            a = ops[-1]
+            one, two = a["call"], b["call"]
+            a.update(call=lambda: (one(), two())[1], w=merged(a["w"] + b["w"]), r=merged(a["r"] + b["r"]), ns=a["ns"] + b["ns"])
 
-    def sel(out, a, pat, op, base, cm):
-        add("gp", lambda: g.affine_select(out[0], a[0], pat, op, 0.0, base, cm), [out], [a], 170 + 2 * CYC * out[2])
+    def merged(parts):
+        masks = {}
+        for name, p0, p1, m in parts:
+            masks[name, p0, p1] = masks.get((name, p0, p1), 0) | m
+        return [k + (m,) for k, m in masks.items()]
+
+    def sel(out, a, pat, op, base, cm, after=()):
+        return add("gp", lambda: g.affine_select(out[0], a[0], pat, op, 0.0, base, cm), [out], [a], 170 + 2 * CYC * out[2], after=after)
 
     def iota(out, pat, base, cm, small):
         if small:
@@ -142,51 +190,62 @@ def build(g, core, T, topo, rank):
         else:
             add("gp", lambda: g.iota(out[0], pat, base, cm), [out], [], 130 + 2 * CYC * out[2])
 
-    def dma(eng, out, a):
-        nd[0] += 1
-        side = out if out[4] else a
-        add(eng, lambda: queue[eng].dma_start(out[0], a[0]), [out], [a], 50, sem="d%d" % (nd[0] - 1), n=16, wake=LOCAL + 128 * side[2] * side[3] / LRATE)
+    def moved(side, times=1):
+        return 8 * (ROW + times * side[2] * side[3] / LRATE)
 
-    def dma_add(out, a):
+    def dma(eng, *pairs, after=()):
         nd[0] += 1
-        return add("gp", lambda: g.dma_start(out[0], a[0], accum_op=Op.add), [out], [a, out], 100, sem="d%d" % (nd[0] - 1), n=16,
-                   wake=LOCAL + 128 * out[2] * out[3] / LRATE)
+        sem = "d%d" % (nd[0] - 1)
+        return add(eng, lambda: [queue[eng].dma_start(o[0], a[0]).then_inc(T.sem[sem], 16) for o, a in pairs], [o for o, a in pairs], [a for o, a in pairs],
+                   2 * ISSUE if eng == "gp" else 50 * len(pairs), sem=sem, n=16 * len(pairs), extra="own", wake=LOCAL, move=sum(moved(o if o[4] else a) for o, a in pairs), after=after)
 
-    def send(k, back, dst, src, after=()):
-        to = T.cores[(rank - back) % N]
-        rid, pid = topo.addr(to)[:2]
-        share = lambda es: es[len(es) // 2:] if src[2] < W else es[:len(es) // 2]
-        mine = share(topo.engines(core, to))
-        mask = sum(1 << e for e in mine)
-        n_in = len(share(topo.engines(T.cores[(rank + back) % N], core)))
-        ns = REMOTE + 128 * src[2] * src[3] / RRATE
-        i = add("gp", lambda: g.remote_dma(dst[0], src[0], T.sem["a%d" % k], T.sem["l%d" % k], pid, rid, mask), [], [src], 2000 if k == 0 else 300,
-                sem="l%d" % k, n=len(mine), extra="remote", wake=ns, after=after)
-        add(None, None, [dst], [], ns, sem="a%d" % k, n=n_in, after=[i])
+    def dma_add(out, a, after=()):
+        nd[0] += 1
+        return add("gp", lambda: g.dma_start(out[0], a[0], accum_op=Op.add), [out], [a, out], ISSUE, sem="d%d" % (nd[0] - 1), n=16, wake=LOCAL, move=moved(out, ADDS),
+                   after=after)
+
+    def hand_over(src, after=()):
+        ks = [k for k in range(len(LONG)) if LONG[k][0] == src]
+        via = helpers(topo, T.cores, rank)[LONG[ks[0]][3]]
+        rid, pid = topo.addr(via)[:2]
+        i = add("gp", lambda: g.remote_dma(T[src][:], T[src][:], T.sem["h" + src], T.sem["l%d" % ks[0]], pid, rid, topo.mask(core, via)), [], [A(src)],
+                2500 if ks[0] == 0 else 300, sem="l%d" % ks[0], n=len(topo.engines(core, via)), extra="own", wake=LOCAL, after=after, move=moved(A(src)))
+        for n, k in enumerate(ks):
+            sender = helpers(topo, T.cores, (rank + LONG[k][1]) % N)[LONG[k][3]]
+            add(None, None, [A(LONG[k][2])], [], 2 * REMOTE + (n + 1) * 128 * A(src)[2] * A(src)[3] / RRATE, sem="a%d" % k, n=len(topo.engines(sender, core)), after=[i])
         return i
 
-    dma("sp", A("ivi"), A("iv"))
-    dma("act", A("taui", slice(0, 8)), A("tau"))
-    dma("sp", A("di"), A("pf"))
-    dma("act", cols("x0", 0, 1024), cols("xs", 0, 1024))
-    dma("sp", cols("x0", 1024, W), cols("xs", 1024, W))
-    dma("act", cols("x0", W, W + 16), cols("xs", 0, 16))
-    dma("sp", A("g0"), A("gn"))
+    def send(k, dst, *srcs):
+        to = T.cores[(rank - 1) % N]
+        rid, pid = topo.addr(to)[:2]
+        call = lambda: g.remote_dma_fused([RemoteDMATransfer(dst_ids=[DstId(rid=rid, pnc=pid)], dma_engine_mask=topo.mask(core, to), remote_sem=T.sem["a%d" % k],
+                                                             srcs=[a[0] for a in srcs], dsts=[dst[0]], alu_op=int(len(srcs) > 1))], local_sem=T.sem["l%d" % k])
+        i = add("gp", call, [], srcs, 300, sem="l%d" % k, n=len(topo.engines(core, to)), extra="own", wake=REMOTE, move=moved(dst))
+        add(None, None, [dst], [], REMOTE + 1000, sem="a%d" % k, n=len(topo.engines(T.cores[(rank + 1) % N], core)), after=[i])
 
-    def rotate(dst, src, s=16):
-        dma("sp", cols(dst, 0, 128), cols(src, 0, 128))
-        dma("sp", A(dst, slice(s, 128), slice(128, C)), A(src, slice(0, 128 - s), slice(128, C)))
-        dma("sp", A(dst, slice(0, s), slice(128, C)), A(src, slice(128 - s, 128), slice(128, C)))
+    i = dma("sp", (A("ivi"), A("iv")))
+    j = dma("act", (A("taui", slice(0, 8)), A("tau")))
+    i = dma("sp", (A("di"), A("pf")), after=[i])
+    dma("act", (cols("x0", 0, 1024), cols("xs", 0, 1024)), after=[i, j])
+    i = dma("sp", (cols("x0", 1024, W), cols("xs", 1024, W)), after=[i])
+
+
+    def rotate(dst, at, src, a, s=16):
+        dma("sp", (A(dst, slice(s, 128), slice(at, at + 128)), A(src, slice(0, 128 - s), slice(a, a + 128))),
+            (A(dst, slice(0, s), slice(at, at + 128)), A(src, slice(128 - s, 128), slice(a, a + 128))))
 
     def shifted(dst, src, s, scale):
         act(cols(dst, s, 128), cols(src, 0, 128 - s), Fn.Identity, scale=scale)
         act(cols(dst, 0, s), cols(src, 128 - s, 128), Fn.Identity, scale=scale)
 
-    rotate("dri", "pf")
-    for name, value in (("one", 1.0), ("s3", 0.0), ("c256", 256.0), ("kt", 1e9), ("rw0", 0.0), ("rw1", 0.0), ("zero", 0.0), ("seg", 1.0)):
+    rotate("dri", 0, "pf", 128)
+    for name, value in (("one", 1.0), ("s3", 0.0), ("c256", 256.0), ("kt", 1e9), ("rw", 0.0), ("zero", 0.0), ("seg", 1.0), ("cin", 0.0)):
         ms(A(name), value)
-    ms(cols("seg", 0, 512, 32), 0.0)
-    ms(cols("xu", W, W + 16), 0.0)
+    ms(cols("seg", 0, C, 32), 0.0)
+    ms(cols("cin", 1, C, 2), 4096.0)
+    ms(cols("cin", C, 384), -15.0 / 32)
+    for name in ("xu", "st0", "st1", "st2"):
+        ms(cols(name, W, W + 16), 0.0)
     ms(cols("zt", W, W + 8), 0.0)
     ms(A("vv", ALL, ALL, slice(16, 17)), 0.0)
     sel(A("tr1"), A("one"), [[-16, 8], [0, 16]], Op.is_ge, 0, 1)
@@ -194,7 +253,7 @@ def build(g, core, T, topo, rank):
     sel(A("e8"), A("one"), [[-1, 8], [0, 16]], Op.is_equal, 0, 1)
     sel(A("idf"), A("one"), [[-1, 128]], Op.is_equal, 0, 1)
     sel(A("blf"), A("tr1"), [[16, 8], [0, 16]], Op.is_ge, 15, -1)
-    sel(A("sel"), A("c256"), [[-1, 16], [-16, 8], [0, 16]], Op.is_equal, 0, 1)
+    gains = dma("gp", (A("g0"), A("gn")), after=[len(ops) - 1])
     iota(A("wc"), [[0, 2]], 128, 1, True)
     iota(A("k3"), [[2, 8]], 0, 0, False)
     iota(A("k4"), [[0, 8]], 0, 1, False)
@@ -208,7 +267,9 @@ def build(g, core, T, topo, rank):
     ts(A("k4"), A("k4"), 8, Op.bitwise_and, 3, Op.logical_shift_right)
     tt(A("k3"), A("k3"), A("k4"), Op.add)
     cp(A("el"), A("k3"))
-    for name, scale in (("id7", 7.0), ("idm", -3.5 / 32), ("idb", 1.0), ("idn", -1.0 / 256), ("i2", 2.0)):
+    ts(A("h32"), A("idf"), -32.0, Op.mult)
+    cp(A("i16"), A("idf"))
+    for name, scale in (("i32", 32.0), ("n32", -32.0), ("i20", 20.0), ("idb", 1.0), ("idn", -1.0 / 256), ("i2", 2.0)):
         act(A(name), A("idf"), Fn.Identity, scale=scale)
     act(A("b4k"), cols("blf", 0, 128, 16), Fn.Identity, scale=4096.0)
     act(A("blk"), A("blf"), Fn.Identity, scale=1.0 / 16)
@@ -218,164 +279,158 @@ def build(g, core, T, topo, rank):
     shifted("back2", "idf", 96, 1.0)
     for j, w in enumerate((-512.0, 32.0, 8192.0)):
         act(A("b3", ALL, ALL, j), cols("blf", 0, 128, 16), Fn.Identity, scale=w)
-    act(cols("cin", 0, 512, 2), cols("c256", 0, C), Fn.Identity, scale=0.0)
-    act(cols("cin", 1, 512, 2), cols("c256", 0, C), Fn.Identity, scale=16.0)
-    act(A("off"), A("one"), Fn.Identity, scale=-15.0 / 32)
 
-    cp(A("ivh"), A("ivi"))
-    cp(A("tauh", slice(0, 8)), A("taui", slice(0, 8)))
-    cp(A("df"), A("di"))
-    for h in range(2):
-        o = A("q5", ALL, slice(16 + h, 32, 2))
-        mm(o, cols("ivh", 128 * h, 128 * h + 128), A("trh"), True, False)
-        mm(o, A("tauh", slice(0, 8), slice(128 * h, 128 * h + 128)), A("e8h", slice(0, 8)), False, True)
-    for h in range(2):
-        mm(q(7, h, 16, 2), A("tauh", slice(0, 8), slice(128 * h, 128 * h + 128)), A("e8h", slice(0, 8), slice(0, 128, 16)))
-    act(A("nt0"), q(7, 0, 16), Fn.Identity, bias=W, scale=-1.0)
-    act(cols("nt1", 0, 16, 2), cols("nt0", 0, 16, 2), Fn.Identity)
-    act(cols("nt1", 3, 16, 2), cols("nt0", 1, 14, 2), Fn.Identity)
-    act(cols("nt1", 1, 2), cols("nt0", 15, 16), Fn.Identity)
-    cp(A("tu"), q(5, C, 2 * C))
-    ts(A("ti"), A("tu"), W - 1, Op.bitwise_and)
-    send(1, 2, A("x2"), A("x0"), [send(0, 1, A("x1"), A("x0"))])
+    def first_times(h):
+        starts = A("tauh", slice(0, 8), slice(128 * h, 128 * h + 128))
+        cp(half("ivh", h), half("ivi", h))
+        mm(q(TC[h], C, 384), half("ivh", h), A("trh"), True, False)
+        mm(q(TC[h], C, 384), starts, A("e8h", slice(0, 8)), False, True)
+        cp(half("tu", h), q(TC[h], C, 384))
+        ts(half("ti", h), half("tu", h), W - 1, Op.bitwise_and)
+        mm(q(4, 8 * h, 8 * h + 8), starts, A("e8h", slice(0, 8), slice(0, 128, 16)))
 
-    def to_list(src, bank, alone=True, last=True):
+    def to_list(src, h, at, alone=True, last=True):
         for m in range(8):
             for gp in range(4):
                 for e in range(2):
-                    a = 4 * gp + 2 * e
-                    mm(q(bank, m, C, 8, slice(32 * gp, 32 * gp + 32)), A("s3", ALL, m, slice(16 - 16 * e, 48 - 16 * e)), A(src, ALL, slice(a, a + 2)),
-                       alone and e == 0, e == 1 if alone else last and (m, e) == (7, 1))
+                    mm(q(TC[h], at + m, at + 128, 8, slice(32 * gp, 32 * gp + 32)), A("s3", ALL, m, slice(16 - 16 * e, 48 - 16 * e)), A(src, ALL, 8 * h + 2 * gp + e),
+                       alone and e == 0, e == 1 if alone else last and (m, e) == (7, 1), (m % 2, gp, e) != (0, 0, 0))
 
-    def centres(bank):
-        act(q(bank, C, 2 * C), A("df"), Fn.Identity, bias=M32, scale=1 + 2.0 ** -15)
-        act(A("lo"), A("df"), Fn.Identity, bias=-M32 - 8192, scale=1 - 2.0 ** -15)
-        tt(A("mb"), q(bank, C, 2 * C), A("lo"), Op.add)
+    def centres(h):
+        ts(half("hi", h), half("df", h), 1.0 / 32, Op.mult, 1024 + 4.015625, Op.add)
+        ts(half("mb", h), half("hi", h), 7.0, Op.mult, -7.0 * (1024 + 9) - MID, Op.add)
+        o = q(TB[h], C, 384)
+        mm(o, A("idf"), half("df", h), True, False)
+        mm(o, A("h32"), half("hi", h), False, False, True)
+        mm(o, A("i32"), half("mb", h), False, True)
+        act(A("at", ALL, h, slice(0, 128)), o, Fn.Identity, bias=BIGH - 36.5 - 1024, scale=-1.0 / 32)
+        n = 128
+        while n < PIECE:
+            if n >= BY_DMA:
+                dma("sp", (A("at", ALL, h, slice(n, 2 * n)), A("at", ALL, h, slice(0, n))))
+            else:
+                copies.append(sel(A("at", ALL, h, slice(n, 2 * n)), A("at", ALL, h, slice(0, n)), [[0, n]], Op.is_ge, 0, 0))
+            n *= 2
 
-    def times(bank):
-        cp(A("th"), A("ti"))
-        to_list("th", bank)
-        cp(A("of0"), q(bank, 0, C))
-        ts(A("of1"), q(bank, 0, C), 1.0, Op.add)
-        ts(A("bi"), A("ti"), 31, Op.bitwise_and)
-        for h in range(2):
-            ts(A("aa", ALL, h, slice(0, 128)), A("th", ALL, slice(h, 16, 2)), 1.0 / 32, Op.mult, 160 - 15.5 / 32, Op.add)
+    def times(h):
+        cp(half("th", h), half("ti", h))
+        to_list("th", h, 0)
+        cp(half("of0", h), q(TC[h], 0, 128))
+        ts(half("of1", h), half("of0", h), 1.0, Op.add)
+        mm(q3(TA[h], 8, 16, 16, 32), A("i16"), half("th", h))
+        ts(A("aa", ALL, h, slice(0, 128)), half("th", h), 1.0 / 32, Op.mult, 160 - 15.5 / 32, Op.add)
+        o = q3(TA[h], 0, 8, 16, 32)
+        mm(o, A("i16"), half("th", h), True, False)
+        mm(o, A("n32"), A("aa", ALL, h, slice(0, 128)), False, False, True)
+        mm(o, A("i20"), half("c256", 0), False, True, True)
         n = 1
         while n < COPIES:
-            ts(A("aa", ALL, ALL, slice(128 * n, 256 * n)), A("aa", ALL, ALL, slice(0, 128 * n)), -float(n), Op.add)
+            ts(A("aa", ALL, h, slice(128 * n, 256 * n)), A("aa", ALL, h, slice(0, 128 * n)), -float(n), Op.add)
             n *= 2
-        for h in range(2):
-            for a in range(0, 64, n):
-                ts(A("oa", ALL, h, slice(128 * a, 128 * (a + n))), A("aa", ALL, h, slice(0, 128 * n)), 160.0 + a, Op.is_equal, cols("wc", 0, 1), Op.mult)
+        for a in range(0, 64, n):
+            ts(A("oa", ALL, h, slice(128 * a, 128 * (a + n))), A("aa", ALL, h), 160.0 + a, Op.is_equal, cols("wc", 0, 1), Op.mult)
 
     def hear(t, h):
-        tab = A("x%d" % t)
-        for j in range(8 * h, 8 * h + 8):
-            w, kq = j // 4 % 2, j % 4
-            xa, bank, a = cols("xa", 512 * kq, 512 * kq + 512), HB[kq], 2048 * h + 512 * kq
-            act(xa, IND(tab, cols("of%d" % w, a // 16, a // 16 + 32)), Fn.Identity)
-            mm(q(bank), A("id7"), xa, True, False)
-            for i in range(4):
-                mm(q(bank, 128 * i, 128 * i + 128), A("idm"), cols("mb", 128 * h, 128 * h + 128), False, i == 3)
-            first = a
-            if j not in VIA_ACT[t]:
-                ts(cols("ind%d" % w, a, a + 512), q(bank), BIG - 896, Op.add, BIG, Op.not_equal)
+        tab = A("st%d" % t)
+        for j in range(4096 // PIECE):
+            w, a = j * PIECE // 2048, 2048 * h + j * PIECE % 2048
+            o, src = cols("ind%d" % w, a, a + PIECE), IND(tab, cols("of%d" % w, a // 16, (a + PIECE) // 16))
+            if (h, j) in FUSED[t]:
+                tt(o, src, A("at", ALL, h), Op.add)
             else:
-                act(cols("ind%d" % w, a, a + 512), q(bank), Fn.Identity, bias=BIGH - 896)
-                if j % 2 == 0:
-                    continue
-                first = a - 512
-                ts(cols("ind%d" % w, first, a + 512), cols("ind%d" % w, first, a + 512), BIGH, Op.not_equal)
-            for b in range(first, a + 512, 128):
-                mm(A("q4", ALL, slice(8 * w, 8 * w + 8), b // 128), cols("ind%d" % w, b, b + 128), A("b4k"))
-            if j % 8 == 3:
-                act(A("t0", ALL, slice(h, 16, 2)), A("q4", ALL, slice(0, 8), slice(16 * h, 16 * h + 16)), Fn.Relu, bias=-5 * 4096.0)
+                heard.append(act(o, src, Fn.Identity))
+                added.append(dma_add(o, A("at", ALL, h), first))
+            ts(o, o, BIGH, Op.not_equal)
+            for b in range(a, a + PIECE, 128):
+                mm(A("q%d" % TA[h], ALL, slice(8 * w, 8 * w + 8), b // 128 % 16), cols("ind%d" % w, b, b + 128), A("b4k"), True, True, b > a)
+            if (j + 1) * PIECE == 2048:
+                act(half("t0", h), q3(TA[h], 0, 8, 0, 16), Fn.Relu, bias=-5 * 4096.0)
 
-    def claims(h):
-        c1, rows, bb = A("q4", ALL, slice(8, 16), slice(16 * h, 16 * h + 16)), slice(h, 16, 2), "bb%d" % h
+    def claims(t, h):
+        c1, bb = q3(TA[h], 8, 16, 0, 16), "bb%d" % h
         ts(c1, c1, -5 * 4096.0, Op.add, 1.0, Op.max)
-        tt(A("ee", ALL, rows), c1, A("t0", ALL, rows), Op.min)
-        tt(A(bb, ALL, slice(0, 2)), A("ee", ALL, rows), A("bi", ALL, rows), Op.add)
+        tt(half("ee", h), c1, half("t0", h), Op.min)
+        tt(A(bb, ALL, slice(0, 2)), q3(TA[h], 0, 8, 16, 32), half("ee", h), Op.add)
         ts(A(bb, ALL, slice(2, 4)), A(bb, ALL, slice(0, 2)), -16.0, Op.add)
         ts(A(bb, ALL, slice(4, 8)), A(bb, ALL, slice(0, 4)), -1.0, Op.add)
+        tt(half("ph", h), q3(TA[h], 8, 16, 16, 32), half("ee", h), Op.add)
+        to_list("ph", h, 128)
+        ts(half("pl%d" % (t % 2), h), q(TC[h], 128, C), float(NONE), Op.min)
 
     def histogram(h):
         ob, bb = "ob%d" % h, "bb%d" % h
         ts(A(ob, ALL, slice(64, 66)), A(bb, ALL, slice(0, 2)), 32.0, Op.is_equal, HALF[h], Op.mult)
-        for a, b, bank in (PIECES if h else ((0, 64, 6),)):
-            for i in range(8):
-                ts(A(ob, ALL, slice(8 * i, 8 * i + 8), slice(a, b)), A(bb, ALL, ALL, slice(a, b)), 2.0 * i, Op.is_equal, HALF[h], Op.mult)
+        for a, b, bank in PIECES:
+            if h == 0:
+                mm(q3(bank, 0, (b - a) // 16, 0, 66), A("idb"), cols("zero", 0, 66 * (b - a) // 16), True, False)
+        for a, b, bank in PIECES:
+            c, d = (a, b) if h else (a // 32 * 32, a // 32 * 32 + 32)
+            for i in range(8 if a == c else 0):
+                ts(A(ob, ALL, slice(8 * i, 8 * i + 8), slice(c, d)), A(bb, ALL, ALL, slice(c, d)), 2.0 * i, Op.is_equal, HALF[h], Op.mult)
             for o in range(a, b):
                 at = 128 * ((o - a) // 16)
-                mm(q(bank, at, at + 66), A("oa", ALL, h, slice(o, 8192, 64)), A(ob, ALL, ALL, o), o % 16 == 0, o % 16 == 15)
-            n = (b - a) // 16
-            part = lambda c, d: q(bank, c, d) if n == 1 else A("q%d" % bank, ALL, slice(0, n), slice(c, d))
-            ts(cols("rr%d" % h, 4 * a, 4 * b), part(0, 64), 4096.0, Op.min)
-            ts(A("rw%d" % h, ALL, slice(a // 16, b // 16), slice(0, 2)), part(64, 66), 4096.0, Op.min)
+                mm(q(bank, at, at + 66), A("oa", ALL, h, slice(o, 8192, 64)), A(ob, ALL, ALL, o), False, h == 1 and o == b - 1, o % 8 > 0)
+            if h:
+                ts(cols("rr", 4 * a, 4 * b), q3(bank, 0, (b - a) // 16, 0, 64), 4096.0, Op.min)
+                ts(A("rw", ALL, slice(a // 16, b // 16), slice(0, 2)), q3(bank, 0, (b - a) // 16, 64, 66), 4096.0, Op.min)
 
     def owners(t):
-        mm(q(4, 0, C), A("idb"), A("zero"), True, False)
-        for h in range(2):
-            for at, same, on in [(0, "idu", "isu"), (128, "idh", "ish")][t == VI - 1:]:
+        for at, same, on in [(0, "idu", "isu"), (128, "idh", "ish")][t == VI - 1:]:
+            for g2 in range(2):
                 for b4 in (1, 0):
-                    for g2 in range(2):
-                        o = q(4, at + b4, at + 128, 2, slice(64 * g2, 64 * g2 + 64))
-                        mm(o, cols("rr%d" % h, 2 * b4 + g2, C, 4), cols(same, g2, 128, 2), False, False)
-                        if b4 == 0:
-                            mm(o, cols("rw%d" % h, g2, 128, 2), cols(on, g2, 128, 2), False, (h, at) == (1, 128))
-        if t < VI - 1:
-            ts(A("u%d" % t), q(4, 0, 128), M512, Op.add, M512 + 512, Op.is_equal)
-        ts(A("idx"), q(4, 128, C), -0.2, Op.add, 700.0, Op.min)
+                    o = q(7, at + b4, at + 128, 2, slice(64 * g2, 64 * g2 + 64))
+                    mm(o, cols("rr", 2 * b4 + g2, C, 4), cols(same, g2, 128, 2), True, b4 == 1, (g2, b4) != (0, 1))
+                    if b4 == 0:
+                        mm(o, cols("rw", g2, 128, 2), cols(on, g2, 128, 2), False, True, True)
+            if at == 0:
+                ts(A("u%d" % t), q(7, 0, 128), M512, Op.add, M512 + 512, Op.is_equal)
+        ts(A("idx"), q(7, 128, C), -0.2, Op.add, 700.0, Op.min)
         for h in range(2):
-            act(cols("kt", C + h, 2 * C, 2), cols("df", 128 * h, 128 * h + 128), Fn.Identity, scale=1.0 / 32)
+            act(cols("kt", C + h, 2 * C, 2), half("df", h), Fn.Identity, scale=1.0 / 32)
 
     def spread(u, j, bank, x=None, sign="idb"):
         if x:
             mm(q(bank), A(sign), cols(x, j, W, 4), True, False)
         for i in range(4):
-            mm(q(bank, i, 512, 4), cols("sel", 128 * (4 * i + j), 128 * (4 * i + j) + 128), A(u), not x, i == 3 or not x)
+            mm(q(bank, i, 512, 4), cols("sel", 128 * (4 * i + j), 128 * (4 * i + j) + 128), A(u), not x, i == 3 or not x, i > 0)
 
     def logs():
-        parts = [(a, a + 512) for a in range(0, W, 512)]
+        parts = [(a, a + 1024) for a in range(0, W, 1024)]
         for a, b in parts:
-            i = act(cols("lg0", a, b), cols("g0", a, b), Fn.Ln, load=1300 * (a == 0))
-        act(A("ef0"), A("df"), Fn.Exp, scale=1.0 / 256, load=1500, after=range(i - 3, i + 1))
+            i = act(cols("lg0", a, b), cols("g0", a, b), Fn.Ln, load=1300 * (a == 0), after=heard[-1:])
+        act(A("ef0"), A("df"), Fn.Exp, scale=1.0 / 256, load=1500, after=range(i - 1, i + 1))
         for a, b in parts:
             act(cols("lg0", a, b), cols("lg0", a, b), Fn.Identity, scale=-4.0)
-            act(cols("xa", a, b), cols("x0", a, b), Fn.Identity, scale=-0.5)
-        dma_add(A("lg0"), A("xa"))
+            act(cols("st2", a, b), cols("x0", a, b), Fn.Identity, scale=-0.5, after=heard[-1:])
+        dma_add(A("lg0"), cols("st2", 0, W))
+        hand_over("lg0")
 
     def terms(t, a, b):
         tt(cols("wv", a, b), IND(A("kt"), cols("idx", a // 16, b // 16)), cols("x%d" % t, a, b), Op.max)
         if b % 1024 == 0:
-            i = dma_add(cols("wv", b - 1024, b), cols("lg%d" % t, b - 1024, b))
-            if (t, b) == (0, W):
-                send(3, 1, A("lg1"), A("lg0"), [i])
-            for c in range(b - 1024, b, 512):
-                act(cols("zt", c, c + 512), cols("wv", c, c + 512), Fn.Exp, scale=-0.25)
-        if b == 1024:
-            act(cols("zt", W, W + 1), cols("zt", 0, 1), Fn.Identity)
+            dma_add(cols("wv", b - 1024, b), cols("lg%d" % t, b - 1024, b))
 
-    def gather_terms(t, parts, to=None):
-        for h, a, b in parts:
-            act(A("zg", ALL, h if to is None else to, slice(128 * a, 128 * b)), IND(A("zt"), cols("pl%d" % (t % 2), 128 * h + 8 * a, 128 * h + 8 * b)), Fn.Identity)
-
-    def halve_terms(t):
-        for h in range(2):
-            for a in (0, 4):
-                gather_terms(t, [(h, a + 8, a + 12), (h, a, a + 4)])
-                dma_add(A("zg", ALL, h, slice(128 * a, 128 * a + 512)), A("zg", ALL, h, slice(128 * a + 1024, 128 * a + 1536)))
-        n = 1024
-        for _ in range(LEVELS[t] - 1):
-            n //= 2
-            dma_add(A("zg", ALL, ALL, slice(0, n)), A("zg", ALL, ALL, slice(n, 2 * n)))
+    def gather_terms(t, h, a, b, to):
+        act(A("zg", ALL, to, slice(128 * a, 128 * b)), IND(A("zt"), cols("pl%d" % (t % 2), 128 * h + 8 * a, 128 * h + 8 * b)), Fn.Identity, after=heard[-1:])
 
     def home(t, h):
         return A("back%d" % t if h and t else "idf")
 
-    def sum_terms(t, bank):
-        n = 16 >> LEVELS[t]
+    def sum_terms(t):
+        for b in (1024, W):
+            act(cols("zt", b - 1024, b), cols("wv", b - 1024, b), Fn.Exp, scale=-0.25, after=heard[-HOLD:][:1])
+        act(cols("zt", W, W + 1), cols("zt", 0, 1), Fn.Identity)
         for h in range(2):
+            for a in (8, 0):
+                gather_terms(t, h, a, a + 8, h)
+            n = 2048
+            for _ in range(LEVELS[t][h]):
+                n //= 2
+                dma_add(A("zg", ALL, h, slice(0, n)), A("zg", ALL, h, slice(n, 2 * n)))
+
+    def add_terms(t, bank):
+        for h in range(2):
+            n = 16 >> LEVELS[t][h]
             for k in range(n):
                 mm(q(bank, 128 * h, 128 * h + 128), home(t, h), A("zg", ALL, h, slice(128 * k, 128 * k + 128)), k == 0, k == n - 1)
         if t == 0:
@@ -387,85 +442,86 @@ def build(g, core, T, topo, rank):
     def taken_columns(t):
         x = "x%d" % t
         for j in range(4):
-            spread("u%d" % t, j, HB[j], x if j % 2 else None)
-            if j % 2:
-                act(cols("xu", j, W, 4), q(HB[j]), Fn.Relu, bias=-256.0)
+            spread("u%d" % t, j, XB[j], None if j in XU_DVE else x)
+            if j in XU_DVE:
+                tt(cols("xu", j, W, 4), q(XB[j]), cols(x, j, W, 4), Op.min)
             else:
-                tt(cols("xu", j, W, 4), q(HB[j]), cols(x, j, W, 4), Op.min)
+                act(cols("xu", j, W, 4), q(XB[j]), Fn.Relu, bias=-256.0)
         cp(cols("xu", W, W + 1), cols("xu", 0, 1))
 
-    def taken(t):
-        mm(q(4), A("idb"), A("cin"), True, False)
-        for h in range(2):
-            mm(q(5 + h, 0, 128), A("idb"), A("off"), True, False)
+    def taken(t, h):
+        mm(q(TA[h], 0, C), A("idb"), cols("cin", 0, C), True, False)
+        mm(q(TB[h], 384, 512), A("idb"), cols("cin", C, 384), True, False)
         for kq in range(4):
-            for h in range(2):
-                a = 2048 * h + 512 * kq
-                o, src = cols("xg", a, a + 512), IND(A("xu"), cols("pl%d" % (t % 2), a // 16, a // 16 + 32))
-                if (h, kq) in XG_DVE:
-                    cp(o, src)
-                else:
-                    act(o, src, Fn.Identity)
-                for k in range(4 * kq, 4 * kq + 4):
-                    a, s = 2048 * h + 128 * k, int(k == 0)
-                    mm(A("q4", ALL, slice(h, 16, 2), slice(2 * k - 1 + s, 2 * k + 2)), cols("xg", a, a + 128), A("b3", ALL, ALL, slice(s, 3)), False, h + k == 16)
-                    mm(q(5 + h, 0, 128), A("r2" if h else "i2"), cols("xg", a, a + 128), False, k == 15)
+            a = 2048 * h + 512 * kq
+            o, src = cols("xg", a, a + 512), IND(A("xu"), cols("pl%d" % (t % 2), a // 16, a // 16 + 32))
+            if (h, kq) in XG_DVE:
+                cp(o, src)
+            else:
+                act(o, src, Fn.Identity)
+            for k in range(4 * kq, 4 * kq + 4):
+                a, s = 2048 * h + 128 * k, int(k == 0)
+                mm(q3(TA[h], 0, 8, 2 * k - 1 + s, 2 * k + 2), cols("xg", a, a + 128), A("b3", ALL, ALL, slice(s, 3)), False, k == 15, k % 4 > 0)
+            for k in range(4 * kq, 4 * kq + 4):
+                a = 2048 * h + 128 * k
+                mm(q(TB[h], 384, 512), A("r2" if h else "i2"), cols("xg", a, a + 128), False, k == 15, k % 4 > 0)
 
     def next_table(t):
-        x = "x%d" % t
         for j in range(4):
-            spread("ul%d" % t, j, (j + 1) % 2, x, "idn")
-            act(cols(x, j, W, 4), q((j + 1) % 2), Fn.Relu, scale=-256.0)
-        act(cols(x, W, W + 1), cols(x, 0, 1), Fn.Identity)
+            bank = (4, 7)[j % 2]
+            spread("ul%d" % t, j, bank, "x%d" % t, "idn")
+            act(cols("st%d" % t, j, W, 4), q(bank), Fn.Identity, scale=-7 * 256.0, bias=-MID)
+        act(cols("st%d" % t, W, W + 1), cols("st%d" % t, 0, 1), Fn.Identity)
 
-    def profiles(t):
-        for h in range(2):
-            act(cols("tnb", 128 * h, 128 * h + 128), A("q4", ALL, slice(h, 16, 2), slice(0, 32, 2)), Fn.Relu, bias=1.0, scale=-1.0)
-        for h in range(2):
-            mm(q(7, 128 * h, 128 * h + 128), cols("tnb", 128 * h, 128 * h + 128), A("idb"))
-        act(A("ntp"), q(7, 0, C), Fn.Identity)
-        for h in range(2):
-            mm(q(7, C + 128 * h, C + 128 * h + 128), A("blr" if h else "blk"), cols("ntp", 128 * h, 128 * h + 128))
-        tt(A("d1"), q(7, C, 2 * C), A("dri" if t == 0 else "drf"), Op.mult)
-        for h in range(2):
-            tt(cols("d2", 128 * h, 128 * h + 128), q(5 + h, 0, 128), cols("d1", 128 * h, 128 * h + 128), Op.add)
-        ts(A("df"), A("d2"), M1, Op.add, -M1, Op.add)
-        centres(6)
-        if t == 0:
-            rotate("drf", "df")
+    def profiles(t, h):
+        act(half("tnb", h), q3(TA[h], 0, 8, 0, 32, 2), Fn.Relu, bias=1.0, scale=-1.0)
+        mm(q(TB[h], 0, 128), half("tnb", h), A("idb"))
+        act(half("ntp", h), q(TB[h], 0, 128), Fn.Identity)
+        mm(q(TB[h], 128, C), A("blr" if h else "blk"), half("ntp", h))
+        tt(half("d1", h), q(TB[h], 128, C), A("drf" if t else "dri") if h else half("df", 0), Op.mult)
+        tt(half("d2", h), q(TB[h], 384, 512), half("d1", h), Op.add)
+        ts(half("df", h), half("d2", h), M1, Op.add, -M1, Op.add)
+        centres(h)
+        if t == 0 and h:
+            rotate("drf", 0, "df", 128)
 
-    def tapes(t):
-        sx, lx = q(4, 0, 512, 2), q(4, 1, 512, 2)
-        tt(cols("sl", 0, 512, 2), sx, A("ee"), Op.min)
-        ts(cols("sl", 1, 512, 2), lx, 0.0, Op.is_lt, B, Op.mult)
-        tt(A("tk"), lx, A("ti"), Op.min)
-        profiles(t)
-        o, d, seg = q(0), A("sl"), A("seg")
+    def tapes(t, h):
+        sx, lx = q3(TA[h], 0, 8, 0, 32, 2), q3(TA[h], 0, 8, 1, 32, 2)
+        rows, bank = slice(8 * h, 8 * h + 8), TC[h]
+        tt(A("sl", ALL, h, slice(0, C, 2)), sx, half("ee", h), Op.min)
+        ts(A("sl", ALL, h, slice(1, C, 2)), lx, 0.0, Op.is_lt, B, Op.mult)
+        tt(q(bank, 0, 128), lx, half("th", h), Op.min)
+        profiles(t, h)
+        o, d, seg = A("sc", ALL, h), A("sl", ALL, h), A("seg")
         add("dve", lambda: g.vector.tensor_tensor_scan(o[0], seg[0], d[0], 0.0, Op.mult, Op.add), [o], [d, seg], vtime(o, d))
-        vv = A("vv", ALL, ALL, slice(0, 16))
-        tt(vv, q(0, 0, 512, 2), A("tk"), Op.add)
+        vv = A("vv", ALL, rows, slice(0, 16))
+        tt(vv, q(bank, 0, 128), A("sc", ALL, h, slice(0, C, 2)), Op.add)
         at = [0]
 
-        def moves(src, spans, bank):
+        def moves(src, spans, row):
             for j, (d, a, b, n) in enumerate(spans):
-                o = cols("cl", at[0], at[0] + 16 * n)
-                at[0] += 16 * n
-                ts(o, A(src, ALL, ALL, slice(a, a + n)), d * B, Op.max, (d + 1) * B, Op.min)
-                mm(A(bank, ALL, slice(0, 16), slice(b, b + n)), A("idf"), o, j == 0, j == len(spans) - 1)
+                o = A("cl", ALL, h, slice(at[0], at[0] + 8 * n))
+                at[0] += 8 * n
+                ts(o, A(src, ALL, rows, slice(a, a + n)), d * B, Op.max, (d + 1) * B, Op.min)
+                mm(q3(bank, row, row + 8, b, b + n), A("idf"), o, j == 0, j == len(spans) - 1)
 
-        moves("vv", [(1, 1, 0, 16)] + [(d, 2 * d - 1, d - 1, 17 - 2 * d) for d in range(2, 9)], "q3")
-        ts(A("c0"), vv, 0.0, Op.max, B, Op.min)
-        tt(A("e2"), A("vv", ALL, ALL, 15), A("nt%d" % t), Op.add)
-        act(A("er"), IND(A("e2"), A("el")), Fn.Identity)
-        tt(A("acc"), q(3, 0, C), A("c0"), Op.add)
-        ts(A("nw"), A("acc", ALL, ALL, slice(0, 8)), W - 1, Op.bitwise_and)
-        tt(A("v2"), A("nw"), A("er"), Op.add)
-        moves("v2", [(e, 0, 16 - e, e) for e in range(8, 0, -1)], "q2")
-        late = A("acc", ALL, ALL, slice(8, 16))
-        tt(late, A("q2", ALL, slice(0, 16), slice(8, 16)), late, Op.add)
-        ts(A("ti", ALL, slice(0, 16, 2)), A("acc", ALL, slice(0, 16, 2)), W - 1, Op.bitwise_and)
-        ts(A("ti", ALL, slice(3, 16, 2)), A("acc", ALL, slice(1, 14, 2)), W - 1, Op.bitwise_and)
-        ts(A("ti", ALL, 1), A("acc", ALL, 15), W - 1, Op.bitwise_and)
+        moves("vv", [(1, 1, 0, 16)] + [(d, 2 * d - 1, d - 1, 17 - 2 * d) for d in range(2, 9)], 16)
+        ts(half("c0", h), vv, 0.0, Op.max, B, Op.min)
+        tt(A("e2", ALL, rows), A("vv", ALL, rows, 15), A("nt%d" % t, ALL, rows), Op.add)
+        tt(half("acc", h), q(bank, C, 384), half("c0", h), Op.add)
+        nw = cols("nw", 64 * h, 64 * h + 64)
+        ts(nw, A("acc", ALL, rows, slice(0, 8)), W - 1, Op.bitwise_and)
+        er = cols("er", 64 * h, 64 * h + 64)
+        act(er, IND(A("e2", ALL, rows), cols("el", 0, 4)), Fn.Identity)
+        tt(A("v2", ALL, rows), nw, er, Op.add)
+        moves("v2", [(e, 0, 16 - e, e) for e in range(8, 0, -1)], 24)
+        late = A("acc", ALL, rows, slice(8, 16))
+        tt(late, q3(bank, 24, 32, 8, 16), late, Op.add)
+        if h:
+            ts(A("ti", ALL, slice(9, 16)), A("acc", ALL, slice(8, 15)), W - 1, Op.bitwise_and)
+            ts(A("ti", ALL, 8), A("acc", ALL, 15), W - 1, Op.bitwise_and)
+        else:
+            ts(half("ti", 0), half("acc", 0), W - 1, Op.bitwise_and)
 
     def last_terms(t):
         for c in range(len(LAST) - 1):
@@ -477,9 +533,17 @@ def build(g, core, T, topo, rank):
             tt(cols("zt", a, b), q(c % 4, 0, b - a), cols("g%d" % t, a, b), Op.mult)
             if a == 0:
                 act(cols("zt", W, W + 1), cols("zt", 0, 1), Fn.Identity)
-        gather_terms(t, [(1, 0, 1), (1, 1, 4), (1, 4, 10), (1, 10, 16)], 0)
-        for k in range(16):
-            mm(q(0, 0, 128), home(t, 1), A("zg", ALL, 0, slice(128 * k, 128 * k + 128)), k == 0, k == 15)
+        for a, b in ((0, 1), (1, 3), (3, 7), (7, TAIL)):
+            gather_terms(t, 1, a, b, 0)
+        o = A("zg", ALL, 0, slice(128 * TAIL, 128 * TAIL + 128))
+        for k in range(TAIL, 16):
+            src = IND(A("zt"), cols("pl%d" % (t % 2), 128 + 8 * k, 128 + 8 * k + 8))
+            if k == TAIL:
+                cp(o, src)
+            else:
+                tt(o, src, o, Op.add)
+        for k in range(min(16, TAIL + 1)):
+            mm(q(5, 0, 128), home(t, 1), A("zg", ALL, 0, slice(128 * k, 128 * k + 128)), k == 0, k == min(15, TAIL))
         for k in range(16):
             src, o = IND(A("zt"), cols("pl%d" % (t % 2), 8 * k, 8 * k + 8)), A("yb" if k % 2 else "ya")
             if k == 1:
@@ -487,45 +551,58 @@ def build(g, core, T, topo, rank):
             else:
                 tt(o, src, cols("yacc", 0, 128) if k == 0 else o, Op.add)
         tt(cols("ys", 0, 128), A("ya"), A("yb"), Op.add)
-        dma("sp", cols("y", 0, 128), cols("ys", 0, 128))
-        tt(cols("ys", 128, C), q(0, 0, 128), cols("yacc", 128, C), Op.add)
-        dma("act", cols("y", 128, C), cols("ys", 128, C))
+        dma("sp", (cols("y", 0, 128), cols("ys", 0, 128)))
+        tt(cols("ys", 128, C), q(5, 0, 128), cols("yacc", 128, C), Op.add)
+        dma("act", (cols("y", 128, C), cols("ys", 128, C)))
 
-    centres(1)
-    times(5)
+    cp(A("tauh", slice(0, 8)), A("taui", slice(0, 8)))
+    cp(A("df"), A("di"))
+    for h in range(2):
+        first_times(h)
+    act(A("nt0"), q(4, 0, 16), Fn.Identity, bias=W, scale=-1.0)
+    act(cols("nt1", 0, 8), cols("nt0", 0, 8), Fn.Identity)
+    act(cols("nt1", 9, 16), cols("nt0", 8, 15), Fn.Identity)
+    act(cols("nt1", 8, 9), cols("nt0", 15, 16), Fn.Identity)
+    for a in (0, 1024):
+        act(cols("st0", a, a + 1024), cols("x0", a, a + 1024), Fn.Identity, scale=7.0, bias=-MID)
+    act(cols("st0", W, W + 1), cols("st0", 0, 1), Fn.Identity)
+    for h in range(2):
+        centres(h)
+        times(h)
+    first = [hand_over("x0", [gains] + copies)]
     for t in range(VI):
-        mm(q(5, 0, C), A("idb"), A("zero"), True, False)
-        to_list("th", 5, False, False)
-        if t == 2:
-            sum_terms(0, 7)
         for h in range(2):
             hear(t, h)
-            claims(h)
+            claims(t, h)
             histogram(h)
-        to_list("ee", 5, False)
-        ts(A("pl%d" % (t % 2)), q(5, 0, C), float(NONE), Op.min)
         if t > 0:
-            halve_terms(t - 1)
+            sum_terms(t - 1)
         owners(t)
         if t == VI - 1:
-            sum_terms(t - 1, 5)
+            add_terms(t - 1, 6)
             last_terms(t)
             break
         if t == 0:
+            hand_over("g0", added[-1:])
+            for a in range(0, 16, 2):
+                sel(cols("sel", 128 * a, 128 * a + C), A("c256"), [[-1, 2], [-16, 8], [0, 16]], Op.is_equal, -a, 1, added[-1:])
             logs()
-            send(2, 1, A("ul1"), A("u0"))
+            send(4, A("ul1"), A("u0"))
         else:
-            act(A("ev"), A("df"), Fn.Exp, scale=1.0 / 256)
-            rotate("ef1", "ev", 112)
-            tt(A("us"), A("u1"), A("ul1"), Op.add)
-            send(5, 2, A("g2"), A("g0"), [send(4, 1, A("ul2"), A("us"))])
+            act(half("ef1", 0), half("df", 0), Fn.Exp, scale=1.0 / 256)
+            act(A("ev"), half("df", 1), Fn.Exp, scale=1.0 / 256)
+            rotate("ef1", 128, "ev", 0, 112)
+            send(5, A("ul2"), A("u1"), A("ul1"))
         taken_columns(t)
-        taken(t)
         for a in range(0, W, STEP):
             terms(t, a, a + STEP)
-        tapes(t)
+        for h in range(2):
+            taken(t, h)
+            tapes(t, h)
+            times(h)
         next_table(t + 1)
-        times(4)
+        if t > 0:
+            add_terms(t - 1, 7)
     if not ORDER:
         ORDER.extend(arrange(ops))
     emit([ops[i] for i in ORDER], queue, T)
@@ -534,6 +611,7 @@ def build(g, core, T, topo, rank):
 def arrange(ops):
     seen, last = {}, {}
     before = []
+    count = len(ops)
     for i, o in enumerate(ops):
         dep = {j: 0 for j in o["after"]}
         for mine, write in ((o["r"], False), (o["w"], True)):
@@ -552,6 +630,13 @@ def arrange(ops):
                         keep.append(e)
                 seen[name] = keep + [(i, write, p0, p1, m)]
         before.append(dep)
+    ops, moving = list(ops), {}
+    for i in range(count):
+        if ops[i]["move"]:
+            moving[i] = len(ops)
+            ops.append({"eng": "dm", "ns": ops[i]["move"], "wake": ops[i]["wake"], "sem": True})
+    before = [{moving[j] if j in moving and (gap or not ops[i]["eng"]) else j: gap for j, gap in dep.items()} for i, dep in enumerate(before)]
+    before += [{i: 0} for i in moving]
     behind = [{} for o in ops]
     for i, dep in enumerate(before):
         for j, gap in dep.items():
@@ -594,20 +679,122 @@ def arrange(ops):
         return end
 
     tail = [o["wake"] if o["sem"] else 0.0 for o in ops]
-    chain = [o["ns"] + w for o, w in zip(ops, tail)]
-    for i in range(len(ops) - 1, -1, -1):
+    chain, left = [o["ns"] + w for o, w in zip(ops, tail)], [len(d) for d in behind]
+    todo = [i for i in range(len(ops)) if not left[i]]
+    while todo:
+        i = todo.pop()
         for j, gap in before[i].items():
             chain[j] = max(chain[j], ops[j]["ns"] + gap + chain[i])
-    turn, best = sorted(range(len(ops)), key=lambda i: -chain[i]), None
-    for how in (place, fit, fit) * ROUNDS:
-        end = how(turn, before, [0.0] * len(ops))
-        span = max(e + w for e, w in zip(end, tail))
-        if best is None or span < best[0]:
-            best = (span, sorted(turn, key=lambda i: end[i] - ops[i]["ns"]))
-        end = how(sorted(turn[::-1], key=lambda i: -end[i] - tail[i]), behind, tail)
-        turn = sorted(turn, key=lambda i: -end[i])
+            left[j] -= 1
+            if not left[j]:
+                todo.append(j)
+    def replay(order, slow):
+        end, free = [0.0] * len(ops), {e: 0.0 for e in ENG + (None,)}
+        for i in order:
+            for j in (i, moving[i]) if i in moving else (i,):
+                e = ops[j]["eng"]
+                end[j] = max([end[k] + gap for k, gap in before[j].items()] + [free[e]]) + ops[j]["ns"] + ops[j].get("more", 0.0) * (slow - 1)
+                free[e] = end[j] if e else 0.0
+        return max(e + w for e, w in zip(end, tail))
+
+    best, seed = None, 1
+    for trial in range(TRIALS):
+        noise = []
+        for i in ops:
+            seed = (seed * 1103515245 + 12345) % 2 ** 31
+            noise.append(seed / 2 ** 31 * NOISE * (trial > 0))
+        turn = sorted(range(len(ops)), key=lambda i: -chain[i] - noise[i])
+        end = place(turn, before, [0.0] * len(ops))
+        turn = sorted(turn, key=lambda i: end[i])
+        for how in (place, fit, fit) * ROUNDS:
+            end = how(turn, before, [0.0] * len(ops))
+            order = [i for i in sorted(turn, key=lambda i: end[i] - ops[i]["ns"]) if i < count]
+            span = sum(replay(order, s) for s in SLOW) / len(SLOW)
+            if best is None or span < best[0]:
+                best = (span, order)
+            end = how(sorted(turn[::-1], key=lambda i: -end[i] - tail[i]), behind, tail)
+            turn = sorted(turn, key=lambda i: -end[i])
+
+    needs = [list(d.items()) for d in before]
+    users = [list(d) for d in behind]
+    lengths = [[o["ns"] + o.get("more", 0.0) * (s - 1) for o in ops] for s in SLOW]
+    issuer = {j: i for i, j in moving.items()}
+
+    def run(lines):
+        left, nxt, prv = [len(d) for d in needs], {}, {}
+        for line in lines.values():
+            for a, b in zip(line, line[1:]):
+                nxt[a], prv[b] = b, a
+                left[b] += 1
+        todo = [i for i in range(len(ops)) if not left[i]]
+        for i in todo:
+            for j in users[i] + [nxt[i]] if i in nxt else users[i]:
+                left[j] -= 1
+                if not left[j]:
+                    todo.append(j)
+        if len(todo) < len(ops):
+            return None
+        runs = []
+        for ns in lengths:
+            end, why = [0.0] * len(ops), [-1] * len(ops)
+            for i in todo:
+                w = prv.get(i, -1)
+                at = end[w] if w >= 0 else 0.0
+                for k, gap in needs[i]:
+                    if end[k] + gap > at:
+                        at, w = end[k] + gap, k
+                end[i], why[i] = at + ns[i], w
+            last = max(range(len(ops)), key=lambda i: end[i] + tail[i])
+            runs.append((end[last] + tail[last], why, last, end))
+        return sum(r[0] for r in runs) / len(runs), runs, prv, todo
+
+    def rnd(n):
+        seed[0] = (seed[0] * 1103515245 + 12345) % 2 ** 31
+        return (seed[0] >> 8) % n
+
+    def settled(lines):
+        now = run(lines)
+        if now:
+            line = sorted(lines["dm"], key=lambda j: now[1][0][3][issuer[j]])
+            if line != lines["dm"]:
+                lines["dm"] = line
+                now = run(lines)
+        return now
+
+    seed = [seed]
+    lines = {e: [i for i in best[1] if ops[i]["eng"] == e] for e in ENG}
+    lines["dm"] = [moving[i] for i in best[1] if i in moving]
+    now = best = settled(lines)
+    for _ in range(MOVES):
+        span, why, i, end = now[1][rnd(len(SLOW))]
+        pairs = []
+        while i >= 0:
+            if why[i] >= 0 and now[2].get(i) == why[i] and why[i] not in before[i]:
+                pairs.append((why[i], i))
+            i = why[i]
+        a, b = pairs[rnd(len(pairs))]
+        if a in issuer:
+            a, b = issuer[a], issuer[b]
+            if ops[a]["eng"] != ops[b]["eng"]:
+                continue
+        old = dict(lines)
+        line = lines[ops[a]["eng"]] = list(lines[ops[a]["eng"]])
+        step = (0, 0, 1, 2, 4, 8, 16, 32)[rnd(8)]
+        if rnd(2):
+            line.remove(b)
+            line.insert(max(0, line.index(a) - step), b)
+        else:
+            line.remove(a)
+            line.insert(line.index(b) + 1 + step, a)
+        new = settled(lines)
+        if new and new[0] <= now[0] + rnd(SLACK):
+            now = new
+            if new[0] < best[0]:
+                best = new
+        else:
+            lines = old
     SPAN.append(best[0])
-    return best[1]
+    return [i for i in best[3] if i < count]
 
 
 def emit(ops, queue, T):
@@ -678,6 +865,10 @@ def emit(ops, queue, T):
 
 def rank_program(g, core, T, topo):
     rank = T.rank_of(core)
-    if rank is None:
+    if rank is not None:
+        build(g, core, T, topo, rank)
         return
-    build(g, core, T, topo, rank)
+    for r in range(N):
+        for me, c in enumerate(helpers(topo, T.cores, r)):
+            if c == core:
+                pass_on(g, core, T, topo, r, me)

@@ -4,21 +4,30 @@ from concourse.mybir import AluOpType as Op, ActivationFunctionType as Fn
 N, W, C, VI = 8, 2048, 256, 3
 BIGH = 1.5 * 2 ** 13
 M1 = 1.5 * 2 ** 23
-M512 = 1.5 * 2 ** 32
+M256 = 1.5 * 2 ** 31
 MID = 945.0
 B = 8192.0
-HALF = (8.0, 8 + 3.0 / 128)
+HALF = (2.0, 2 + 3.0 / 512)
+M2K = 1.5 * 2 ** 34
+OFF = 1023.5
 NONE = W + 2
 COPIES = 4
-PIECES = ((0, 32, 1), (32, 48, 3), (48, 64, 4))
+PIECES = ((0, 2, 1), (2, 4, 3))
 LEVELS = ((2, 2), (1, 1))
 PIECE = 1024
-FUSED = ((), (), ())
+NEW = (((0, 16),), ((0, 16),))
+HEAR = (((0, 0, 8), (0, 8, 16), (1, 0, 8), (1, 8, 16)), ((0, 0, 8), (0, 8, 16), (1, 0, 8), (1, 8, 12), (1, 12, 16)))
+ROWS = ((16,), (8, 16))
+COUNT = ((0, 8, 16), (0, 8, 16))
+JOIN = ((3, 5, 7, 9, 11, 13, 15), ())
 XB = (5, 6, 0, 2)
 XU_DVE = (3,)
 XG_DVE = ((0, 0), (0, 2))
-HOLD = 1
-BY_DMA = 512
+VV_PE = False
+TNB_DVE = (0,)
+ER_DVE = (0,)
+XG = (0, 4, 8, 12, 16)
+DOUBLE = ((("act", "dve", "dve"), ("act", "dve", "gp")), (("act", "gp", "gp"), ("act", "gp", "gp")))
 TAIL = 13
 STEP = 256
 LAST = (0, 256, 768, 1280, 1792, 2048)
@@ -28,41 +37,35 @@ S, P = "sbuf", "psum"
 X3 = [128, W + 16]
 H3 = [128, 16, 16]
 SCRATCH = {
-    "x0": (S, [128, W], "bfloat16"), "x1": (S, [128, W], "bfloat16"), "x2": (S, [128, W], "bfloat16"),
-    "st0": (S, X3, "bfloat16"), "st1": (S, X3, "bfloat16"), "st2": (S, X3, "bfloat16"),
+    "x0": (S, X3, "bfloat16"), "x1": (S, X3, "bfloat16"), "x2": (S, X3, "bfloat16"),
     "g0": (S, [128, W], "bfloat16"), "g2": (S, [128, W], "bfloat16"), "lg0": (S, [128, W], "float32"), "lg1": (S, [128, W], "float32"),
-    "xu": (S, X3, "bfloat16"), "zt": (S, [128, W + 8], "float32"), "wv": (S, [128, W], "float32"),
-    "xg": (S, [128, 4096], "bfloat16"), "zg": (S, [128, 2, 2048], "float32"),
+    "xu": (S, X3, "bfloat16"), "zt": (S, [128, W + 8], "float32"), "wv": (S, [128, W + 8], "float32"),
+    "xg": (S, [128, 4096], "bfloat16"), "zg0": (S, [128, 2, 2048], "float32"), "zg1": (S, [128, 2, 2048], "float32"),
     "ind0": (S, [128, 4096], "bfloat16"), "ind1": (S, [128, 4096], "bfloat16"),
-    "oa": (S, [128, 2, 8192], "float16"), "ob0": (S, [128, 66, 64], "float16"), "ob1": (S, [128, 66, 64], "float16"),
+    "oa": (S, [128, 2, 8192], "float16"), "ob0": (S, [128, 264, 16], "float16"), "ob1": (S, [128, 264, 16], "float16"),
     "ivi": (S, [128, C], "int32"), "ivh": (S, [128, C], "float16"), "taui": (S, [128, C], "int32"), "tauh": (S, [128, C], "float16"),
     "di": (S, [128, C], "int32"), "df": (S, [128, C], "float32"), "dri": (S, [128, 128], "int32"), "drf": (S, [128, 128], "float32"),
-    "kt": (S, [128, 704], "float32"), "mb": (S, [128, C], "bfloat16"), "hi": (S, [128, C], "float16"), "at": (S, [128, 2, PIECE], "float32"),
-    "tu": (S, [128, C], "int32"), "ti": (S, H3, "int32"), "th": (S, H3, "float16"), "ph": (S, H3, "float16"),
+    "kt": (S, [128, 264], "float32"), "mb": (S, [128, C], "bfloat16"), "hi": (S, [128, C], "float16"), "at": (S, [128, 2, PIECE], "float32"),
+    "tu": (S, H3, "float32"), "th": (S, H3, "float16"),
     "of0": (S, [128, C], "uint16"), "of1": (S, [128, C], "uint16"), "pl0": (S, [128, C], "uint16"), "pl1": (S, [128, C], "uint16"),
-    "t0": (S, [128, C], "float32"), "ee": (S, H3, "bfloat16"),
-    "aa": (S, [128, 2, 128 * COPIES], "bfloat16"), "bb0": (S, [128, 8, 64], "bfloat16"), "bb1": (S, [128, 8, 64], "bfloat16"),
+    "on": (S, H3, "bfloat16"), "m0": (S, H3, "bfloat16"), "ee": (S, H3, "bfloat16"),
+    "aa": (S, [128, 2, 128 * COPIES], "bfloat16"), "bb": (S, [128, 64, 16], "bfloat16"),
+    "s32": (S, [128, 8, 48], "bfloat16"), "n80k": (S, [128, 128], "bfloat16"),
     "rr": (S, [128, C], "float16"), "rw": (S, [128, 4, 32], "float16"),
     "ef0": (S, [128, C], "float32"), "ev": (S, [128, 128], "float32"), "ef1": (S, [128, C], "float32"), "zero": (S, [128, C], "bfloat16"),
     "u0": (S, [128, 128], "bfloat16"), "u1": (S, [128, 128], "bfloat16"),
     "ul1": (S, [128, 128], "bfloat16"), "ul2": (S, [128, 128], "bfloat16"), "idx": (S, [128, 128], "uint16"),
-    "tnb": (S, [128, C], "bfloat16"), "sl": (S, [128, 2, C], "float32"), "seg": (S, [128, C], "float32"), "sc": (S, [128, 2, C], "float32"),
-    "vv": (S, [128, 16, 17], "float32"), "acc": (S, H3, "int32"), "cl": (S, [128, 2, 808], "float32"), "c0": (S, [128, C], "float32"),
-    "e2": (S, [128, 16], "float32"), "nw": (S, [128, 128], "int32"), "er": (S, [128, 128], "float32"), "v2": (S, [128, 16, 8], "float32"),
+    "tnb": (S, [128, C], "bfloat16"), "sl": (S, [128, 2, C], "bfloat16"), "seg": (S, [128, C], "float32"), "sc": (S, [128, 2, C], "float32"),
+    "cl": (S, [128, 8 * 43, 16], "float32"), "e2": (S, [128, 16], "float32"), "er": (S, [128, C], "float32"), "dx": (S, [128, 128], "float32"),
     "nt0": (S, [128, 16], "float32"), "nt1": (S, [128, 16], "float32"),
     "ntp": (S, [128, C], "bfloat16"), "d1": (S, [128, C], "float32"), "d2": (S, [128, C], "float32"),
-    "ya": (S, [128, 128], "float32"), "yb": (S, [128, 128], "float32"), "ys": (S, [128, C], "float32"), "yacc": (S, [128, C], "float32"),
-    "one": (S, [128, 128], "float32"), "tr1": (S, [128, 128], "float32"), "tri": (S, [128, 128], "float32"), "blf": (S, [128, 128], "float32"),
-    "e8": (S, [128, 128], "float32"), "trh": (S, [128, 128], "float16"), "e8h": (S, [128, 128], "float16"),
-    "idf": (S, [128, 128], "float32"), "idb": (S, [128, 128], "bfloat16"), "i32": (S, [128, 128], "bfloat16"), "h32": (S, [128, 128], "float16"),
-    "n32": (S, [128, 128], "bfloat16"), "i20": (S, [128, 128], "bfloat16"), "i16": (S, [128, 128], "float16"),
-    "idh": (S, [128, 128], "float16"), "ish": (S, [128, 128], "float16"), "idu": (S, [128, 128], "float16"), "isu": (S, [128, 128], "float16"),
-    "i2": (S, [128, 128], "bfloat16"), "r2": (S, [128, 128], "bfloat16"),
-    "back1": (S, [128, 128], "float32"), "back2": (S, [128, 128], "float32"), "idn": (S, [128, 128], "bfloat16"),
-    "blk": (S, [128, 128], "bfloat16"), "blr": (S, [128, 128], "bfloat16"), "b4k": (S, [128, 8], "bfloat16"), "b3": (S, [128, 8, 3], "bfloat16"),
-    "s3": (S, [128, 8, 48], "float16"), "c256": (S, [128, C], "bfloat16"), "sel": (S, [128, W], "bfloat16"),
+    "ya": (S, [128, C], "float32"), "yb": (S, [128, C], "float32"), "ys": (S, [128, C], "float32"), "yacc": (S, [128, 384], "float32"),
+    "one": (S, [128, 128], "bfloat16"), "tr1": (S, [128, 128], "bfloat16"), "tri": (S, [128, 128], "bfloat16"), "blf": (S, [128, 128], "bfloat16"),
+    "e8": (S, [128, 128], "bfloat16"), "idf": (S, [128, C], "float32"), "idb": (S, [128, C], "bfloat16"),
+    "n32": (S, [128, 128], "bfloat16"), "i24": (S, [128, 128], "bfloat16"), "blr": (S, [128, 128], "bfloat16"), "b4k": (S, [128, 8], "bfloat16"), "b3": (S, [128, 8, 3], "bfloat16"),
+    "s3": (S, [128, 8, 48], "bfloat16"), "c256": (S, [128, C], "bfloat16"), "sel": (S, [128, W], "bfloat16"),
     "cin": (S, [128, 384], "bfloat16"), "wc": (S, [128, 2], "bfloat16"),
-    "k3": (S, [128, 8], "int32"), "k4": (S, [128, 8], "int32"), "el": (S, [128, 8], "uint16"),
+    "k3": (S, [128, 8], "int32"), "el": (S, [128, 8], "uint16"),
 }
 for _b in range(8):
     SCRATCH["q%d" % _b] = (P, [128, 16, 32] if _b in TA else [128, 32, 16] if _b in TC else [128, 4, 128], "float32")
@@ -76,7 +79,9 @@ MASKS = {}
 ORDER = []
 CYC, PCYC, GATHER, VCALL, SCALL, WAKE, LOCAL, REMOTE, ISSUE, ROW, LRATE, RRATE = 0.83, 0.45, 1.4, 15, 65, 130, 2200, 3000, 700, 50, 38, 60
 ADDS = 1.5
-ROUNDS, PATIENCE, TRIALS, NOISE, SLOW, MOVES, SLACK = 3, 30, 20, 300, (0.8, 1.15), 8000, 20
+ROUNDS, PATIENCE, TRIALS, NOISE, MOVES, SLACK = 3, 30, 2, 300, 36000, 20
+SLOW, MIDDLE = ((0.8, 1.05, 1.25, 1), (1.3, 1.05, 1, 1.6), (0.85, 1.3, 1, 1.3), (1.35, 1.4, 1.2, 1)), (1.1, 1.2, 1.1, 1)
+STRETCH, ANEW = 150, 3
 SPAN = []
 
 
@@ -101,7 +106,7 @@ def pass_on(g, core, T, topo, rank, me):
 def build(g, core, T, topo, rank):
     ops = []
     nd = [0]
-    heard, added, copies = [], [], []
+    heard, added = [], []
     queue = {"pe": g.tensor, "act": g.scalar, "dve": g.vector, "gp": g, "sp": g.sync}
 
     def A(name, *ix):
@@ -213,6 +218,7 @@ def build(g, core, T, topo, rank):
         for n, k in enumerate(ks):
             sender = helpers(topo, T.cores, (rank + LONG[k][1]) % N)[LONG[k][3]]
             add(None, None, [A(LONG[k][2])], [], 2 * REMOTE + (n + 1) * 128 * A(src)[2] * A(src)[3] / RRATE, sem="a%d" % k, n=len(topo.engines(sender, core)), after=[i])
+            ops[-1]["from"] = "l%d" % ks[0]
         return i
 
     def send(k, dst, *srcs):
@@ -222,13 +228,13 @@ def build(g, core, T, topo, rank):
                                                              srcs=[a[0] for a in srcs], dsts=[dst[0]], alu_op=int(len(srcs) > 1))], local_sem=T.sem["l%d" % k])
         i = add("gp", call, [], srcs, 300, sem="l%d" % k, n=len(topo.engines(core, to)), extra="own", wake=REMOTE, move=moved(dst))
         add(None, None, [dst], [], REMOTE + 1000, sem="a%d" % k, n=len(topo.engines(T.cores[(rank + 1) % N], core)), after=[i])
+        ops[-1]["from"] = "l%d" % k
 
-    i = dma("sp", (A("ivi"), A("iv")))
-    j = dma("act", (A("taui", slice(0, 8)), A("tau")))
-    i = dma("sp", (A("di"), A("pf")), after=[i])
-    dma("act", (cols("x0", 0, 1024), cols("xs", 0, 1024)), after=[i, j])
-    i = dma("sp", (cols("x0", 1024, W), cols("xs", 1024, W)), after=[i])
-
+    dma("sp", (A("ivi"), A("iv")))
+    dma("act", (A("taui", slice(0, 8)), A("tau")))
+    dma("sp", (A("di"), A("pf")))
+    dma("act", (cols("x0", 0, 1024), cols("xs", 0, 1024)), (cols("x0", W, W + 16), cols("xs", 0, 16)))
+    dma("sp", (cols("x0", 1024, W), cols("xs", 1024, W)))
 
     def rotate(dst, at, src, a, s=16):
         dma("sp", (A(dst, slice(s, 128), slice(at, at + 128)), A(src, slice(0, 128 - s), slice(a, a + 128))),
@@ -239,90 +245,104 @@ def build(g, core, T, topo, rank):
         act(cols(dst, 0, s), cols(src, 128 - s, 128), Fn.Identity, scale=scale)
 
     rotate("dri", 0, "pf", 128)
-    for name, value in (("one", 1.0), ("s3", 0.0), ("c256", 256.0), ("kt", 1e9), ("rw", 0.0), ("zero", 0.0), ("seg", 1.0), ("cin", 0.0)):
+    for name, value in (("one", 1.0), ("s3", 0.0), ("c256", 256.0), ("rw", 0.0), ("zero", 0.0), ("seg", 1.0), ("cin", 0.0)):
         ms(A(name), value)
     ms(cols("seg", 0, C, 32), 0.0)
     ms(cols("cin", 1, C, 2), 4096.0)
-    ms(cols("cin", C, 384), -15.0 / 32)
-    for name in ("xu", "st0", "st1", "st2"):
-        ms(cols(name, W, W + 16), 0.0)
+    ms(cols("cin", C, 384), -15.0 / 64)
+    ms(cols("kt", 0, 1), 1e9)
+    ms(cols("kt", C + 1, C + 8), 1e9)
+    ms(cols("xu", W, W + 16), 0.0)
     ms(cols("zt", W, W + 8), 0.0)
-    ms(A("vv", ALL, ALL, slice(16, 17)), 0.0)
+    ms(cols("wv", W, W + 8), 1e9)
     sel(A("tr1"), A("one"), [[-16, 8], [0, 16]], Op.is_ge, 0, 1)
     sel(A("tri"), A("tr1"), [[1, 128]], Op.is_ge, 0, -1)
     sel(A("e8"), A("one"), [[-1, 8], [0, 16]], Op.is_equal, 0, 1)
-    sel(A("idf"), A("one"), [[-1, 128]], Op.is_equal, 0, 1)
+    ident, identf = half("idb", 0), half("idf", 0)
+    sel(ident, A("one"), [[-1, 128]], Op.is_equal, 0, 1)
     sel(A("blf"), A("tr1"), [[16, 8], [0, 16]], Op.is_ge, 15, -1)
     gains = dma("gp", (A("g0"), A("gn")), after=[len(ops) - 1])
     iota(A("wc"), [[0, 2]], 128, 1, True)
-    iota(A("k3"), [[2, 8]], 0, 0, False)
-    iota(A("k4"), [[0, 8]], 0, 1, False)
-    cp(A("trh"), A("tri"))
-    cp(A("e8h"), A("e8"))
-    cp(A("s3", ALL, ALL, slice(16, 32)), A("idf"))
-    for same, on, scale in (("idh", "ish", 0.25), ("idu", "isu", 1537.0 / 4096)):
-        ts(A(same), A("idf"), scale, Op.mult)
-        cp(cols(on, 2, 128), cols(same, 0, 126))
-        cp(cols(on, 0, 2), cols(same, 126, 128))
-    ts(A("k4"), A("k4"), 8, Op.bitwise_and, 3, Op.logical_shift_right)
-    tt(A("k3"), A("k3"), A("k4"), Op.add)
+    iota(A("k3"), [[1, 8]], 0, 0, False)
+    cp(A("s3", ALL, ALL, slice(16, 32)), ident)
+    cp(half("idb", 1), ident)
     cp(A("el"), A("k3"))
-    ts(A("h32"), A("idf"), -32.0, Op.mult)
-    cp(A("i16"), A("idf"))
-    for name, scale in (("i32", 32.0), ("n32", -32.0), ("i20", 20.0), ("idb", 1.0), ("idn", -1.0 / 256), ("i2", 2.0)):
-        act(A(name), A("idf"), Fn.Identity, scale=scale)
+    ts(A("s32"), A("s3"), 32.0, Op.mult)
+    for name, scale in (("n32", -32.0), ("i24", 24.0), ("n80k", -20 * 4096.0)):
+        ts(A(name), ident, scale, Op.mult)
+    for h in range(2):
+        act(half("idf", h), ident, Fn.Identity)
     act(A("b4k"), cols("blf", 0, 128, 16), Fn.Identity, scale=4096.0)
-    act(A("blk"), A("blf"), Fn.Identity, scale=1.0 / 16)
-    shifted("r2", "idf", 16, 2.0)
-    shifted("blr", "blf", 16, 1.0 / 16)
-    shifted("back1", "idf", 112, 1.0)
-    shifted("back2", "idf", 96, 1.0)
+    shifted("blr", "blf", 16, 1.0 / 32)
     for j, w in enumerate((-512.0, 32.0, 8192.0)):
         act(A("b3", ALL, ALL, j), cols("blf", 0, 128, 16), Fn.Identity, scale=w)
 
     def first_times(h):
         starts = A("tauh", slice(0, 8), slice(128 * h, 128 * h + 128))
         cp(half("ivh", h), half("ivi", h))
-        mm(q(TC[h], C, 384), half("ivh", h), A("trh"), True, False)
-        mm(q(TC[h], C, 384), starts, A("e8h", slice(0, 8)), False, True)
-        cp(half("tu", h), q(TC[h], C, 384))
-        ts(half("ti", h), half("tu", h), W - 1, Op.bitwise_and)
-        mm(q(4, 8 * h, 8 * h + 8), starts, A("e8h", slice(0, 8), slice(0, 128, 16)))
+        mm(q(TC[h], C, 384), half("ivh", h), A("tri"), True, False)
+        mm(q(TC[h], C, 384), starts, A("e8", slice(0, 8)), False, True)
+        wrap(h, False, TC[h], 16, 0, 16)
+        offsets(h, 0, 16)
+        mm(q(4, 8 * h, 8 * h + 8), starts, A("e8", slice(0, 8), slice(0, 128, 16)))
 
-    def to_list(src, h, at, alone=True, last=True):
+    def wrap(h, on, bank, row, k0, k1):
+        rows, ks = slice(8 * h, 8 * h + 8), slice(k0, k1)
+        ts(A("tu", ALL, rows, ks), q3(bank, row, row + 8, k0, k1), M2K, Op.add, -M2K, Op.add)
+        if on:
+            tt(A("th", ALL, slice(9, 16), ks), q3(bank, row, row + 7, k0, k1), A("tu", ALL, slice(8, 15), ks), Op.subtract)
+            tt(A("th", ALL, 8, ks), q3(bank, row + 7, row + 8, k0, k1), A("tu", ALL, 15, ks), Op.subtract)
+        else:
+            tt(A("th", ALL, rows, ks), q3(bank, row, row + 8, k0, k1), A("tu", ALL, rows, ks), Op.subtract)
+
+    def offsets(h, k0, k1):
+        to_list(TC[h], 8 * k0, 8 * k1, "s3", lambda grp: A("th", ALL, 8 * h + grp, slice(k0, k1)), True, True)
+        a, b = 128 * h + 8 * k0, 128 * h + 8 * k1
+        ts(cols("of0", a, b), q(TC[h], 8 * k0, 8 * k1), OFF, Op.add)
+        ts(cols("of1", a, b), cols("of0", a, b), 1.0, Op.add)
+
+    def to_list(bank, a, b, pick, group, alone, last):
         for m in range(8):
             for gp in range(4):
                 for e in range(2):
-                    mm(q(TC[h], at + m, at + 128, 8, slice(32 * gp, 32 * gp + 32)), A("s3", ALL, m, slice(16 - 16 * e, 48 - 16 * e)), A(src, ALL, 8 * h + 2 * gp + e),
-                       alone and e == 0, e == 1 if alone else last and (m, e) == (7, 1), (m % 2, gp, e) != (0, 0, 0))
+                    mm(q(bank, a + m, b, 8, slice(32 * gp, 32 * gp + 32)), A(pick, ALL, m, slice(16 - 16 * e, 48 - 16 * e)), group(2 * gp + e),
+                       alone and e == 0, e == 1 and (alone or last and m == 7), (m % 2, gp, e) != (0, 0, 0))
 
-    def centres(h):
-        ts(half("hi", h), half("df", h), 1.0 / 32, Op.mult, 1024 + 4.015625, Op.add)
-        ts(half("mb", h), half("hi", h), 7.0, Op.mult, -7.0 * (1024 + 9) - MID, Op.add)
+    def claimed(last):
+        if last:
+            to_list(TC[0], 128, 384, "s3", lambda grp: A("bb", ALL, slice(grp, 64, 32)), False, True)
+        else:
+            mm(q(TC[0], 128, 384), ident, A("zero"), True, False)
+            to_list(TC[0], 128, 384, "s32", lambda grp: A("aa", ALL, ALL, slice(16 * grp, 16 * grp + 16)), False, False)
+
+    def centres(t, h, src):
+        ts(half("hi", h), half(src, h), 1.0 / (16 if t else 32), Op.mult, 1024 + 4.015625, Op.add)
+        ts(half("mb", h), half("hi", h), -7.0, Op.mult, 7.0 * (1024 + 9) + MID, Op.add)
         o = q(TB[h], C, 384)
-        mm(o, A("idf"), half("df", h), True, False)
-        mm(o, A("h32"), half("hi", h), False, False, True)
-        mm(o, A("i32"), half("mb", h), False, True)
-        act(A("at", ALL, h, slice(0, 128)), o, Fn.Identity, bias=BIGH - 36.5 - 1024, scale=-1.0 / 32)
-        n = 128
-        while n < PIECE:
-            if n >= BY_DMA:
-                dma("sp", (A("at", ALL, h, slice(n, 2 * n)), A("at", ALL, h, slice(0, n))))
+        mm(o, identf, half("df", h), True, False)
+        mm(o, A("n32"), half("hi", h), False, False, True)
+        mm(o, A("n32"), half("mb", h), False, True)
+        for n in (0, 128) if DOUBLE[t > 0][h][0] == "act" else (0,):
+            act(A("at", ALL, h, slice(n, n + 128)), o, Fn.Identity, bias=BIGH - 36.5 - 1024 + M1 / 32, scale=-1.0 / 32)
+        for n, by in zip((128, 256, 512), DOUBLE[t > 0][h]):
+            o, a = A("at", ALL, h, slice(n, 2 * n)), A("at", ALL, h, slice(0, n))
+            if by == "act":
+                continue
+            elif by == "dve":
+                cp(o, a)
+            elif by == "sp":
+                dma("sp", (o, a))
             else:
-                copies.append(sel(A("at", ALL, h, slice(n, 2 * n)), A("at", ALL, h, slice(0, n)), [[0, n]], Op.is_ge, 0, 0))
-            n *= 2
+                sel(o, a, [[0, n]], Op.is_ge, 0, 0)
 
     def times(h):
-        cp(half("th", h), half("ti", h))
-        to_list("th", h, 0)
-        cp(half("of0", h), q(TC[h], 0, 128))
-        ts(half("of1", h), half("of0", h), 1.0, Op.add)
-        mm(q3(TA[h], 8, 16, 16, 32), A("i16"), half("th", h))
-        ts(A("aa", ALL, h, slice(0, 128)), half("th", h), 1.0 / 32, Op.mult, 160 - 15.5 / 32, Op.add)
+        ts(A("aa", ALL, h, slice(0, 128)), half("th", h), 1.0 / 32, Op.mult, 160 + (OFF - 15.5) / 32, Op.add)
         o = q3(TA[h], 0, 8, 16, 32)
-        mm(o, A("i16"), half("th", h), True, False)
+        mm(o, ident, half("th", h), True, False)
         mm(o, A("n32"), A("aa", ALL, h, slice(0, 128)), False, False, True)
-        mm(o, A("i20"), half("c256", 0), False, True, True)
+        mm(o, A("i24"), half("c256", 0), False, True, True)
+        if h:
+            claimed(False)
         n = 1
         while n < COPIES:
             ts(A("aa", ALL, h, slice(128 * n, 256 * n)), A("aa", ALL, h, slice(0, 128 * n)), -float(n), Op.add)
@@ -330,67 +350,69 @@ def build(g, core, T, topo, rank):
         for a in range(0, 64, n):
             ts(A("oa", ALL, h, slice(128 * a, 128 * (a + n))), A("aa", ALL, h), 160.0 + a, Op.is_equal, cols("wc", 0, 1), Op.mult)
 
-    def hear(t, h):
-        tab = A("st%d" % t)
-        for j in range(4096 // PIECE):
-            w, a = j * PIECE // 2048, 2048 * h + j * PIECE % 2048
-            o, src = cols("ind%d" % w, a, a + PIECE), IND(tab, cols("of%d" % w, a // 16, (a + PIECE) // 16))
-            if (h, j) in FUSED[t]:
-                tt(o, src, A("at", ALL, h), Op.add)
-            else:
-                heard.append(act(o, src, Fn.Identity))
-                added.append(dma_add(o, A("at", ALL, h), first))
-            ts(o, o, BIGH, Op.not_equal)
-            for b in range(a, a + PIECE, 128):
-                mm(A("q%d" % TA[h], ALL, slice(8 * w, 8 * w + 8), b // 128 % 16), cols("ind%d" % w, b, b + 128), A("b4k"), True, True, b > a)
-            if (j + 1) * PIECE == 2048:
-                act(half("t0", h), q3(TA[h], 0, 8, 0, 16), Fn.Relu, bias=-5 * 4096.0)
+    def hear(t, h, w, k0, k1):
+        a, n = 2048 * h + 128 * k0, 128 * (k1 - k0)
+        o, src = cols("ind%d" % w, a, a + n), IND(A("x%d" % t), cols("of%d" % w, a // 16, (a + n) // 16))
+        heard.append(act(o, src, Fn.Identity, scale=7.0, bias=-MID, after=heard[-1:]))
+        added.append(dma_add(o, A("at", ALL, h, slice(0, n))))
+        ts(o, o, BIGH, Op.not_equal)
 
-    def claims(t, h):
-        c1, bb = q3(TA[h], 8, 16, 0, 16), "bb%d" % h
-        ts(c1, c1, -5 * 4096.0, Op.add, 1.0, Op.max)
-        tt(half("ee", h), c1, half("t0", h), Op.min)
-        tt(A(bb, ALL, slice(0, 2)), q3(TA[h], 0, 8, 16, 32), half("ee", h), Op.add)
-        ts(A(bb, ALL, slice(2, 4)), A(bb, ALL, slice(0, 2)), -16.0, Op.add)
-        ts(A(bb, ALL, slice(4, 8)), A(bb, ALL, slice(0, 4)), -1.0, Op.add)
-        tt(half("ph", h), q3(TA[h], 8, 16, 16, 32), half("ee", h), Op.add)
-        to_list("ph", h, 128)
-        ts(half("pl%d" % (t % 2), h), q(TC[h], 128, C), float(NONE), Op.min)
+    def count(h, w, k0, k1):
+        for k in range(k0, k1):
+            mm(q3(TA[h], 8 * w, 8 * w + 8, k, k + 1), cols("ind%d" % w, 2048 * h + 128 * k, 2048 * h + 128 * k + 128), A("b4k"), not w, not w or k + 1 in ROWS[h], k > k0)
 
-    def histogram(h):
-        ob, bb = "ob%d" % h, "bb%d" % h
-        ts(A(ob, ALL, slice(64, 66)), A(bb, ALL, slice(0, 2)), 32.0, Op.is_equal, HALF[h], Op.mult)
+    def on_time(t, h):
+        ts(half("on", h), q3(TA[h], 0, 8, 0, 16), 5 * 4096.0, Op.is_le, 0.25, Op.add)
+        tt(half("m0", h), q3(TA[h], 0, 8, 16, 32), half("on", h), Op.subtract)
+        if t < VI - 1:
+            act(half("ee", h), half("on", h), Fn.Identity, scale=-1.0, bias=1.25)
+
+    def below(h, k0, k1):
+        o, rows, ks = q3(TA[h], 8, 16, k0, k1), slice(8 * h, 8 * h + 8), slice(k0, k1)
+        mm(o, ident, A("m0", ALL, rows, ks), True, False)
+        mm(o, A("n80k"), A("on", ALL, rows, ks), False, False, True)
+
+    def copies(h, a, b, ks):
+        return A("bb", ALL, slice(32 * h + a, 32 * h + b), ks)
+
+    def claims(h, k0, k1):
+        ks = slice(k0, k1)
+        tt(copies(h, 0, 8, ks), q3(TA[h], 8, 16, k0, k1), A("m0", ALL, slice(8 * h, 8 * h + 8), ks), Op.max)
+        ts(copies(h, 8, 16, ks), copies(h, 0, 8, ks), -16.0, Op.add)
+        ts(copies(h, 16, 32, ks), copies(h, 0, 16, ks), -1.0, Op.add)
+
+    def histogram(h, k0, k1):
+        ob, ks, done = "ob%d" % h, slice(k0, k1), h == 1 and k1 == 16
+        ts(A(ob, ALL, slice(256, 264), ks), copies(h, 0, 8, ks), 31.25, Op.is_equal, HALF[h], Op.mult)
+        for i in range(8):
+            ts(A(ob, ALL, slice(32 * i, 32 * i + 32), ks), copies(h, 0, 32, ks), 2.0 * i - 0.75, Op.is_equal, HALF[h], Op.mult)
         for a, b, bank in PIECES:
-            if h == 0:
-                mm(q3(bank, 0, (b - a) // 16, 0, 66), A("idb"), cols("zero", 0, 66 * (b - a) // 16), True, False)
-        for a, b, bank in PIECES:
-            c, d = (a, b) if h else (a // 32 * 32, a // 32 * 32 + 32)
-            for i in range(8 if a == c else 0):
-                ts(A(ob, ALL, slice(8 * i, 8 * i + 8), slice(c, d)), A(bb, ALL, ALL, slice(c, d)), 2.0 * i, Op.is_equal, HALF[h], Op.mult)
-            for o in range(a, b):
-                at = 128 * ((o - a) // 16)
-                mm(q(bank, at, at + 66), A("oa", ALL, h, slice(o, 8192, 64)), A(ob, ALL, ALL, o), False, h == 1 and o == b - 1, o % 8 > 0)
-            if h:
-                ts(cols("rr", 4 * a, 4 * b), q3(bank, 0, (b - a) // 16, 0, 64), 4096.0, Op.min)
-                ts(A("rw", ALL, slice(a // 16, b // 16), slice(0, 2)), q3(bank, 0, (b - a) // 16, 64, 66), 4096.0, Op.min)
+            if h == k0 == 0:
+                mm(q3(bank, 0, b - a, 0, 66), ident, cols("zero", 0, 66 * (b - a)), True, False)
+            for pair in range(a, b):
+                for k in range(k0, k1):
+                    mm(q3(bank, pair - a, pair - a + 1, 0, 66), A("oa", ALL, h, slice(16 * pair + k, 8192, 64)), A(ob, ALL, slice(pair, 264, 4), k), False,
+                       done and (pair, k) == (b - 1, 15), k > k0)
+            if done:
+                ts(cols("rr", 64 * a, 64 * b), q3(bank, 0, b - a, 0, 64), -127.75, Op.add, 1024.0, Op.min)
+                ts(A("rw", ALL, slice(a, b), slice(0, 2)), q3(bank, 0, b - a, 64, 66), 1024.0, Op.min)
 
     def owners(t):
-        for at, same, on in [(0, "idu", "isu"), (128, "idh", "ish")][t == VI - 1:]:
-            for g2 in range(2):
-                for b4 in (1, 0):
-                    o = q(7, at + b4, at + 128, 2, slice(64 * g2, 64 * g2 + 64))
-                    mm(o, cols("rr", 2 * b4 + g2, C, 4), cols(same, g2, 128, 2), True, b4 == 1, (g2, b4) != (0, 1))
-                    if b4 == 0:
-                        mm(o, cols("rw", g2, 128, 2), cols(on, g2, 128, 2), False, True, True)
-            if at == 0:
-                ts(A("u%d" % t), q(7, 0, 128), M512, Op.add, M512 + 512, Op.is_equal)
-        ts(A("idx"), q(7, 128, C), -0.2, Op.add, 700.0, Op.min)
+        for g2 in range(2):
+            for b4 in (1, 0):
+                o = q(7, b4, 128, 2, slice(64 * g2, 64 * g2 + 64))
+                mm(o, cols("rr", 2 * b4 + g2, C, 4), cols("idb", g2, 128, 2), True, b4 == 1, (g2, b4) != (0, 1))
+                if b4 == 0:
+                    mm(o, cols("rw", g2, 128, 2), cols("idb", 126 + g2, 254, 2), False, True, True)
+        if t < VI - 1:
+            ts(A("u%d" % t), q(7, 0, 128), M256, Op.add, M256 + 256, Op.is_equal)
+        ts(A("idx"), q(7, 0, 128), -127.45, Op.add, C + 1.0, Op.min)
         for h in range(2):
-            act(cols("kt", C + h, 2 * C, 2), half("df", h), Fn.Identity, scale=1.0 / 32)
+            act(cols("kt", 1 + h, C + 1, 2), half("df", h), Fn.Identity, scale=1.0 / 32, bias=-M1 / 32)
 
-    def spread(u, j, bank, x=None, sign="idb"):
+    def spread(u, j, bank, x=None):
         if x:
-            mm(q(bank), A(sign), cols(x, j, W, 4), True, False)
+            mm(q(bank), ident, cols(x, j, W, 4), True, False)
         for i in range(4):
             mm(q(bank, i, 512, 4), cols("sel", 128 * (4 * i + j), 128 * (4 * i + j) + 128), A(u), not x, i == 3 or not x, i > 0)
 
@@ -398,11 +420,11 @@ def build(g, core, T, topo, rank):
         parts = [(a, a + 1024) for a in range(0, W, 1024)]
         for a, b in parts:
             i = act(cols("lg0", a, b), cols("g0", a, b), Fn.Ln, load=1300 * (a == 0), after=heard[-1:])
-        act(A("ef0"), A("df"), Fn.Exp, scale=1.0 / 256, load=1500, after=range(i - 1, i + 1))
+        act(A("ef0"), A("df"), Fn.Exp, scale=1.0 / 256, bias=-M1 / 256, load=1500, after=range(i - 1, i + 1))
         for a, b in parts:
             act(cols("lg0", a, b), cols("lg0", a, b), Fn.Identity, scale=-4.0)
-            act(cols("st2", a, b), cols("x0", a, b), Fn.Identity, scale=-0.5, after=heard[-1:])
-        dma_add(A("lg0"), cols("st2", 0, W))
+            act(cols("ind0", a, b), cols("x0", a, b), Fn.Identity, scale=-0.5, after=heard[-1:])
+        dma_add(A("lg0"), cols("ind0", 0, W))
         hand_over("lg0")
 
     def terms(t, a, b):
@@ -411,33 +433,35 @@ def build(g, core, T, topo, rank):
             dma_add(cols("wv", b - 1024, b), cols("lg%d" % t, b - 1024, b))
 
     def gather_terms(t, h, a, b, to):
-        act(A("zg", ALL, to, slice(128 * a, 128 * b)), IND(A("zt"), cols("pl%d" % (t % 2), 128 * h + 8 * a, 128 * h + 8 * b)), Fn.Identity, after=heard[-1:])
+        o, rows = A("zg%d" % (t % 2), ALL, to, slice(128 * a, 128 * b)), cols("pl%d" % (t % 2), 128 * h + 8 * a, 128 * h + 8 * b)
+        if t < VI - 1:
+            act(o, IND(A("wv"), rows), Fn.Exp, scale=-0.25, after=heard[-1:])
+        else:
+            act(o, IND(A("zt"), rows), Fn.Identity)
 
     def home(t, h):
-        return A("back%d" % t if h and t else "idf")
+        return cols("idf", 16 * t * h, 16 * t * h + 128)
 
     def sum_terms(t):
-        for b in (1024, W):
-            act(cols("zt", b - 1024, b), cols("wv", b - 1024, b), Fn.Exp, scale=-0.25, after=heard[-HOLD:][:1])
-        act(cols("zt", W, W + 1), cols("zt", 0, 1), Fn.Identity)
+        act(cols("wv", W, W + 1), cols("wv", 0, 1), Fn.Identity)
         for h in range(2):
             for a in (8, 0):
                 gather_terms(t, h, a, a + 8, h)
             n = 2048
             for _ in range(LEVELS[t][h]):
                 n //= 2
-                dma_add(A("zg", ALL, h, slice(0, n)), A("zg", ALL, h, slice(n, 2 * n)))
+                dma_add(A("zg%d" % t, ALL, h, slice(0, n)), A("zg%d" % t, ALL, h, slice(n, 2 * n)))
 
     def add_terms(t, bank):
         for h in range(2):
             n = 16 >> LEVELS[t][h]
             for k in range(n):
-                mm(q(bank, 128 * h, 128 * h + 128), home(t, h), A("zg", ALL, h, slice(128 * k, 128 * k + 128)), k == 0, k == n - 1)
+                mm(q(bank, 128 * h, 128 * h + 128), home(t, h), A("zg%d" % t, ALL, h, slice(128 * k, 128 * k + 128)), k == 0, k == n - 1)
         if t == 0:
-            tt(A("yacc"), q(bank, 0, C), A("ef0"), Op.mult)
+            tt(cols("yacc", 128, 384), q(bank, 0, C), A("ef0"), Op.mult)
         else:
-            tt(q(bank, 0, C), q(bank, 0, C), A("ef1"), Op.mult)
-            tt(A("yacc"), q(bank, 0, C), A("yacc"), Op.add)
+            tt(cols("yacc", 0, 128), q(bank, 0, 128), half("ef1", 0), Op.mult)
+            tt(half("yb", 0), q(bank, 128, C), half("ef1", 1), Op.mult)
 
     def taken_columns(t):
         x = "x%d" % t
@@ -450,83 +474,89 @@ def build(g, core, T, topo, rank):
         cp(cols("xu", W, W + 1), cols("xu", 0, 1))
 
     def taken(t, h):
-        mm(q(TA[h], 0, C), A("idb"), cols("cin", 0, C), True, False)
-        mm(q(TB[h], 384, 512), A("idb"), cols("cin", C, 384), True, False)
-        for kq in range(4):
-            a = 2048 * h + 512 * kq
-            o, src = cols("xg", a, a + 512), IND(A("xu"), cols("pl%d" % (t % 2), a // 16, a // 16 + 32))
+        mm(q(TA[h], 0, C), ident, cols("cin", 0, C), True, False)
+        mm(q(TB[h], 384, 512), ident, cols("cin", C, 384), True, False)
+        for kq, (k0, k1) in enumerate(zip(XG, XG[1:])):
+            a, b = 2048 * h + 128 * k0, 2048 * h + 128 * k1
+            o, src = cols("xg", a, b), IND(A("xu"), cols("pl%d" % (t % 2), a // 16, b // 16))
             if (h, kq) in XG_DVE:
                 cp(o, src)
             else:
                 act(o, src, Fn.Identity)
-            for k in range(4 * kq, 4 * kq + 4):
+            for k in range(k0, k1):
                 a, s = 2048 * h + 128 * k, int(k == 0)
-                mm(q3(TA[h], 0, 8, 2 * k - 1 + s, 2 * k + 2), cols("xg", a, a + 128), A("b3", ALL, ALL, slice(s, 3)), False, k == 15, k % 4 > 0)
-            for k in range(4 * kq, 4 * kq + 4):
+                mm(q3(TA[h], 0, 8, 2 * k - 1 + s, 2 * k + 2), cols("xg", a, a + 128), A("b3", ALL, ALL, slice(s, 3)), False, k == 15, k > k0)
+            for k in range(k0, k1):
                 a = 2048 * h + 128 * k
-                mm(q(TB[h], 384, 512), A("r2" if h else "i2"), cols("xg", a, a + 128), False, k == 15, k % 4 > 0)
+                mm(q(TB[h], 384, 512), cols("idb", 112 * h, 112 * h + 128), cols("xg", a, a + 128), False, k == 15, k > k0)
 
     def next_table(t):
         for j in range(4):
             bank = (4, 7)[j % 2]
-            spread("ul%d" % t, j, bank, "x%d" % t, "idn")
-            act(cols("st%d" % t, j, W, 4), q(bank), Fn.Identity, scale=-7 * 256.0, bias=-MID)
-        act(cols("st%d" % t, W, W + 1), cols("st%d" % t, 0, 1), Fn.Identity)
+            spread("ul%d" % t, j, bank, "x%d" % t)
+            act(cols("x%d" % t, j, W, 4), q(bank), Fn.Identity)
+        act(cols("x%d" % t, W, W + 1), cols("x%d" % t, 0, 1), Fn.Identity)
 
     def profiles(t, h):
-        act(half("tnb", h), q3(TA[h], 0, 8, 0, 32, 2), Fn.Relu, bias=1.0, scale=-1.0)
-        mm(q(TB[h], 0, 128), half("tnb", h), A("idb"))
+        if h in TNB_DVE:
+            ts(half("tnb", h), q3(TA[h], 0, 8, 0, 32, 2), 0.0, Op.is_equal)
+        else:
+            act(half("tnb", h), q3(TA[h], 0, 8, 0, 32, 2), Fn.Relu, bias=1.0, scale=-1.0)
+        mm(q(TB[h], 0, 128), half("tnb", h), ident)
         act(half("ntp", h), q(TB[h], 0, 128), Fn.Identity)
-        mm(q(TB[h], 128, C), A("blr" if h else "blk"), half("ntp", h))
-        tt(half("d1", h), q(TB[h], 128, C), A("drf" if t else "dri") if h else half("df", 0), Op.mult)
+        mm(q(TB[h], 128, C), A("blr" if h else "blf"), half("ntp", h))
+        tt(half("d1", h), q(TB[h], 128, C), A("drf" if t else "dri") if h else cols("kt", 1, C + 1, 2), Op.mult)
         tt(half("d2", h), q(TB[h], 384, 512), half("d1", h), Op.add)
-        ts(half("df", h), half("d2", h), M1, Op.add, -M1, Op.add)
-        centres(h)
+        act(half("df", h), half("d2", h), Fn.Identity, bias=M1, scale=2.0)
+        centres(t + 1, h, "d2")
         if t == 0 and h:
-            rotate("drf", 0, "df", 128)
+            act(A("dx"), half("df", 1), Fn.Identity, bias=-M1)
+            rotate("drf", 0, "dx", 0)
 
     def tapes(t, h):
         sx, lx = q3(TA[h], 0, 8, 0, 32, 2), q3(TA[h], 0, 8, 1, 32, 2)
-        rows, bank = slice(8 * h, 8 * h + 8), TC[h]
+        rows = slice(8 * h, 8 * h + 8)
+        leave, moved_by = A("sl", ALL, h, slice(1, C, 2)), A("sc", ALL, h, slice(0, C, 2))
         tt(A("sl", ALL, h, slice(0, C, 2)), sx, half("ee", h), Op.min)
-        ts(A("sl", ALL, h, slice(1, C, 2)), lx, 0.0, Op.is_lt, B, Op.mult)
-        tt(q(bank, 0, 128), lx, half("th", h), Op.min)
+        ts(leave, lx, 0.0, Op.is_lt, B, Op.mult)
         profiles(t, h)
         o, d, seg = A("sc", ALL, h), A("sl", ALL, h), A("seg")
-        add("dve", lambda: g.vector.tensor_tensor_scan(o[0], seg[0], d[0], 0.0, Op.mult, Op.add), [o], [d, seg], vtime(o, d))
-        vv = A("vv", ALL, rows, slice(0, 16))
-        tt(vv, q(bank, 0, 128), A("sc", ALL, h, slice(0, C, 2)), Op.add)
-        at = [0]
-
-        def moves(src, spans, row):
-            for j, (d, a, b, n) in enumerate(spans):
-                o = A("cl", ALL, h, slice(at[0], at[0] + 8 * n))
-                at[0] += 8 * n
-                ts(o, A(src, ALL, rows, slice(a, a + n)), d * B, Op.max, (d + 1) * B, Op.min)
-                mm(q3(bank, row, row + 8, b, b + n), A("idf"), o, j == 0, j == len(spans) - 1)
-
-        moves("vv", [(1, 1, 0, 16)] + [(d, 2 * d - 1, d - 1, 17 - 2 * d) for d in range(2, 9)], 16)
-        ts(half("c0", h), vv, 0.0, Op.max, B, Op.min)
-        tt(A("e2", ALL, rows), A("vv", ALL, rows, 15), A("nt%d" % t, ALL, rows), Op.add)
-        tt(half("acc", h), q(bank, C, 384), half("c0", h), Op.add)
-        nw = cols("nw", 64 * h, 64 * h + 64)
-        ts(nw, A("acc", ALL, rows, slice(0, 8)), W - 1, Op.bitwise_and)
-        er = cols("er", 64 * h, 64 * h + 64)
-        act(er, IND(A("e2", ALL, rows), cols("el", 0, 4)), Fn.Identity)
-        tt(A("v2", ALL, rows), nw, er, Op.add)
-        moves("v2", [(e, 0, 16 - e, e) for e in range(8, 0, -1)], 24)
-        late = A("acc", ALL, rows, slice(8, 16))
-        tt(late, q3(bank, 24, 32, 8, 16), late, Op.add)
-        if h:
-            ts(A("ti", ALL, slice(9, 16)), A("acc", ALL, slice(8, 15)), W - 1, Op.bitwise_and)
-            ts(A("ti", ALL, 8), A("acc", ALL, 15), W - 1, Op.bitwise_and)
+        add("dve", lambda: g.vector.tensor_tensor_scan(o[0], seg[0], d[0], 0.0, Op.mult, Op.add), [o], [d, seg], vtime(o, seg))
+        vv = q3(TA[h], 8, 16, 0, 16)
+        mm(vv, ident, half("th", h), True, False)
+        mm(vv, A("n32"), leave, False, not VV_PE, True)
+        if VV_PE:
+            mm(vv, identf, moved_by, False, True)
         else:
-            ts(half("ti", 0), half("acc", 0), W - 1, Op.bitwise_and)
+            tt(vv, vv, moved_by, Op.add)
+        at = 8 * 26 * h
+        for k0, k1 in NEW[h]:
+            bank, row = (TC[h], 16) if k0 == 0 else (TC[1 - h], 24)
+            for s in range(k1 + 1):
+                i = max(k0, s - 1)
+                if s == 1 and k1 == 16:
+                    tt(A("e2", ALL, rows), q3(TA[h], 8, 16, 15, 16), A("nt%d" % t, ALL, rows), Op.add)
+                    if h in ER_DVE:
+                        cp(half("er", h), IND(A("e2", ALL, rows), A("el")))
+                    else:
+                        act(half("er", h), IND(A("e2", ALL, rows), A("el")), Fn.Identity)
+                    tt(q3(TA[h], 8, 16, 16, 32), vv, half("er", h), Op.add)
+                if s not in JOIN[h]:
+                    at, i0, s0 = at + 8, i, s
+                c = A("cl", ALL, slice(at - 8, at), slice(i, k1))
+                to = q3(TA[h], 0, 8, 16 * (s // 2 % 2) + i, 16 * (s // 2 % 2) + k1) if s in JOIN[h] else c
+                ts(to, q3(TA[h], 8, 16, i + s, k1 + s), (s - 0.5) * B, Op.max, (s + 0.5) * B, Op.min)
+                if s in JOIN[h]:
+                    tt(c, to, c, Op.add)
+                if s + 1 not in JOIN[h] or s == k1:
+                    mm(q3(bank, row, row + 8, i0, k1), identf, A("cl", ALL, slice(at - 8, at), slice(i0, k1)), s0 == 0, s == k1)
+            wrap(h, h == 1, bank, row, k0, k1)
+            offsets(h, k0, k1)
 
     def last_terms(t):
         for c in range(len(LAST) - 1):
             a, b = LAST[c], LAST[c + 1]
-            o = cols("wv", a, b)
+            o = cols("zt", a, b)
             tt(o, IND(A("kt"), cols("idx", a // 16, b // 16)), cols("x%d" % t, a, b), Op.subtract)
             act(o, o, Fn.Abs)
             act(q(c % 4, 0, b - a), o, Fn.Exp, scale=-1.0 / 8)
@@ -535,46 +565,55 @@ def build(g, core, T, topo, rank):
                 act(cols("zt", W, W + 1), cols("zt", 0, 1), Fn.Identity)
         for a, b in ((0, 1), (1, 3), (3, 7), (7, TAIL)):
             gather_terms(t, 1, a, b, 0)
-        o = A("zg", ALL, 0, slice(128 * TAIL, 128 * TAIL + 128))
+        o = A("zg0", ALL, 0, slice(128 * TAIL, 128 * TAIL + 128))
         for k in range(TAIL, 16):
             src = IND(A("zt"), cols("pl%d" % (t % 2), 128 + 8 * k, 128 + 8 * k + 8))
             if k == TAIL:
                 cp(o, src)
             else:
                 tt(o, src, o, Op.add)
+        mm(q(5, 0, 128), identf, half("yb", 0), True, False)
         for k in range(min(16, TAIL + 1)):
-            mm(q(5, 0, 128), home(t, 1), A("zg", ALL, 0, slice(128 * k, 128 * k + 128)), k == 0, k == min(15, TAIL))
-        for k in range(16):
-            src, o = IND(A("zt"), cols("pl%d" % (t % 2), 8 * k, 8 * k + 8)), A("yb" if k % 2 else "ya")
-            if k == 1:
-                cp(o, src)
-            else:
-                tt(o, src, cols("yacc", 0, 128) if k == 0 else o, Op.add)
-        tt(cols("ys", 0, 128), A("ya"), A("yb"), Op.add)
+            mm(q(5, 0, 128), home(t, 1), A("zg0", ALL, 0, slice(128 * k, 128 * k + 128)), False, k == min(15, TAIL))
+        for k in range(8):
+            src = IND(A("zt"), cols("pl%d" % (t % 2), 16 * k, 16 * k + 16))
+            tt(A("ya"), src, cols("yacc", 0, C) if k == 0 else A("ya"), Op.add)
+        tt(cols("ys", 0, 128), half("ya", 0), half("ya", 1), Op.add)
         dma("sp", (cols("y", 0, 128), cols("ys", 0, 128)))
-        tt(cols("ys", 128, C), q(5, 0, 128), cols("yacc", 128, C), Op.add)
+        tt(cols("ys", 128, C), q(5, 0, 128), cols("yacc", C, 384), Op.add)
         dma("act", (cols("y", 128, C), cols("ys", 128, C)))
 
-    cp(A("tauh", slice(0, 8)), A("taui", slice(0, 8)))
-    cp(A("df"), A("di"))
+    ts(A("tauh", slice(0, 8)), A("taui", slice(0, 8)), -OFF, Op.add)
+    ts(A("df"), A("di"), M1, Op.add)
     for h in range(2):
         first_times(h)
-    act(A("nt0"), q(4, 0, 16), Fn.Identity, bias=W, scale=-1.0)
+    act(A("nt0"), q(4, 0, 16), Fn.Identity, scale=-1.0)
     act(cols("nt1", 0, 8), cols("nt0", 0, 8), Fn.Identity)
     act(cols("nt1", 9, 16), cols("nt0", 8, 15), Fn.Identity)
     act(cols("nt1", 8, 9), cols("nt0", 15, 16), Fn.Identity)
-    for a in (0, 1024):
-        act(cols("st0", a, a + 1024), cols("x0", a, a + 1024), Fn.Identity, scale=7.0, bias=-MID)
-    act(cols("st0", W, W + 1), cols("st0", 0, 1), Fn.Identity)
     for h in range(2):
-        centres(h)
+        centres(0, h, "di")
         times(h)
-    first = [hand_over("x0", [gains] + copies)]
+    hand_over("x0", [gains])
     for t in range(VI):
         for h in range(2):
-            hear(t, h)
-            claims(t, h)
-            histogram(h)
+            k0 = 0
+            for piece in HEAR[h]:
+                hear(t, h, *piece)
+            for w, k, k1 in sorted(HEAR[h]):
+                if w and k == k0:
+                    below(h, k0, min(r for r in ROWS[h] if r > k0))
+                count(h, w, k, k1)
+                if (w, k1) == (0, 16):
+                    on_time(t, h)
+                if w and k1 in ROWS[h]:
+                    claims(h, k0, k1)
+                    for a, b in zip(COUNT[h], COUNT[h][1:]):
+                        if k0 <= a < k1:
+                            histogram(h, a, b)
+                    k0 = k1
+        claimed(True)
+        ts(A("pl%d" % (t % 2)), q(TC[0], 128, 384), 0.75 - 32 * 160, Op.add, float(NONE), Op.min)
         if t > 0:
             sum_terms(t - 1)
         owners(t)
@@ -589,8 +628,8 @@ def build(g, core, T, topo, rank):
             logs()
             send(4, A("ul1"), A("u0"))
         else:
-            act(half("ef1", 0), half("df", 0), Fn.Exp, scale=1.0 / 256)
-            act(A("ev"), half("df", 1), Fn.Exp, scale=1.0 / 256)
+            act(half("ef1", 0), half("df", 0), Fn.Exp, scale=1.0 / 256, bias=-M1 / 256)
+            act(A("ev"), half("df", 1), Fn.Exp, scale=1.0 / 256, bias=-M1 / 256)
             rotate("ef1", 128, "ev", 0, 112)
             send(5, A("ul2"), A("u1"), A("ul1"))
         taken_columns(t)
@@ -635,6 +674,16 @@ def arrange(ops):
         if ops[i]["move"]:
             moving[i] = len(ops)
             ops.append({"eng": "dm", "ns": ops[i]["move"], "wake": ops[i]["wake"], "sem": True})
+
+    def length(o, slow, engines, dmas, wake):
+        return o["ns"] * dmas if o["sem"] else (o["ns"] + o["more"] * (slow - 1)) * engines
+
+    def waits(links, slow, engines, dmas, wake):
+        return [[(k, gap * (wake if gap == WAKE else dmas)) for k, gap in d.items()] for d in links]
+
+    lengths = [[length(o, *s) for o in ops] for s in SLOW]
+    weight = [1 / (s[1] * (0.6 + 0.4 * max(s[0], 1))) for s in SLOW]
+    ops = [dict(o, ns=length(o, *MIDDLE)) for o in ops]
     before = [{moving[j] if j in moving and (gap or not ops[i]["eng"]) else j: gap for j, gap in dep.items()} for i, dep in enumerate(before)]
     before += [{i: 0} for i in moving]
     behind = [{} for o in ops]
@@ -688,12 +737,12 @@ def arrange(ops):
             left[j] -= 1
             if not left[j]:
                 todo.append(j)
-    def replay(order, slow):
+    def replay(order, ns):
         end, free = [0.0] * len(ops), {e: 0.0 for e in ENG + (None,)}
         for i in order:
             for j in (i, moving[i]) if i in moving else (i,):
                 e = ops[j]["eng"]
-                end[j] = max([end[k] + gap for k, gap in before[j].items()] + [free[e]]) + ops[j]["ns"] + ops[j].get("more", 0.0) * (slow - 1)
+                end[j] = max([end[k] + gap for k, gap in before[j].items()] + [free[e]]) + ns[j]
                 free[e] = end[j] if e else 0.0
         return max(e + w for e, w in zip(end, tail))
 
@@ -709,92 +758,153 @@ def arrange(ops):
         for how in (place, fit, fit) * ROUNDS:
             end = how(turn, before, [0.0] * len(ops))
             order = [i for i in sorted(turn, key=lambda i: end[i] - ops[i]["ns"]) if i < count]
-            span = sum(replay(order, s) for s in SLOW) / len(SLOW)
+            span = sum(replay(order, ns) * w for ns, w in zip(lengths, weight)) / len(SLOW)
             if best is None or span < best[0]:
                 best = (span, order)
             end = how(sorted(turn[::-1], key=lambda i: -end[i] - tail[i]), behind, tail)
             turn = sorted(turn, key=lambda i: -end[i])
 
-    needs = [list(d.items()) for d in before]
-    users = [list(d) for d in behind]
-    lengths = [[o["ns"] + o.get("more", 0.0) * (s - 1) for o in ops] for s in SLOW]
+    cases = [(ns, waits(before, *s), waits(behind, *s)) for ns, s in zip(lengths, SLOW)]
     issuer = {j: i for i, j in moving.items()}
-
-    def run(lines):
-        left, nxt, prv = [len(d) for d in needs], {}, {}
-        for line in lines.values():
-            for a, b in zip(line, line[1:]):
-                nxt[a], prv[b] = b, a
-                left[b] += 1
-        todo = [i for i in range(len(ops)) if not left[i]]
-        for i in todo:
-            for j in users[i] + [nxt[i]] if i in nxt else users[i]:
-                left[j] -= 1
-                if not left[j]:
-                    todo.append(j)
-        if len(todo) < len(ops):
-            return None
-        runs = []
-        for ns in lengths:
-            end, why = [0.0] * len(ops), [-1] * len(ops)
-            for i in todo:
-                w = prv.get(i, -1)
-                at = end[w] if w >= 0 else 0.0
-                for k, gap in needs[i]:
-                    if end[k] + gap > at:
-                        at, w = end[k] + gap, k
-                end[i], why[i] = at + ns[i], w
-            last = max(range(len(ops)), key=lambda i: end[i] + tail[i])
-            runs.append((end[last] + tail[last], why, last, end))
-        return sum(r[0] for r in runs) / len(runs), runs, prv, todo
+    eng, every = [o["eng"] for o in ops], range(len(ops))
 
     def rnd(n):
         seed[0] = (seed[0] * 1103515245 + 12345) % 2 ** 31
         return (seed[0] >> 8) % n
 
-    def settled(lines):
-        now = run(lines)
-        if now:
-            line = sorted(lines["dm"], key=lambda j: now[1][0][3][issuer[j]])
-            if line != lines["dm"]:
-                lines["dm"] = line
-                now = run(lines)
+    def forwards(order):
+        prv, nxt, last = [-1] * len(ops), [-1] * len(ops), {}
+        for i in order:
+            if eng[i]:
+                if eng[i] in last:
+                    prv[i], nxt[last[eng[i]]] = last[eng[i]], i
+                last[eng[i]] = i
+        ends = []
+        for ns, needs, users in cases:
+            end = [0.0] * (len(ops) + 1)
+            for i in order:
+                at = end[prv[i]]
+                for k, gap in needs[i]:
+                    if end[k] + gap > at:
+                        at = end[k] + gap
+                end[i] = at + ns[i]
+            ends.append(end)
+        spans = [max(e + w for e, w in zip(end, tail)) for end in ends]
+        return {"order": order, "prv": prv, "nxt": nxt, "ends": ends, "spans": spans, "span": sum(s * w for s, w in zip(spans, weight)) / len(spans)}
+
+    def settled(now):
+        end, ns = now["ends"][0], lengths[0]
+        order = [j for i in sorted((i for i in now["order"] if i < count), key=lambda i: end[i] - ns[i]) for j in ((i, moving[i]) if i in moving else (i,))]
+        if [i for i in order if i >= count] != [i for i in now["order"] if i >= count]:
+            now = forwards(order)
+        now["order"], now["at"], now["rests"], now["pairs"] = order, {i: n for n, i in enumerate(order)}, [], []
+        for (ns, needs, users), end, span in zip(cases, now["ends"], now["spans"]):
+            rest, nxt = [0.0] * (len(ops) + 1), now["nxt"]
+            for i in reversed(order):
+                at = max(rest[nxt[i]], tail[i])
+                for k, gap in users[i]:
+                    if rest[k] + gap > at:
+                        at = rest[k] + gap
+                rest[i] = at + ns[i]
+            now["rests"].append(rest)
+            now["pairs"] += [(i, nxt[i]) for i in every if nxt[i] >= 0 and end[i] + rest[nxt[i]] > span - 1 and i not in before[nxt[i]]]
         return now
 
-    seed = [seed]
-    lines = {e: [i for i in best[1] if ops[i]["eng"] == e] for e in ENG}
-    lines["dm"] = [moving[i] for i in best[1] if i in moving]
-    now = best = settled(lines)
-    for _ in range(MOVES):
-        span, why, i, end = now[1][rnd(len(SLOW))]
-        pairs = []
-        while i >= 0:
-            if why[i] >= 0 and now[2].get(i) == why[i] and why[i] not in before[i]:
-                pairs.append((why[i], i))
-            i = why[i]
-        a, b = pairs[rnd(len(pairs))]
+    def moved(now):
+        a, b = now["pairs"][rnd(len(now["pairs"]))]
         if a in issuer:
             a, b = issuer[a], issuer[b]
-            if ops[a]["eng"] != ops[b]["eng"]:
-                continue
-        old = dict(lines)
-        line = lines[ops[a]["eng"]] = list(lines[ops[a]["eng"]])
-        step = (0, 0, 1, 2, 4, 8, 16, 32)[rnd(8)]
-        if rnd(2):
-            line.remove(b)
-            line.insert(max(0, line.index(a) - step), b)
-        else:
-            line.remove(a)
-            line.insert(line.index(b) + 1 + step, a)
-        new = settled(lines)
-        if new and new[0] <= now[0] + rnd(SLACK):
-            now = new
-            if new[0] < best[0]:
-                best = new
-        else:
-            lines = old
-    SPAN.append(best[0])
-    return [i for i in best[3] if i < count]
+        order, at, up = now["order"], now["at"], rnd(2)
+        side, links = (now["prv"], before) if up else (now["nxt"], behind)
+        mine, past = (b, a) if up else (a, b)
+        for _ in range((0, 0, 1, 2, 4, 8, 16, 32)[rnd(8)]):
+            past = side[past] if side[past] >= 0 else past
+        lo, hi = sorted((at[mine], at[past]))
+        hi += order[hi] in moving
+        along, todo = {mine}, [mine]
+        for i in todo:
+            near = list(links[i]) + ([side[i]] if eng[i] != eng[mine] and i != moving.get(mine) else []) + ([moving[i]] if i in moving else [])
+            for j in near:
+                if j >= 0 and j not in along and lo <= at[j] <= hi:
+                    along.add(j)
+                    todo.append(j)
+        if past in along or lo >= hi:
+            return None
+        return valued(now, lo, hi, sorted(order[lo:hi + 1], key=lambda i: (i in along) != up))
+
+    def ends_of(now, old):
+        first, last = {}, {}
+        for i in old:
+            first.setdefault(eng[i], now["prv"][i])
+            last[eng[i]] = now["nxt"][i]
+        return first, last
+
+    def replanned(now):
+        order, at, s = now["order"], now["at"], rnd(len(SLOW))
+        (ns, needs, users), ends, rest = cases[s], now["ends"][s], now["rests"][s]
+        lo = rnd(len(order))
+        lo -= order[lo] >= count
+        hi = min(len(order) - 1, lo + 20 + rnd(STRETCH))
+        hi += order[hi] in moving
+        old, noise, patience = order[lo:hi + 1], rnd(NOISE) + 1, rnd(8) * PATIENCE
+        first, last = ends_of(now, old)
+        chain, left, ready, start = {}, {}, {e: [] for e in first}, {}
+        for i in reversed(old):
+            chain[i] = ns[i] + max([tail[i], rest[last[eng[i]]] if eng[i] else 0] + [gap + (chain[k] if k in chain else rest[k]) for k, gap in users[i]])
+        for i in old:
+            chain[i] += rnd(noise)
+            left[i] = sum(at[k] >= lo for k, gap in needs[i])
+            start[i] = max([0.0] + [ends[k] + gap for k, gap in needs[i] if at[k] < lo])
+            if not left[i]:
+                ready[eng[i]].append(i)
+        free, new = {e: ends[i] if e else 0.0 for e, i in first.items()}, []
+        while len(new) < len(old):
+            t, e = min(((max(free[e], min(start[i] for i in r)), e) for e, r in ready.items() if r), key=lambda x: x[0])
+            i = max((j for j in ready[e] if start[j] <= t + patience), key=chain.get)
+            for i in (i, moving[i]) if i in moving else (i,):
+                ready[eng[i]].remove(i)
+                new.append(i)
+                t = max(free[eng[i]], start[i]) + ns[i]
+                free[eng[i]] = t if eng[i] else 0.0
+                for k, gap in users[i]:
+                    if k in left:
+                        start[k] = max(start[k], t + gap)
+                        left[k] -= 1
+                        if not left[k]:
+                            ready[eng[k]].append(k)
+        return valued(now, lo, hi, new) if new != old else None
+
+    def valued(now, lo, hi, new):
+        order, at = now["order"], now["at"]
+        first, last = ends_of(now, order[lo:hi + 1])
+        total = 0.0
+        for (ns, needs, users), ends, rest, w in zip(cases, now["ends"], now["rests"], weight):
+            end, free, span = {}, {e: ends[i] for e, i in first.items()}, 0.0
+            for i in new:
+                t = free[eng[i]] if eng[i] else 0.0
+                for k, gap in needs[i]:
+                    t = max(t, end.get(k, ends[k]) + gap)
+                end[i] = free[eng[i]] = t = t + ns[i]
+                span = max(span, t + tail[i])
+                for k, gap in users[i]:
+                    if at[k] > hi and t + gap + rest[k] > span:
+                        span = t + gap + rest[k]
+            total += w * max([span] + [free[e] + rest[i] for e, i in last.items() if e])
+        return total / len(weight), order[:lo] + new + order[hi + 1:]
+
+    seed = [seed]
+    now = best = settled(forwards([j for i in best[1] for j in ((i, moving[i]) if i in moving else (i,))]))
+    for n in range(MOVES):
+        limit = now["span"] + rnd(SLACK) * (1 - n / MOVES)
+        new = moved(now) if n % ANEW else replanned(now)
+        if new and new[0] <= limit:
+            new = forwards(new[1])
+            if new["span"] <= limit:
+                now = settled(new)
+                if now["span"] < best["span"]:
+                    best = now
+    SPAN.append(best["span"])
+    return [i for i in best["order"] if i < count]
 
 
 def emit(ops, queue, T):

from concourse.bass import DstId, RemoteDMATransfer
from concourse.mybir import AluOpType as Op, ActivationFunctionType as Fn

N, W, C, VI = 8, 2048, 256, 3
BIGH = 1.5 * 2 ** 13
M1 = 1.5 * 2 ** 23
M256 = 1.5 * 2 ** 31
MID = 945.0
B = 8192.0
HALF = (2.0, 2 + 3.0 / 512)
M2K = 1.5 * 2 ** 34
OFF = 1023.5
NONE = W + 2
COPIES = 4
PIECES = ((0, 2, 1), (2, 4, 3))
LEVELS = ((2, 2), (1, 1))
PIECE = 1024
NEW = (((0, 16),), ((0, 16),))
HEAR = (((0, 0, 8), (0, 8, 16), (1, 0, 8), (1, 8, 16)), ((0, 0, 8), (0, 8, 16), (1, 0, 8), (1, 8, 12), (1, 12, 16)))
ROWS = ((16,), (8, 16))
COUNT = ((0, 8, 16), (0, 8, 16))
JOIN = ((3, 5, 7, 9, 11, 13, 15), ())
XB = (5, 6, 0, 2)
XU_DVE = (3,)
XG_DVE = ((0, 0), (0, 2))
VV_PE = False
TNB_DVE = (0,)
ER_DVE = (0,)
XG = (0, 4, 8, 12, 16)
DOUBLE = ((("act", "dve", "dve"), ("act", "dve", "gp")), (("act", "gp", "gp"), ("act", "gp", "gp")))
TAIL = 13
STEP = 256
LAST = (0, 256, 768, 1280, 1792, 2048)
TA, TB, TC = (5, 6), (1, 3), (0, 2)

S, P = "sbuf", "psum"
X3 = [128, W + 16]
H3 = [128, 16, 16]
SCRATCH = {
    "x0": (S, X3, "bfloat16"), "x1": (S, X3, "bfloat16"), "x2": (S, X3, "bfloat16"),
    "g0": (S, [128, W], "bfloat16"), "g2": (S, [128, W], "bfloat16"), "lg0": (S, [128, W], "float32"), "lg1": (S, [128, W], "float32"),
    "xu": (S, X3, "bfloat16"), "zt": (S, [128, W + 8], "float32"), "wv": (S, [128, W + 8], "float32"),
    "xg": (S, [128, 4096], "bfloat16"), "zg0": (S, [128, 2, 2048], "float32"), "zg1": (S, [128, 2, 2048], "float32"),
    "ind0": (S, [128, 4096], "bfloat16"), "ind1": (S, [128, 4096], "bfloat16"),
    "oa": (S, [128, 2, 8192], "float16"), "ob0": (S, [128, 264, 16], "float16"), "ob1": (S, [128, 264, 16], "float16"),
    "ivi": (S, [128, C], "int32"), "ivh": (S, [128, C], "float16"), "taui": (S, [128, C], "int32"), "tauh": (S, [128, C], "float16"),
    "di": (S, [128, C], "int32"), "df": (S, [128, C], "float32"), "dri": (S, [128, 128], "int32"), "drf": (S, [128, 128], "float32"),
    "kt": (S, [128, 264], "float32"), "mb": (S, [128, C], "bfloat16"), "hi": (S, [128, C], "float16"), "at": (S, [128, 2, PIECE], "float32"),
    "tu": (S, H3, "float32"), "th": (S, H3, "float16"),
    "of0": (S, [128, C], "uint16"), "of1": (S, [128, C], "uint16"), "pl0": (S, [128, C], "uint16"), "pl1": (S, [128, C], "uint16"),
    "on": (S, H3, "bfloat16"), "m0": (S, H3, "bfloat16"), "ee": (S, H3, "bfloat16"),
    "aa": (S, [128, 2, 128 * COPIES], "bfloat16"), "bb": (S, [128, 64, 16], "bfloat16"),
    "s32": (S, [128, 8, 48], "bfloat16"), "n80k": (S, [128, 128], "bfloat16"),
    "rr": (S, [128, C], "float16"), "rw": (S, [128, 4, 32], "float16"),
    "ef0": (S, [128, C], "float32"), "ev": (S, [128, 128], "float32"), "ef1": (S, [128, C], "float32"), "zero": (S, [128, C], "bfloat16"),
    "u0": (S, [128, 128], "bfloat16"), "u1": (S, [128, 128], "bfloat16"),
    "ul1": (S, [128, 128], "bfloat16"), "ul2": (S, [128, 128], "bfloat16"), "idx": (S, [128, 128], "uint16"),
    "tnb": (S, [128, C], "bfloat16"), "sl": (S, [128, 2, C], "bfloat16"), "seg": (S, [128, C], "float32"), "sc": (S, [128, 2, C], "float32"),
    "cl": (S, [128, 8 * 43, 16], "float32"), "e2": (S, [128, 16], "float32"), "er": (S, [128, C], "float32"), "dx": (S, [128, 128], "float32"),
    "nt0": (S, [128, 16], "float32"), "nt1": (S, [128, 16], "float32"),
    "ntp": (S, [128, C], "bfloat16"), "d1": (S, [128, C], "float32"), "d2": (S, [128, C], "float32"),
    "ya": (S, [128, C], "float32"), "yb": (S, [128, C], "float32"), "ys": (S, [128, C], "float32"), "yacc": (S, [128, 384], "float32"),
    "one": (S, [128, 128], "bfloat16"), "tr1": (S, [128, 128], "bfloat16"), "tri": (S, [128, 128], "bfloat16"), "blf": (S, [128, 128], "bfloat16"),
    "e8": (S, [128, 128], "bfloat16"), "idf": (S, [128, C], "float32"), "idb": (S, [128, C], "bfloat16"),
    "n32": (S, [128, 128], "bfloat16"), "i24": (S, [128, 128], "bfloat16"), "blr": (S, [128, 128], "bfloat16"), "b4k": (S, [128, 8], "bfloat16"), "b3": (S, [128, 8, 3], "bfloat16"),
    "s3": (S, [128, 8, 48], "bfloat16"), "c256": (S, [128, C], "bfloat16"), "sel": (S, [128, W], "bfloat16"),
    "cin": (S, [128, 384], "bfloat16"), "wc": (S, [128, 2], "bfloat16"),
    "k3": (S, [128, 8], "int32"), "el": (S, [128, 8], "uint16"),
}
for _b in range(8):
    SCRATCH["q%d" % _b] = (P, [128, 16, 32] if _b in TA else [128, 32, 16] if _b in TC else [128, 4, 128], "float32")
SHAPES = {"xs": [128, W], "gn": [128, W], "tau": [8, C], "iv": [128, C], "pf": [128, C], "y": [128, C]}
ENG = ("pe", "act", "dve", "gp", "sp", "dm")
LONG = (("x0", 1, "x1", 0), ("x0", 2, "x2", 0), ("g0", 2, "g2", 1), ("lg0", 1, "lg1", 0))
SEMAPHORES = (["pe", "act", "dve", "gp"] + ["d%d" % i for i in range(70)] + ["l%d" % i for i in range(6)] + ["a%d" % i for i in range(6)]
              + ["hx0", "hg0", "hlg0"])
ALL = slice(None)
MASKS = {}
ORDER = []
CYC, PCYC, GATHER, VCALL, SCALL, WAKE, LOCAL, REMOTE, ISSUE, ROW, LRATE, RRATE = 0.83, 0.45, 1.4, 15, 65, 130, 2200, 3000, 700, 50, 38, 60
ADDS = 1.5
ROUNDS, PATIENCE, TRIALS, NOISE, MOVES, SLACK = 3, 30, 2, 300, 36000, 20
SLOW, MIDDLE = ((0.8, 1.05, 1.25, 1), (1.3, 1.05, 1, 1.6), (0.85, 1.3, 1, 1.3), (1.35, 1.4, 1.2, 1)), (1.1, 1.2, 1.1, 1)
STRETCH, ANEW = 150, 3
SPAN = []


def helpers(topo, cores, rank):
    core = cores[rank]
    free = [c for c in topo.cores_of(core) if c not in cores]
    far = [c for c in free if topo.die(c) != topo.die(core) and topo.may_write(c, cores[(rank - 1) % N])]
    near = [c for c in free if topo.die(c) == topo.die(core) and topo.may_write(c, cores[(rank - 2) % N])]
    return [far[0], near[0]]


def pass_on(g, core, T, topo, rank, me):
    mine = [(k, src, dst, T.cores[(rank - back) % N]) for k, (src, back, dst, by) in enumerate(LONG) if by == me]
    for k, src, dst, to in mine:
        rid, pid = topo.addr(to)[:2]
        g.wait_ge(T.sem["h" + src], len(topo.engines(T.cores[rank], core)))
        g.remote_dma(T[dst][:], T[src][:], T.sem["a%d" % k], T.sem["l%d" % k], pid, rid, topo.mask(core, to))
    for k, src, dst, to in mine:
        g.wait_ge(T.sem["l%d" % k], len(topo.engines(core, to)))


def build(g, core, T, topo, rank):
    ops = []
    nd = [0]
    heard, added = [], []
    queue = {"pe": g.tensor, "act": g.scalar, "dve": g.vector, "gp": g, "sp": g.sync}

    def A(name, *ix):
        where, shape, dt = (None, SHAPES[name], "") if name in SHAPES else SCRATCH[name]
        ix = list(ix) + [ALL] * (len(shape) - len(ix))
        rs = [range(n)[s] if isinstance(s, slice) else range(s, s + 1) for s, n in zip(ix, shape)]
        key = (shape[-1],) + tuple((r.start, r.stop, r.step) for r in rs[1:])
        if key not in MASKS:
            row = sum(1 << c for c in rs[-1])
            MASKS[key] = row if len(shape) == 2 else sum(row << (b * shape[-1]) for b in rs[1])
        return (T[name][tuple(ix)], [(name, rs[0][0], rs[0][-1], MASKS[key])], MASKS[key].bit_count(), 2 if "16" in dt else 4, where)

    def cols(name, a, b, s=1, part=ALL):
        shape = SHAPES[name] if name in SHAPES else SCRATCH[name][1]
        if len(shape) == 2:
            return A(name, part, slice(a, b, s))
        n = shape[2]
        if a // n == (b - 1) // n:
            return A(name, part, a // n, slice(a % n, (b - 1) % n + 1, s))
        return A(name, part, slice(a // n, b // n), slice(a % n, n, s))

    def half(name, h):
        return cols(name, 128 * h, 128 * h + 128)

    def q(b, a=0, e=512, s=1, part=ALL):
        return cols("q%d" % b, a, e, s, part)

    def q3(b, a, e, c, d, s=1):
        return A("q%d" % b, ALL, slice(a, e), slice(c, d, s))

    def IND(win, off):
        return (win[0].indirect(off[0]), win[1] + off[1], 16 * off[2], win[3], "gather")

    def add(eng, call, outs, ins, ns, sem=None, n=0, extra=None, wake=WAKE, after=(), move=0.0):
        ops.append({"eng": eng, "call": call, "w": [b for o in outs for b in o[1]], "ns": ns, "wake": wake, "after": list(after), "move": move,
                    "more": sum(CYC * GATHER * i[2] for i in ins if isinstance(i, tuple) and i[4] == "gather"),
                    "r": [b for i in ins if isinstance(i, tuple) for b in i[1]], "sem": sem, "n": n, "inc": False, "extra": extra})
        return len(ops) - 1

    def v(x):
        return x[0] if isinstance(x, tuple) else x

    def vtime(out, a, slow=False):
        if a[4] == "gather":
            return 50 + CYC * GATHER * out[2]
        return VCALL + CYC * max(64, out[2] * (2 if slow else 0.5 if out[3] == a[3] == 2 else 1))

    def ts(out, in0, s1, op0, s2=None, op1=None):
        if op1 is None:
            return add("dve", lambda: g.vector.tensor_scalar(out[0], in0[0], v(s1), None, op0), [out], [in0, s1], vtime(out, in0))
        return add("dve", lambda: g.vector.tensor_scalar(out[0], in0[0], v(s1), v(s2), op0, op1), [out], [in0, s1, s2], vtime(out, in0))

    def tt(out, a, b, op):
        return add("dve", lambda: g.vector.tensor_tensor(out[0], a[0], b[0], op), [out], [a, b], vtime(out, a, a[4] == b[4] == S))

    def cp(out, a):
        return add("dve", lambda: g.vector.tensor_copy(out[0], a[0]), [out], [a], vtime(out, a))

    def ms(out, c):
        add("dve", lambda: g.vector.memset(out[0], c), [out], [], vtime(out, out))

    def act(out, a, f, bias=0.0, scale=1.0, load=0, after=()):
        return add("act", lambda: g.scalar.activation(out[0], a[0], f, bias=float(bias), scale=float(scale)), [out], [a],
                   load + SCALL + CYC * out[2] * (GATHER if a[4] == "gather" else 1), after=after)

    def mm(out, l, r, start=True, stop=True, joined=False):
        add("pe", lambda: g.tensor.matmul(out[0], l[0], r[0], start, stop), [out], [l, r], PCYC * max(min(64, l[2]), r[2]) * (4 if l[3] == 4 else 1))
        if joined:
            b = ops.pop()
            a = ops[-1]
            one, two = a["call"], b["call"]
            a.update(call=lambda: (one(), two())[1], w=merged(a["w"] + b["w"]), r=merged(a["r"] + b["r"]), ns=a["ns"] + b["ns"])

    def merged(parts):
        masks = {}
        for name, p0, p1, m in parts:
            masks[name, p0, p1] = masks.get((name, p0, p1), 0) | m
        return [k + (m,) for k, m in masks.items()]

    def sel(out, a, pat, op, base, cm, after=()):
        return add("gp", lambda: g.affine_select(out[0], a[0], pat, op, 0.0, base, cm), [out], [a], 170 + 2 * CYC * out[2], after=after)

    def iota(out, pat, base, cm, small):
        if small:
            add("gp", lambda: g.iota(out[0], pat, base, cm, allow_small_or_imprecise_dtypes=True), [out], [], 130 + 2 * CYC * out[2])
        else:
            add("gp", lambda: g.iota(out[0], pat, base, cm), [out], [], 130 + 2 * CYC * out[2])

    def moved(side, times=1):
        return 8 * (ROW + times * side[2] * side[3] / LRATE)

    def dma(eng, *pairs, after=()):
        nd[0] += 1
        sem = "d%d" % (nd[0] - 1)
        return add(eng, lambda: [queue[eng].dma_start(o[0], a[0]).then_inc(T.sem[sem], 16) for o, a in pairs], [o for o, a in pairs], [a for o, a in pairs],
                   2 * ISSUE if eng == "gp" else 50 * len(pairs), sem=sem, n=16 * len(pairs), extra="own", wake=LOCAL, move=sum(moved(o if o[4] else a) for o, a in pairs), after=after)

    def dma_add(out, a, after=()):
        nd[0] += 1
        return add("gp", lambda: g.dma_start(out[0], a[0], accum_op=Op.add), [out], [a, out], ISSUE, sem="d%d" % (nd[0] - 1), n=16, wake=LOCAL, move=moved(out, ADDS),
                   after=after)

    def hand_over(src, after=()):
        ks = [k for k in range(len(LONG)) if LONG[k][0] == src]
        via = helpers(topo, T.cores, rank)[LONG[ks[0]][3]]
        rid, pid = topo.addr(via)[:2]
        i = add("gp", lambda: g.remote_dma(T[src][:], T[src][:], T.sem["h" + src], T.sem["l%d" % ks[0]], pid, rid, topo.mask(core, via)), [], [A(src)],
                2500 if ks[0] == 0 else 300, sem="l%d" % ks[0], n=len(topo.engines(core, via)), extra="own", wake=LOCAL, after=after, move=moved(A(src)))
        for n, k in enumerate(ks):
            sender = helpers(topo, T.cores, (rank + LONG[k][1]) % N)[LONG[k][3]]
            add(None, None, [A(LONG[k][2])], [], 2 * REMOTE + (n + 1) * 128 * A(src)[2] * A(src)[3] / RRATE, sem="a%d" % k, n=len(topo.engines(sender, core)), after=[i])
            ops[-1]["from"] = "l%d" % ks[0]
        return i

    def send(k, dst, *srcs):
        to = T.cores[(rank - 1) % N]
        rid, pid = topo.addr(to)[:2]
        call = lambda: g.remote_dma_fused([RemoteDMATransfer(dst_ids=[DstId(rid=rid, pnc=pid)], dma_engine_mask=topo.mask(core, to), remote_sem=T.sem["a%d" % k],
                                                             srcs=[a[0] for a in srcs], dsts=[dst[0]], alu_op=int(len(srcs) > 1))], local_sem=T.sem["l%d" % k])
        i = add("gp", call, [], srcs, 300, sem="l%d" % k, n=len(topo.engines(core, to)), extra="own", wake=REMOTE, move=moved(dst))
        add(None, None, [dst], [], REMOTE + 1000, sem="a%d" % k, n=len(topo.engines(T.cores[(rank + 1) % N], core)), after=[i])
        ops[-1]["from"] = "l%d" % k

    dma("sp", (A("ivi"), A("iv")))
    dma("act", (A("taui", slice(0, 8)), A("tau")))
    dma("sp", (A("di"), A("pf")))
    dma("act", (cols("x0", 0, 1024), cols("xs", 0, 1024)), (cols("x0", W, W + 16), cols("xs", 0, 16)))
    dma("sp", (cols("x0", 1024, W), cols("xs", 1024, W)))

    def rotate(dst, at, src, a, s=16):
        dma("sp", (A(dst, slice(s, 128), slice(at, at + 128)), A(src, slice(0, 128 - s), slice(a, a + 128))),
            (A(dst, slice(0, s), slice(at, at + 128)), A(src, slice(128 - s, 128), slice(a, a + 128))))

    def shifted(dst, src, s, scale):
        act(cols(dst, s, 128), cols(src, 0, 128 - s), Fn.Identity, scale=scale)
        act(cols(dst, 0, s), cols(src, 128 - s, 128), Fn.Identity, scale=scale)

    rotate("dri", 0, "pf", 128)
    for name, value in (("one", 1.0), ("s3", 0.0), ("c256", 256.0), ("rw", 0.0), ("zero", 0.0), ("seg", 1.0), ("cin", 0.0)):
        ms(A(name), value)
    ms(cols("seg", 0, C, 32), 0.0)
    ms(cols("cin", 1, C, 2), 4096.0)
    ms(cols("cin", C, 384), -15.0 / 64)
    ms(cols("kt", 0, 1), 1e9)
    ms(cols("kt", C + 1, C + 8), 1e9)
    ms(cols("xu", W, W + 16), 0.0)
    ms(cols("zt", W, W + 8), 0.0)
    ms(cols("wv", W, W + 8), 1e9)
    sel(A("tr1"), A("one"), [[-16, 8], [0, 16]], Op.is_ge, 0, 1)
    sel(A("tri"), A("tr1"), [[1, 128]], Op.is_ge, 0, -1)
    sel(A("e8"), A("one"), [[-1, 8], [0, 16]], Op.is_equal, 0, 1)
    ident, identf = half("idb", 0), half("idf", 0)
    sel(ident, A("one"), [[-1, 128]], Op.is_equal, 0, 1)
    sel(A("blf"), A("tr1"), [[16, 8], [0, 16]], Op.is_ge, 15, -1)
    gains = dma("gp", (A("g0"), A("gn")), after=[len(ops) - 1])
    iota(A("wc"), [[0, 2]], 128, 1, True)
    iota(A("k3"), [[1, 8]], 0, 0, False)
    cp(A("s3", ALL, ALL, slice(16, 32)), ident)
    cp(half("idb", 1), ident)
    cp(A("el"), A("k3"))
    ts(A("s32"), A("s3"), 32.0, Op.mult)
    for name, scale in (("n32", -32.0), ("i24", 24.0), ("n80k", -20 * 4096.0)):
        ts(A(name), ident, scale, Op.mult)
    for h in range(2):
        act(half("idf", h), ident, Fn.Identity)
    act(A("b4k"), cols("blf", 0, 128, 16), Fn.Identity, scale=4096.0)
    shifted("blr", "blf", 16, 1.0 / 32)
    for j, w in enumerate((-512.0, 32.0, 8192.0)):
        act(A("b3", ALL, ALL, j), cols("blf", 0, 128, 16), Fn.Identity, scale=w)

    def first_times(h):
        starts = A("tauh", slice(0, 8), slice(128 * h, 128 * h + 128))
        cp(half("ivh", h), half("ivi", h))
        mm(q(TC[h], C, 384), half("ivh", h), A("tri"), True, False)
        mm(q(TC[h], C, 384), starts, A("e8", slice(0, 8)), False, True)
        wrap(h, False, TC[h], 16, 0, 16)
        offsets(h, 0, 16)
        mm(q(4, 8 * h, 8 * h + 8), starts, A("e8", slice(0, 8), slice(0, 128, 16)))

    def wrap(h, on, bank, row, k0, k1):
        rows, ks = slice(8 * h, 8 * h + 8), slice(k0, k1)
        ts(A("tu", ALL, rows, ks), q3(bank, row, row + 8, k0, k1), M2K, Op.add, -M2K, Op.add)
        if on:
            tt(A("th", ALL, slice(9, 16), ks), q3(bank, row, row + 7, k0, k1), A("tu", ALL, slice(8, 15), ks), Op.subtract)
            tt(A("th", ALL, 8, ks), q3(bank, row + 7, row + 8, k0, k1), A("tu", ALL, 15, ks), Op.subtract)
        else:
            tt(A("th", ALL, rows, ks), q3(bank, row, row + 8, k0, k1), A("tu", ALL, rows, ks), Op.subtract)

    def offsets(h, k0, k1):
        to_list(TC[h], 8 * k0, 8 * k1, "s3", lambda grp: A("th", ALL, 8 * h + grp, slice(k0, k1)), True, True)
        a, b = 128 * h + 8 * k0, 128 * h + 8 * k1
        ts(cols("of0", a, b), q(TC[h], 8 * k0, 8 * k1), OFF, Op.add)
        ts(cols("of1", a, b), cols("of0", a, b), 1.0, Op.add)

    def to_list(bank, a, b, pick, group, alone, last):
        for m in range(8):
            for gp in range(4):
                for e in range(2):
                    mm(q(bank, a + m, b, 8, slice(32 * gp, 32 * gp + 32)), A(pick, ALL, m, slice(16 - 16 * e, 48 - 16 * e)), group(2 * gp + e),
                       alone and e == 0, e == 1 and (alone or last and m == 7), (m % 2, gp, e) != (0, 0, 0))

    def claimed(last):
        if last:
            to_list(TC[0], 128, 384, "s3", lambda grp: A("bb", ALL, slice(grp, 64, 32)), False, True)
        else:
            mm(q(TC[0], 128, 384), ident, A("zero"), True, False)
            to_list(TC[0], 128, 384, "s32", lambda grp: A("aa", ALL, ALL, slice(16 * grp, 16 * grp + 16)), False, False)

    def centres(t, h, src):
        ts(half("hi", h), half(src, h), 1.0 / (16 if t else 32), Op.mult, 1024 + 4.015625, Op.add)
        ts(half("mb", h), half("hi", h), -7.0, Op.mult, 7.0 * (1024 + 9) + MID, Op.add)
        o = q(TB[h], C, 384)
        mm(o, identf, half("df", h), True, False)
        mm(o, A("n32"), half("hi", h), False, False, True)
        mm(o, A("n32"), half("mb", h), False, True)
        for n in (0, 128) if DOUBLE[t > 0][h][0] == "act" else (0,):
            act(A("at", ALL, h, slice(n, n + 128)), o, Fn.Identity, bias=BIGH - 36.5 - 1024 + M1 / 32, scale=-1.0 / 32)
        for n, by in zip((128, 256, 512), DOUBLE[t > 0][h]):
            o, a = A("at", ALL, h, slice(n, 2 * n)), A("at", ALL, h, slice(0, n))
            if by == "act":
                continue
            elif by == "dve":
                cp(o, a)
            elif by == "sp":
                dma("sp", (o, a))
            else:
                sel(o, a, [[0, n]], Op.is_ge, 0, 0)

    def times(h):
        ts(A("aa", ALL, h, slice(0, 128)), half("th", h), 1.0 / 32, Op.mult, 160 + (OFF - 15.5) / 32, Op.add)
        o = q3(TA[h], 0, 8, 16, 32)
        mm(o, ident, half("th", h), True, False)
        mm(o, A("n32"), A("aa", ALL, h, slice(0, 128)), False, False, True)
        mm(o, A("i24"), half("c256", 0), False, True, True)
        if h:
            claimed(False)
        n = 1
        while n < COPIES:
            ts(A("aa", ALL, h, slice(128 * n, 256 * n)), A("aa", ALL, h, slice(0, 128 * n)), -float(n), Op.add)
            n *= 2
        for a in range(0, 64, n):
            ts(A("oa", ALL, h, slice(128 * a, 128 * (a + n))), A("aa", ALL, h), 160.0 + a, Op.is_equal, cols("wc", 0, 1), Op.mult)

    def hear(t, h, w, k0, k1):
        a, n = 2048 * h + 128 * k0, 128 * (k1 - k0)
        o, src = cols("ind%d" % w, a, a + n), IND(A("x%d" % t), cols("of%d" % w, a // 16, (a + n) // 16))
        heard.append(act(o, src, Fn.Identity, scale=7.0, bias=-MID, after=heard[-1:]))
        added.append(dma_add(o, A("at", ALL, h, slice(0, n))))
        ts(o, o, BIGH, Op.not_equal)

    def count(h, w, k0, k1):
        for k in range(k0, k1):
            mm(q3(TA[h], 8 * w, 8 * w + 8, k, k + 1), cols("ind%d" % w, 2048 * h + 128 * k, 2048 * h + 128 * k + 128), A("b4k"), not w, not w or k + 1 in ROWS[h], k > k0)

    def on_time(t, h):
        ts(half("on", h), q3(TA[h], 0, 8, 0, 16), 5 * 4096.0, Op.is_le, 0.25, Op.add)
        tt(half("m0", h), q3(TA[h], 0, 8, 16, 32), half("on", h), Op.subtract)
        if t < VI - 1:
            act(half("ee", h), half("on", h), Fn.Identity, scale=-1.0, bias=1.25)

    def below(h, k0, k1):
        o, rows, ks = q3(TA[h], 8, 16, k0, k1), slice(8 * h, 8 * h + 8), slice(k0, k1)
        mm(o, ident, A("m0", ALL, rows, ks), True, False)
        mm(o, A("n80k"), A("on", ALL, rows, ks), False, False, True)

    def copies(h, a, b, ks):
        return A("bb", ALL, slice(32 * h + a, 32 * h + b), ks)

    def claims(h, k0, k1):
        ks = slice(k0, k1)
        tt(copies(h, 0, 8, ks), q3(TA[h], 8, 16, k0, k1), A("m0", ALL, slice(8 * h, 8 * h + 8), ks), Op.max)
        ts(copies(h, 8, 16, ks), copies(h, 0, 8, ks), -16.0, Op.add)
        ts(copies(h, 16, 32, ks), copies(h, 0, 16, ks), -1.0, Op.add)

    def histogram(h, k0, k1):
        ob, ks, done = "ob%d" % h, slice(k0, k1), h == 1 and k1 == 16
        ts(A(ob, ALL, slice(256, 264), ks), copies(h, 0, 8, ks), 31.25, Op.is_equal, HALF[h], Op.mult)
        for i in range(8):
            ts(A(ob, ALL, slice(32 * i, 32 * i + 32), ks), copies(h, 0, 32, ks), 2.0 * i - 0.75, Op.is_equal, HALF[h], Op.mult)
        for a, b, bank in PIECES:
            if h == k0 == 0:
                mm(q3(bank, 0, b - a, 0, 66), ident, cols("zero", 0, 66 * (b - a)), True, False)
            for pair in range(a, b):
                for k in range(k0, k1):
                    mm(q3(bank, pair - a, pair - a + 1, 0, 66), A("oa", ALL, h, slice(16 * pair + k, 8192, 64)), A(ob, ALL, slice(pair, 264, 4), k), False,
                       done and (pair, k) == (b - 1, 15), k > k0)
            if done:
                ts(cols("rr", 64 * a, 64 * b), q3(bank, 0, b - a, 0, 64), -127.75, Op.add, 1024.0, Op.min)
                ts(A("rw", ALL, slice(a, b), slice(0, 2)), q3(bank, 0, b - a, 64, 66), 1024.0, Op.min)

    def owners(t):
        for g2 in range(2):
            for b4 in (1, 0):
                o = q(7, b4, 128, 2, slice(64 * g2, 64 * g2 + 64))
                mm(o, cols("rr", 2 * b4 + g2, C, 4), cols("idb", g2, 128, 2), True, b4 == 1, (g2, b4) != (0, 1))
                if b4 == 0:
                    mm(o, cols("rw", g2, 128, 2), cols("idb", 126 + g2, 254, 2), False, True, True)
        if t < VI - 1:
            ts(A("u%d" % t), q(7, 0, 128), M256, Op.add, M256 + 256, Op.is_equal)
        ts(A("idx"), q(7, 0, 128), -127.45, Op.add, C + 1.0, Op.min)
        for h in range(2):
            act(cols("kt", 1 + h, C + 1, 2), half("df", h), Fn.Identity, scale=1.0 / 32, bias=-M1 / 32)

    def spread(u, j, bank, x=None):
        if x:
            mm(q(bank), ident, cols(x, j, W, 4), True, False)
        for i in range(4):
            mm(q(bank, i, 512, 4), cols("sel", 128 * (4 * i + j), 128 * (4 * i + j) + 128), A(u), not x, i == 3 or not x, i > 0)

    def logs():
        parts = [(a, a + 1024) for a in range(0, W, 1024)]
        for a, b in parts:
            i = act(cols("lg0", a, b), cols("g0", a, b), Fn.Ln, load=1300 * (a == 0), after=heard[-1:])
        act(A("ef0"), A("df"), Fn.Exp, scale=1.0 / 256, bias=-M1 / 256, load=1500, after=range(i - 1, i + 1))
        for a, b in parts:
            act(cols("lg0", a, b), cols("lg0", a, b), Fn.Identity, scale=-4.0)
            act(cols("ind0", a, b), cols("x0", a, b), Fn.Identity, scale=-0.5, after=heard[-1:])
        dma_add(A("lg0"), cols("ind0", 0, W))
        hand_over("lg0")

    def terms(t, a, b):
        tt(cols("wv", a, b), IND(A("kt"), cols("idx", a // 16, b // 16)), cols("x%d" % t, a, b), Op.max)
        if b % 1024 == 0:
            dma_add(cols("wv", b - 1024, b), cols("lg%d" % t, b - 1024, b))

    def gather_terms(t, h, a, b, to):
        o, rows = A("zg%d" % (t % 2), ALL, to, slice(128 * a, 128 * b)), cols("pl%d" % (t % 2), 128 * h + 8 * a, 128 * h + 8 * b)
        if t < VI - 1:
            act(o, IND(A("wv"), rows), Fn.Exp, scale=-0.25, after=heard[-1:])
        else:
            act(o, IND(A("zt"), rows), Fn.Identity)

    def home(t, h):
        return cols("idf", 16 * t * h, 16 * t * h + 128)

    def sum_terms(t):
        act(cols("wv", W, W + 1), cols("wv", 0, 1), Fn.Identity)
        for h in range(2):
            for a in (8, 0):
                gather_terms(t, h, a, a + 8, h)
            n = 2048
            for _ in range(LEVELS[t][h]):
                n //= 2
                dma_add(A("zg%d" % t, ALL, h, slice(0, n)), A("zg%d" % t, ALL, h, slice(n, 2 * n)))

    def add_terms(t, bank):
        for h in range(2):
            n = 16 >> LEVELS[t][h]
            for k in range(n):
                mm(q(bank, 128 * h, 128 * h + 128), home(t, h), A("zg%d" % t, ALL, h, slice(128 * k, 128 * k + 128)), k == 0, k == n - 1)
        if t == 0:
            tt(cols("yacc", 128, 384), q(bank, 0, C), A("ef0"), Op.mult)
        else:
            tt(cols("yacc", 0, 128), q(bank, 0, 128), half("ef1", 0), Op.mult)
            tt(half("yb", 0), q(bank, 128, C), half("ef1", 1), Op.mult)

    def taken_columns(t):
        x = "x%d" % t
        for j in range(4):
            spread("u%d" % t, j, XB[j], None if j in XU_DVE else x)
            if j in XU_DVE:
                tt(cols("xu", j, W, 4), q(XB[j]), cols(x, j, W, 4), Op.min)
            else:
                act(cols("xu", j, W, 4), q(XB[j]), Fn.Relu, bias=-256.0)
        cp(cols("xu", W, W + 1), cols("xu", 0, 1))

    def taken(t, h):
        mm(q(TA[h], 0, C), ident, cols("cin", 0, C), True, False)
        mm(q(TB[h], 384, 512), ident, cols("cin", C, 384), True, False)
        for kq, (k0, k1) in enumerate(zip(XG, XG[1:])):
            a, b = 2048 * h + 128 * k0, 2048 * h + 128 * k1
            o, src = cols("xg", a, b), IND(A("xu"), cols("pl%d" % (t % 2), a // 16, b // 16))
            if (h, kq) in XG_DVE:
                cp(o, src)
            else:
                act(o, src, Fn.Identity)
            for k in range(k0, k1):
                a, s = 2048 * h + 128 * k, int(k == 0)
                mm(q3(TA[h], 0, 8, 2 * k - 1 + s, 2 * k + 2), cols("xg", a, a + 128), A("b3", ALL, ALL, slice(s, 3)), False, k == 15, k > k0)
            for k in range(k0, k1):
                a = 2048 * h + 128 * k
                mm(q(TB[h], 384, 512), cols("idb", 112 * h, 112 * h + 128), cols("xg", a, a + 128), False, k == 15, k > k0)

    def next_table(t):
        for j in range(4):
            bank = (4, 7)[j % 2]
            spread("ul%d" % t, j, bank, "x%d" % t)
            act(cols("x%d" % t, j, W, 4), q(bank), Fn.Identity)
        act(cols("x%d" % t, W, W + 1), cols("x%d" % t, 0, 1), Fn.Identity)

    def profiles(t, h):
        if h in TNB_DVE:
            ts(half("tnb", h), q3(TA[h], 0, 8, 0, 32, 2), 0.0, Op.is_equal)
        else:
            act(half("tnb", h), q3(TA[h], 0, 8, 0, 32, 2), Fn.Relu, bias=1.0, scale=-1.0)
        mm(q(TB[h], 0, 128), half("tnb", h), ident)
        act(half("ntp", h), q(TB[h], 0, 128), Fn.Identity)
        mm(q(TB[h], 128, C), A("blr" if h else "blf"), half("ntp", h))
        tt(half("d1", h), q(TB[h], 128, C), A("drf" if t else "dri") if h else cols("kt", 1, C + 1, 2), Op.mult)
        tt(half("d2", h), q(TB[h], 384, 512), half("d1", h), Op.add)
        act(half("df", h), half("d2", h), Fn.Identity, bias=M1, scale=2.0)
        centres(t + 1, h, "d2")
        if t == 0 and h:
            act(A("dx"), half("df", 1), Fn.Identity, bias=-M1)
            rotate("drf", 0, "dx", 0)

    def tapes(t, h):
        sx, lx = q3(TA[h], 0, 8, 0, 32, 2), q3(TA[h], 0, 8, 1, 32, 2)
        rows = slice(8 * h, 8 * h + 8)
        leave, moved_by = A("sl", ALL, h, slice(1, C, 2)), A("sc", ALL, h, slice(0, C, 2))
        tt(A("sl", ALL, h, slice(0, C, 2)), sx, half("ee", h), Op.min)
        ts(leave, lx, 0.0, Op.is_lt, B, Op.mult)
        profiles(t, h)
        o, d, seg = A("sc", ALL, h), A("sl", ALL, h), A("seg")
        add("dve", lambda: g.vector.tensor_tensor_scan(o[0], seg[0], d[0], 0.0, Op.mult, Op.add), [o], [d, seg], vtime(o, seg))
        vv = q3(TA[h], 8, 16, 0, 16)
        mm(vv, ident, half("th", h), True, False)
        mm(vv, A("n32"), leave, False, not VV_PE, True)
        if VV_PE:
            mm(vv, identf, moved_by, False, True)
        else:
            tt(vv, vv, moved_by, Op.add)
        at = 8 * 26 * h
        for k0, k1 in NEW[h]:
            bank, row = (TC[h], 16) if k0 == 0 else (TC[1 - h], 24)
            for s in range(k1 + 1):
                i = max(k0, s - 1)
                if s == 1 and k1 == 16:
                    tt(A("e2", ALL, rows), q3(TA[h], 8, 16, 15, 16), A("nt%d" % t, ALL, rows), Op.add)
                    if h in ER_DVE:
                        cp(half("er", h), IND(A("e2", ALL, rows), A("el")))
                    else:
                        act(half("er", h), IND(A("e2", ALL, rows), A("el")), Fn.Identity)
                    tt(q3(TA[h], 8, 16, 16, 32), vv, half("er", h), Op.add)
                if s not in JOIN[h]:
                    at, i0, s0 = at + 8, i, s
                c = A("cl", ALL, slice(at - 8, at), slice(i, k1))
                to = q3(TA[h], 0, 8, 16 * (s // 2 % 2) + i, 16 * (s // 2 % 2) + k1) if s in JOIN[h] else c
                ts(to, q3(TA[h], 8, 16, i + s, k1 + s), (s - 0.5) * B, Op.max, (s + 0.5) * B, Op.min)
                if s in JOIN[h]:
                    tt(c, to, c, Op.add)
                if s + 1 not in JOIN[h] or s == k1:
                    mm(q3(bank, row, row + 8, i0, k1), identf, A("cl", ALL, slice(at - 8, at), slice(i0, k1)), s0 == 0, s == k1)
            wrap(h, h == 1, bank, row, k0, k1)
            offsets(h, k0, k1)

    def last_terms(t):
        for c in range(len(LAST) - 1):
            a, b = LAST[c], LAST[c + 1]
            o = cols("zt", a, b)
            tt(o, IND(A("kt"), cols("idx", a // 16, b // 16)), cols("x%d" % t, a, b), Op.subtract)
            act(o, o, Fn.Abs)
            act(q(c % 4, 0, b - a), o, Fn.Exp, scale=-1.0 / 8)
            tt(cols("zt", a, b), q(c % 4, 0, b - a), cols("g%d" % t, a, b), Op.mult)
            if a == 0:
                act(cols("zt", W, W + 1), cols("zt", 0, 1), Fn.Identity)
        for a, b in ((0, 1), (1, 3), (3, 7), (7, TAIL)):
            gather_terms(t, 1, a, b, 0)
        o = A("zg0", ALL, 0, slice(128 * TAIL, 128 * TAIL + 128))
        for k in range(TAIL, 16):
            src = IND(A("zt"), cols("pl%d" % (t % 2), 128 + 8 * k, 128 + 8 * k + 8))
            if k == TAIL:
                cp(o, src)
            else:
                tt(o, src, o, Op.add)
        mm(q(5, 0, 128), identf, half("yb", 0), True, False)
        for k in range(min(16, TAIL + 1)):
            mm(q(5, 0, 128), home(t, 1), A("zg0", ALL, 0, slice(128 * k, 128 * k + 128)), False, k == min(15, TAIL))
        for k in range(8):
            src = IND(A("zt"), cols("pl%d" % (t % 2), 16 * k, 16 * k + 16))
            tt(A("ya"), src, cols("yacc", 0, C) if k == 0 else A("ya"), Op.add)
        tt(cols("ys", 0, 128), half("ya", 0), half("ya", 1), Op.add)
        dma("sp", (cols("y", 0, 128), cols("ys", 0, 128)))
        tt(cols("ys", 128, C), q(5, 0, 128), cols("yacc", C, 384), Op.add)
        dma("act", (cols("y", 128, C), cols("ys", 128, C)))

    ts(A("tauh", slice(0, 8)), A("taui", slice(0, 8)), -OFF, Op.add)
    ts(A("df"), A("di"), M1, Op.add)
    for h in range(2):
        first_times(h)
    act(A("nt0"), q(4, 0, 16), Fn.Identity, scale=-1.0)
    act(cols("nt1", 0, 8), cols("nt0", 0, 8), Fn.Identity)
    act(cols("nt1", 9, 16), cols("nt0", 8, 15), Fn.Identity)
    act(cols("nt1", 8, 9), cols("nt0", 15, 16), Fn.Identity)
    for h in range(2):
        centres(0, h, "di")
        times(h)
    hand_over("x0", [gains])
    for t in range(VI):
        for h in range(2):
            k0 = 0
            for piece in HEAR[h]:
                hear(t, h, *piece)
            for w, k, k1 in sorted(HEAR[h]):
                if w and k == k0:
                    below(h, k0, min(r for r in ROWS[h] if r > k0))
                count(h, w, k, k1)
                if (w, k1) == (0, 16):
                    on_time(t, h)
                if w and k1 in ROWS[h]:
                    claims(h, k0, k1)
                    for a, b in zip(COUNT[h], COUNT[h][1:]):
                        if k0 <= a < k1:
                            histogram(h, a, b)
                    k0 = k1
        claimed(True)
        ts(A("pl%d" % (t % 2)), q(TC[0], 128, 384), 0.75 - 32 * 160, Op.add, float(NONE), Op.min)
        if t > 0:
            sum_terms(t - 1)
        owners(t)
        if t == VI - 1:
            add_terms(t - 1, 6)
            last_terms(t)
            break
        if t == 0:
            hand_over("g0", added[-1:])
            for a in range(0, 16, 2):
                sel(cols("sel", 128 * a, 128 * a + C), A("c256"), [[-1, 2], [-16, 8], [0, 16]], Op.is_equal, -a, 1, added[-1:])
            logs()
            send(4, A("ul1"), A("u0"))
        else:
            act(half("ef1", 0), half("df", 0), Fn.Exp, scale=1.0 / 256, bias=-M1 / 256)
            act(A("ev"), half("df", 1), Fn.Exp, scale=1.0 / 256, bias=-M1 / 256)
            rotate("ef1", 128, "ev", 0, 112)
            send(5, A("ul2"), A("u1"), A("ul1"))
        taken_columns(t)
        for a in range(0, W, STEP):
            terms(t, a, a + STEP)
        for h in range(2):
            taken(t, h)
            tapes(t, h)
            times(h)
        next_table(t + 1)
        if t > 0:
            add_terms(t - 1, 7)
    if not ORDER:
        ORDER.extend(arrange(ops))
    emit([ops[i] for i in ORDER], queue, T)


def arrange(ops):
    seen, last = {}, {}
    before = []
    count = len(ops)
    for i, o in enumerate(ops):
        dep = {j: 0 for j in o["after"]}
        for mine, write in ((o["r"], False), (o["w"], True)):
            for (name, p0, p1, m) in mine:
                if name in SCRATCH and SCRATCH[name][0] == P:
                    j = last.get(name, i)
                    if j != i:
                        dep[j] = max(dep.get(j, 0), ops[j]["wake"] if ops[j]["eng"] != o["eng"] else 0)
                    last[name] = i
                keep = []
                for e in seen.get(name, []):
                    j, wr, a0, a1, b = e
                    if j != i and (wr or write) and a0 <= p1 and p0 <= a1 and b & m:
                        dep[j] = 0 if ops[j]["eng"] == o["eng"] == "pe" else ops[j]["wake"]
                    if not (write and p0 <= a0 and a1 <= p1 and (b | m) == m):
                        keep.append(e)
                seen[name] = keep + [(i, write, p0, p1, m)]
        before.append(dep)
    ops, moving = list(ops), {}
    for i in range(count):
        if ops[i]["move"]:
            moving[i] = len(ops)
            ops.append({"eng": "dm", "ns": ops[i]["move"], "wake": ops[i]["wake"], "sem": True})

    def length(o, slow, engines, dmas, wake):
        return o["ns"] * dmas if o["sem"] else (o["ns"] + o["more"] * (slow - 1)) * engines

    def waits(links, slow, engines, dmas, wake):
        return [[(k, gap * (wake if gap == WAKE else dmas)) for k, gap in d.items()] for d in links]

    lengths = [[length(o, *s) for o in ops] for s in SLOW]
    weight = [1 / (s[1] * (0.6 + 0.4 * max(s[0], 1))) for s in SLOW]
    ops = [dict(o, ns=length(o, *MIDDLE)) for o in ops]
    before = [{moving[j] if j in moving and (gap or not ops[i]["eng"]) else j: gap for j, gap in dep.items()} for i, dep in enumerate(before)]
    before += [{i: 0} for i in moving]
    behind = [{} for o in ops]
    for i, dep in enumerate(before):
        for j, gap in dep.items():
            behind[j][i] = gap

    def fit(turn, needs, lead):
        end = [0.0] * len(ops)
        busy = {e: [] for e in ENG}
        for i in turn:
            at, ns = max([end[j] + gap for j, gap in needs[i].items()] + [lead[i]]), ops[i]["ns"]
            if ops[i]["eng"]:
                line = busy[ops[i]["eng"]]
                k = len(line)
                while k and line[k - 1][1] > at:
                    k -= 1
                while k < len(line) and line[k][0] < at + ns:
                    at = max(at, line[k][1])
                    k += 1
                line.insert(k, (at, at + ns))
            end[i] = at + ns
        return end

    def place(turn, needs, lead):
        rank = {i: n for n, i in enumerate(turn)}
        users = behind if needs is before else before
        left, at, end = [len(d) for d in needs], list(lead), [0.0] * len(ops)
        ready = {e: [i for i in turn if not left[i] and ops[i]["eng"] == e] for e in ENG + (None,)}
        free = {e: 0.0 for e in ready}
        for _ in ops:
            now, e = min(((max(free[e], min(at[i] for i in ready[e])), e) for e in ready if ready[e]), key=lambda x: x[0])
            i = min((j for j in ready[e] if at[j] <= now + PATIENCE), key=rank.get)
            ready[e].remove(i)
            end[i] = max(now, at[i]) + ops[i]["ns"]
            free[e] = end[i] if e else 0.0
            for j, gap in users[i].items():
                at[j] = max(at[j], end[i] + gap)
                left[j] -= 1
                if not left[j]:
                    ready[ops[j]["eng"]].append(j)
        return end

    tail = [o["wake"] if o["sem"] else 0.0 for o in ops]
    chain, left = [o["ns"] + w for o, w in zip(ops, tail)], [len(d) for d in behind]
    todo = [i for i in range(len(ops)) if not left[i]]
    while todo:
        i = todo.pop()
        for j, gap in before[i].items():
            chain[j] = max(chain[j], ops[j]["ns"] + gap + chain[i])
            left[j] -= 1
            if not left[j]:
                todo.append(j)
    def replay(order, ns):
        end, free = [0.0] * len(ops), {e: 0.0 for e in ENG + (None,)}
        for i in order:
            for j in (i, moving[i]) if i in moving else (i,):
                e = ops[j]["eng"]
                end[j] = max([end[k] + gap for k, gap in before[j].items()] + [free[e]]) + ns[j]
                free[e] = end[j] if e else 0.0
        return max(e + w for e, w in zip(end, tail))

    best, seed = None, 1
    for trial in range(TRIALS):
        noise = []
        for i in ops:
            seed = (seed * 1103515245 + 12345) % 2 ** 31
            noise.append(seed / 2 ** 31 * NOISE * (trial > 0))
        turn = sorted(range(len(ops)), key=lambda i: -chain[i] - noise[i])
        end = place(turn, before, [0.0] * len(ops))
        turn = sorted(turn, key=lambda i: end[i])
        for how in (place, fit, fit) * ROUNDS:
            end = how(turn, before, [0.0] * len(ops))
            order = [i for i in sorted(turn, key=lambda i: end[i] - ops[i]["ns"]) if i < count]
            span = sum(replay(order, ns) * w for ns, w in zip(lengths, weight)) / len(SLOW)
            if best is None or span < best[0]:
                best = (span, order)
            end = how(sorted(turn[::-1], key=lambda i: -end[i] - tail[i]), behind, tail)
            turn = sorted(turn, key=lambda i: -end[i])

    cases = [(ns, waits(before, *s), waits(behind, *s)) for ns, s in zip(lengths, SLOW)]
    issuer = {j: i for i, j in moving.items()}
    eng, every = [o["eng"] for o in ops], range(len(ops))

    def rnd(n):
        seed[0] = (seed[0] * 1103515245 + 12345) % 2 ** 31
        return (seed[0] >> 8) % n

    def forwards(order):
        prv, nxt, last = [-1] * len(ops), [-1] * len(ops), {}
        for i in order:
            if eng[i]:
                if eng[i] in last:
                    prv[i], nxt[last[eng[i]]] = last[eng[i]], i
                last[eng[i]] = i
        ends = []
        for ns, needs, users in cases:
            end = [0.0] * (len(ops) + 1)
            for i in order:
                at = end[prv[i]]
                for k, gap in needs[i]:
                    if end[k] + gap > at:
                        at = end[k] + gap
                end[i] = at + ns[i]
            ends.append(end)
        spans = [max(e + w for e, w in zip(end, tail)) for end in ends]
        return {"order": order, "prv": prv, "nxt": nxt, "ends": ends, "spans": spans, "span": sum(s * w for s, w in zip(spans, weight)) / len(spans)}

    def settled(now):
        end, ns = now["ends"][0], lengths[0]
        order = [j for i in sorted((i for i in now["order"] if i < count), key=lambda i: end[i] - ns[i]) for j in ((i, moving[i]) if i in moving else (i,))]
        if [i for i in order if i >= count] != [i for i in now["order"] if i >= count]:
            now = forwards(order)
        now["order"], now["at"], now["rests"], now["pairs"] = order, {i: n for n, i in enumerate(order)}, [], []
        for (ns, needs, users), end, span in zip(cases, now["ends"], now["spans"]):
            rest, nxt = [0.0] * (len(ops) + 1), now["nxt"]
            for i in reversed(order):
                at = max(rest[nxt[i]], tail[i])
                for k, gap in users[i]:
                    if rest[k] + gap > at:
                        at = rest[k] + gap
                rest[i] = at + ns[i]
            now["rests"].append(rest)
            now["pairs"] += [(i, nxt[i]) for i in every if nxt[i] >= 0 and end[i] + rest[nxt[i]] > span - 1 and i not in before[nxt[i]]]
        return now

    def moved(now):
        a, b = now["pairs"][rnd(len(now["pairs"]))]
        if a in issuer:
            a, b = issuer[a], issuer[b]
        order, at, up = now["order"], now["at"], rnd(2)
        side, links = (now["prv"], before) if up else (now["nxt"], behind)
        mine, past = (b, a) if up else (a, b)
        for _ in range((0, 0, 1, 2, 4, 8, 16, 32)[rnd(8)]):
            past = side[past] if side[past] >= 0 else past
        lo, hi = sorted((at[mine], at[past]))
        hi += order[hi] in moving
        along, todo = {mine}, [mine]
        for i in todo:
            near = list(links[i]) + ([side[i]] if eng[i] != eng[mine] and i != moving.get(mine) else []) + ([moving[i]] if i in moving else [])
            for j in near:
                if j >= 0 and j not in along and lo <= at[j] <= hi:
                    along.add(j)
                    todo.append(j)
        if past in along or lo >= hi:
            return None
        return valued(now, lo, hi, sorted(order[lo:hi + 1], key=lambda i: (i in along) != up))

    def ends_of(now, old):
        first, last = {}, {}
        for i in old:
            first.setdefault(eng[i], now["prv"][i])
            last[eng[i]] = now["nxt"][i]
        return first, last

    def replanned(now):
        order, at, s = now["order"], now["at"], rnd(len(SLOW))
        (ns, needs, users), ends, rest = cases[s], now["ends"][s], now["rests"][s]
        lo = rnd(len(order))
        lo -= order[lo] >= count
        hi = min(len(order) - 1, lo + 20 + rnd(STRETCH))
        hi += order[hi] in moving
        old, noise, patience = order[lo:hi + 1], rnd(NOISE) + 1, rnd(8) * PATIENCE
        first, last = ends_of(now, old)
        chain, left, ready, start = {}, {}, {e: [] for e in first}, {}
        for i in reversed(old):
            chain[i] = ns[i] + max([tail[i], rest[last[eng[i]]] if eng[i] else 0] + [gap + (chain[k] if k in chain else rest[k]) for k, gap in users[i]])
        for i in old:
            chain[i] += rnd(noise)
            left[i] = sum(at[k] >= lo for k, gap in needs[i])
            start[i] = max([0.0] + [ends[k] + gap for k, gap in needs[i] if at[k] < lo])
            if not left[i]:
                ready[eng[i]].append(i)
        free, new = {e: ends[i] if e else 0.0 for e, i in first.items()}, []
        while len(new) < len(old):
            t, e = min(((max(free[e], min(start[i] for i in r)), e) for e, r in ready.items() if r), key=lambda x: x[0])
            i = max((j for j in ready[e] if start[j] <= t + patience), key=chain.get)
            for i in (i, moving[i]) if i in moving else (i,):
                ready[eng[i]].remove(i)
                new.append(i)
                t = max(free[eng[i]], start[i]) + ns[i]
                free[eng[i]] = t if eng[i] else 0.0
                for k, gap in users[i]:
                    if k in left:
                        start[k] = max(start[k], t + gap)
                        left[k] -= 1
                        if not left[k]:
                            ready[eng[k]].append(k)
        return valued(now, lo, hi, new) if new != old else None

    def valued(now, lo, hi, new):
        order, at = now["order"], now["at"]
        first, last = ends_of(now, order[lo:hi + 1])
        total = 0.0
        for (ns, needs, users), ends, rest, w in zip(cases, now["ends"], now["rests"], weight):
            end, free, span = {}, {e: ends[i] for e, i in first.items()}, 0.0
            for i in new:
                t = free[eng[i]] if eng[i] else 0.0
                for k, gap in needs[i]:
                    t = max(t, end.get(k, ends[k]) + gap)
                end[i] = free[eng[i]] = t = t + ns[i]
                span = max(span, t + tail[i])
                for k, gap in users[i]:
                    if at[k] > hi and t + gap + rest[k] > span:
                        span = t + gap + rest[k]
            total += w * max([span] + [free[e] + rest[i] for e, i in last.items() if e])
        return total / len(weight), order[:lo] + new + order[hi + 1:]

    seed = [seed]
    now = best = settled(forwards([j for i in best[1] for j in ((i, moving[i]) if i in moving else (i,))]))
    for n in range(MOVES):
        limit = now["span"] + rnd(SLACK) * (1 - n / MOVES)
        new = moved(now) if n % ANEW else replanned(now)
        if new and new[0] <= limit:
            new = forwards(new[1])
            if new["span"] <= limit:
                now = settled(new)
                if now["span"] < best["span"]:
                    best = now
    SPAN.append(best["span"])
    return [i for i in best["order"] if i < count]


def emit(ops, queue, T):
    seen = {}
    for i, o in enumerate(ops):
        dep = set()
        for mine, write in ((o["w"], True), (o["r"], False)):
            for (name, p0, p1, m) in mine:
                bank = name in SCRATCH and SCRATCH[name][0] == P
                for (j, wr, a0, a1, b) in seen.get(name, []):
                    other = ops[j]
                    same = other["eng"] == o["eng"] and other["sem"] is None and o["sem"] is None
                    if same and o["eng"] == "pe":
                        continue
                    if (bank and not same) or ((wr or write) and a0 <= p1 and p0 <= a1 and b & m):
                        dep.add(j)
        o["dep"] = dep
        for mine, write in ((o["r"], False), (o["w"], True)):
            for (name, p0, p1, m) in mine:
                keep = []
                for e in seen.get(name, []):
                    same = ops[e[0]]["eng"] == o["eng"] and ops[e[0]]["sem"] is None and o["sem"] is None
                    if (write or (same and not e[1])) and p0 <= e[2] and e[3] <= p1 and (e[4] | m) == m:
                        continue
                    keep.append(e)
                keep.append((i, write, p0, p1, m))
                seen[name] = keep
    known = {e: {} for e in ENG}
    for i, o in enumerate(ops):
        o["wait"] = []
        if o["eng"] is None:
            o["know"] = {o["sem"]: i}
            continue
        kn = known[o["eng"]]
        for j in sorted(o["dep"], reverse=True):
            key = ops[j]["sem"] or ops[j]["eng"]
            if kn.get(key, -1) >= j:
                continue
            o["wait"].append(j)
            ops[j]["inc"] = True
            for k2, val in ops[j]["know"].items():
                if kn.get(k2, -1) < val:
                    kn[k2] = val
        o["know"] = dict(kn)
        o["know"][o["sem"] or o["eng"]] = i
    cnt = {e: 0 for e in ENG}
    waited = {}
    for o in ops:
        if o["eng"] is None:
            continue
        for j in o["wait"]:
            p = ops[j]
            key, val = (p["sem"], p["n"]) if p["sem"] else (p["eng"], p["val"])
            queue[o["eng"]].wait_ge(T.sem[key], val)
            waited[key] = max(waited.get(key, 0), val)
        ins = o["call"]()
        if o["sem"]:
            if o["extra"] is None:
                ins.then_inc(T.sem[o["sem"]], 16)
        elif o["inc"]:
            cnt[o["eng"]] += 1
            o["val"] = cnt[o["eng"]]
            ins.then_inc(T.sem[o["eng"]], 1)
    for o in ops:
        if o["sem"] and waited.get(o["sem"], 0) < o["n"]:
            queue["gp"].wait_ge(T.sem[o["sem"]], o["n"])


def rank_program(g, core, T, topo):
    rank = T.rank_of(core)
    if rank is not None:
        build(g, core, T, topo, rank)
        return
    for r in range(N):
        for me, c in enumerate(helpers(topo, T.cores, r)):
            if c == core:
                pass_on(g, core, T, topo, r, me)
